import numpy as np, ml_dtypes
CORES = [6,15,38,47]
N = 4
BF = ml_dtypes.bfloat16
V, A, S, RO = 4096, 256, 2, 4
def parts(rng):
    od = np.argsort(np.arange(V) + rng.choice(np.array([24, 400, 4 * V]), (N, 8, 1)) * rng.random((N, 8, V)), axis=-1); inv = np.argsort(od, axis=-1)
    c = rng.choice(np.array([8, 16]), (1, 8, 1, 1)); e = rng.choice(np.array([1.0, 1.5, 2.0]), (1, 8, 1, 1))
    w = np.arange(V) // c * c + (c * rng.random((N, 8, 16, V)) ** e).astype(np.int64)
    w = np.where(rng.random(w.shape) < 0.125, rng.integers(0, V, w.shape), w)
    nb = np.take_along_axis(np.take_along_axis(od[:, :, None], w, 3), inv[:, :, None], 3)
    x = np.minimum(np.maximum(rng.integers(0, 16, (1, 1, 16, V)) + rng.integers(-2, 3, (N, 8, 16, V)), 0), 15)
    return od, nb, np.take_along_axis(x, inv[:, :, None], 3)
def seeds(rng, od, m, lo, hi):
    mp = np.full((N, 8, V), V); iv = np.full((N, 8, V), V); ky = np.full((N, 8, V), 1000)
    for r in range(N):
        q = (r + 1) % N
        for g in range(8):
            h = (g + (r == N - 1)) % 8
            p = np.flatnonzero(m[r, g][od[r, g]]); w = p + 0
            e = np.flatnonzero(rng.random(len(p)) < 0.1); w[e] = p[rng.permutation(e)]
            u = od[r, g][p]; v = od[q, h][w]
            mp[r, g, u] = v; iv[q, h, v] = u; ky[q, h, v] = rng.integers(lo, hi, len(v))
    return mp, iv, ky
def pack(x, nb, mp, iv, ky):
    return {"x": np.ascontiguousarray(x.reshape(N, 128, V)).astype(np.float32).astype(BF), "nb": np.ascontiguousarray(nb.reshape(N, 128, V)).astype(np.int32),
            "mp": mp.astype(np.int32), "iv": iv.astype(np.int32), "ky": ky.astype(np.int32)}
def setup_inputs(rng):
    od, nb, x = parts(rng); m = rng.random((N, 8, V)) < rng.choice(np.array([0.35, 0.5, 0.65]), (N, 8, 1))
    return pack(x, nb, *seeds(rng, od, m, -80, 160))
def setup_inputs_room(rng):
    od, nb, x = parts(rng); m = np.ones((N, 8, V), bool); T = V // S
    for r in range(N):
        for k in range(S):
            c = np.array([A, A + 1, T, A - 1, 1, 0, A, A + 1])
            if r or k: c = rng.permutation(c)
            for g in range(8): m[r, g, k * T + rng.permutation(T)[:int(c[g])]] = False
    return pack(x, nb, *seeds(rng, od, m, -80, 300))
def setup_inputs_ties(rng):
    od, nb, x = parts(rng); m = rng.random((N, 8, V)) < 0.5
    x[:, :4] = x[:1, :1, :, :1] + 0
    x[:, 4:] = np.where(x[:, 4:, :1] < 8, 3, 4)
    mp, iv, ky = seeds(rng, od, m, 0, 1)
    ky = np.where(iv < V, rng.choice(np.array([-64, -48, -47, -33, -32, -31, -17, 999]), (N, 8, V)), 1000)
    return pack(x, nb, mp, iv, ky)
def setup_inputs_alike(rng):
    od, nb, x = parts(rng); m = rng.random((N, 8, V)) < 0.5; T = V // S
    nb[:, 0] = nb[:, 0, :1] + 0; x[:, 0] = x[:1, 0, :, :1] + 0
    m[:, 1, 0] = True; m[:, 1, V - 1] = True; nb[:, 1] = rng.choice(np.array([0, V - 1]), (N, 16, V))
    m[:, 2, 0] = False
    for r in range(N): nb[r, 2] = rng.choice(np.flatnonzero(~m[r, 2]), (16, V))
    nb[:, 3, :8] = np.arange(V)
    nb[:, 4, 1::2] = nb[:, 4, 0::2] + 0
    nb[:, 5, 8:] = nb[:, 5, :8] + 0
    few = np.array([0, 1, V // 2, V - 1]); m[:, 6, few] = True; nb[:, 6] = rng.choice(few, (N, 16, V))
    o = np.arange(V) % T; m[:, 7] = (o >= 3) & (o < T - 40)
    mp, iv, ky = seeds(rng, od, m, -80, 300)
    ky[:, 0] = np.where((iv[:, 0] < V) & (rng.random((N, V)) < 0.3), -256, ky[:, 0])
    return pack(x, nb, mp, iv, ky)
def setup_inputs_evict(rng):
    od, nb, x = parts(rng); m = rng.random((N, 8, V)) < rng.choice(np.array([0.8, 0.85, 0.9]), (N, 8, 1))
    return pack(x, nb, *seeds(rng, od, m, 209, 1000))
def setup_inputs_spread(rng):
    od, nb, x = parts(rng); m = rng.random((N, 8, V)) < rng.choice(np.array([0.05, 0.2, 0.5, 0.8, 0.95]), (N, 8, 1))
    y = (16 * rng.random((N, 8, 16, V)) ** np.exp2(rng.integers(-2, 4, (N, 8, 1, V)))).astype(np.int64)
    x = np.where(rng.random((N, 8, 1, V)) < 0.5, np.minimum(y, 15), x)
    low = (V * rng.random(nb.shape) ** 6).astype(np.int64)
    nb = np.where(rng.random(nb.shape) < rng.choice(np.array([0.02, 0.2]), (N, 8, 1, 1)), np.minimum(low, V - 1), nb)
    return pack(x, nb, *seeds(rng, od, m, -256, 1000))
def check_inputs(d):
    bad = []; x = np.asarray(d["x"]).astype(np.float32)
    if not np.all((x >= 0) & (x <= 15) & (x == np.floor(x))): bad.append("numbers of x")
    for k, lo, hi in (("nb", 0, V - 1), ("mp", 0, V), ("iv", 0, V), ("ky", -256, 1000)):
        if np.min(d[k]) < lo or np.max(d[k]) > hi: bad.append("range of " + k)
    if bad: return bad
    mp = np.asarray(d["mp"]).astype(np.int64); iv = np.asarray(d["iv"]).astype(np.int64); ky = np.asarray(d["ky"])
    r, g, u = np.nonzero(mp < V)
    if np.any(iv[(r + 1) % N, np.where(r == N - 1, g + 1, g) % 8, mp[r, g, u]] != u): bad.append("iv is not the inverse of mp")
    r, g, v = np.nonzero(iv < V)
    if np.any(mp[(r - 1) % N, np.where(r == 0, g + 7, g) % 8, iv[r, g, v]] != v): bad.append("mp is not the inverse of iv")
    if np.any((ky == 1000) != (iv == V)): bad.append("keys of unmatched nodes")
    return bad
def reference(x, nb, mp, iv, ky):
    X = x.astype(np.float32).astype(np.int64).reshape(N, 8, 16, V); B = nb.astype(np.int64).reshape(N, 8, 16, V)
    M = mp.astype(np.int64); I = iv.astype(np.int64); K = ky.astype(np.int64); T = V // S
    for t in range(RO):
        lo = (t % S) * T; todo = []
        row = ((np.arange(16) + t) & 15)[:, None]
        for r in range(N):
            q = (r + 1) % N
            for g in range(8):
                h = (g + 1) % 8 if r == N - 1 else g
                u = lo + np.flatnonzero(M[r, g, lo:lo + T] == V)[:A]
                z = M[r, g][B[r, g][:, u]]; has = z < V
                v = np.where(has, B[q, h][row, np.minimum(z, V - 1)], 0)
                s = np.add.reduce(((v[:, None] == v[None]) & has[None]).astype(np.int64), axis=1)
                d = np.add.reduce(np.abs(X[r, g][:, u][:, None] - X[q, h][:, v]), axis=0)
                sc = np.where(has & (s >= 2), d - 16 * s, 5000)
                j = np.argmin(sc, axis=0); a = np.arange(len(u)); best = sc[j, a]; v = v[j, a]
                a = np.flatnonzero(best < 5000); u, v, best = u[a], v[a], best[a]
                o = np.lexsort((u, best, v)); u, v, best = u[o], v[o], best[o]
                first = np.ones(len(v), bool); first[1:] = v[1:] != v[:-1]
                a = np.flatnonzero(first & (best < K[q, h][v])); u, v, best = u[a], v[a], best[a]
                todo.append((r, g, q, h, u, v, best, (3 * X[q, h][:, v] + X[r, g][:, u]) >> 2))
        for r, g, q, h, u, v, best, col in todo:
            old = I[q, h][v]; M[r, g, old[old < V]] = V
            M[r, g, u] = v; I[q, h, v] = u; K[q, h, v] = best; X[q, h][:, v] = col
    return {"ym": M.astype(np.float32), "yk": K.astype(np.float32)}

@@ -1,0 +1,785 @@
+from concourse.bass import DstId, RemoteDMATransfer
+from concourse.mybir import AluOpType as A, AxisListType, ActivationFunctionType as AF
+
+V = 4096
+RO = 4
+FN, FP, FD, FE = 256, 4352, 4384, 4640
+DUMP = 4128
+CR = 12582912.0
+CAP = 241.0 * 65536
+XG_V = (3,)
+PEN_V = (1,)
+RED_V = 4
+ORDER = "f0 g0 e0 u0 x0 f1 q0 e1 a0 c0 x1 f2 q1 e2 x2 s0 f3 q2 e3 a1 c1 x3 q3 a2 c2 s1 b0 k0 a3 c3 b1"
+CY, PE, GA, SC, HOP = 1.0, 0.5, 1.5, 3.5, 80.0
+
+f32, bf, f16, i32, u16 = "float32", "bfloat16", "float16", "int32", "uint16"
+
+
+def _sb(n, dt):
+    return ("sbuf", [128] + (n if isinstance(n, list) else [n]), dt)
+
+
+SCRATCH = {
+    "B": _sb(4104, i32), "F": _sb(FE, f32), "BG": _sb(4112, i32), "XH": _sb(4384, bf), "XS": _sb(4096, bf),
+    "XG": _sb(4384, bf), "BKI": _sb(4384, f32), "FL": _sb(4384, bf),
+    "FO": _sb(4096, f16), "XO": _sb(4096, bf), "AB": _sb([32, 128], bf), "EQ": _sb([16, 128], bf),
+    "VO": _sb(256, u16), "V16": _sb(256, f16), "WL": _sb(256, u16), "YA": _sb(256, bf),
+    "PI": _sb(8, i32), "CO": _sb(64, f32), "N256": _sb(256, f32), "QN": _sb(256, f32), "GN": _sb(128, f32),
+    "IDX2": _sb(256, f32), "J2": _sb([8, 32], f32), "SEI": _sb(16, f32),
+    "DM": _sb(256, f32), "M12": _sb(256, f32), "RST": _sb(256, f32), "I2A": _sb(256, f32), "STA": _sb(256, bf),
+    "UB": _sb(144, bf), "UBf": _sb(144, f32), "SAMEG": _sb(128, bf), "TRI": _sb(128, bf),
+    "ID": _sb(512, bf), "IDf": _sb(384, f32), "S": _sb(2048, bf), "ROT": _sb([8, 32], bf),
+    "PD": _sb(1024, bf), "CK": _sb([8, 256], bf), "JT": _sb(512, bf), "ONE": _sb(2048, bf),
+    "B8s": _sb(8, bf), "SM": _sb(16 * 32, f32), "SI": _sb(64, i32), "SU": _sb(16 * 12, u16), "MF": _sb(16, bf),
+    "MP": _sb(256, i32), "T1": _sb([16, 32], f32), "T2": _sb([16, 32], f32), "T3": _sb(256, f32), "WS": _sb(256, u16),
+    "WF": _sb(128, f32), "IF": _sb(128, bf), "CC": _sb(136, f32), "ZC": _sb(256, f32), "W0": _sb(256, u16),
+    "Y0": _sb(256, bf), "U0": _sb(16, f32), "WR": _sb(256, u16), "UR": _sb(16, f32),
+    "KC": _sb(512, i32), "KF": _sb(512, f32),
+    "CUM": _sb(2048, bf), "P": _sb(136, f32), "CMP": _sb(256, bf), "JK": _sb(4096, bf),
+    "PEN": _sb(256, bf), "KS": _sb(256, f32),
+    "E1": _sb(256, f32), "E2": _sb(256, bf), "E3": _sb(256, f32), "E4": _sb(256, f32), "E5": _sb(256, f32),
+    "E6": _sb(256, f32), "EU": _sb(256, f32),
+    "G1": _sb(256, f32), "TB": _sb(256, f32), "R": _sb(256, bf), "LE": _sb(256, bf), "LO": _sb(256, bf),
+    "NEW": _sb(256, f32), "FB": _sb(256, f32), "FW": _sb(512, f32), "XT": _sb(256, bf),
+    "NX": _sb(768, bf), "VS": _sb(64, u16), "XU": _sb(768, bf), "LU": _sb(48, u16),
+    "FC": _sb(256, f32), "FR": _sb(512, f32), "MO": _sb(512, f32), "GV": _sb(512, f32), "ML": _sb(32, u16),
+    "HX": _sb(2048, bf), "HB": _sb(2048, i32), "NR": _sb(768, bf), "VR": _sb(48, u16), "IDR": _sb(128, bf),
+    "dZ": ("dram", [128, 256], f32), "dM": ("dram", [128, 256], f32), "dB": ("dram", [4, 128, 1024], i32),
+}
+for _k in range(8):
+    SCRATCH["ps%d" % _k] = ("psum", [128, 512], f32)
+SIZE = {f32: 4, i32: 4, bf: 2, f16: 2, u16: 2}
+
+MSG = ["W", "w", "y", "u", "Z", "X0", "X1", "B0", "B1", "B2", "B3", "N0", "N1", "N2", "L0", "L1", "L2", "M", "G", "E"]
+SEMAPHORES = (["qv", "qa", "qt", "qg", "sent", "h0", "h1", "h2"] + ["a" + m for m in MSG]
+              + ["d%d" % k for k in range(30)])
+
+
+def _mask(engines):
+    m = 0
+    for e in engines:
+        m |= 1 << e
+    return m
+
+
+def helper_of(T, topo, r):
+    me, nxt = T.cores[r], T.cores[(r + 1) % len(T.cores)]
+    for c in topo.cores_of(me):
+        if T.rank_of(c) is None and topo.die(c) != topo.die(me) and topo.may_write(c, nxt):
+            return c
+    return None
+
+
+def landing(T, rot):
+    d = {"X0": T["XG"][:, 0:2048], "X1": T["XG"][:, 2048:4096]}
+    for k in range(4):
+        lo = 1024 * k + (8 if k >= 2 else 0)
+        d["B%d" % k] = T["dB"][k] if rot else T["BG"][:, lo:lo + 1024]
+    return d
+
+
+def helper_program(g, core, T, topo, r):
+    n = len(T.cores)
+    nxt = T.cores[(r + 1) % n]
+    land = landing(T, (r + 1) % n == 0)
+    cnt = len([e for e in topo.engines(T.cores[r], core) if e not in topo.engines(T.cores[r], nxt)])
+    rid, pid, _ = topo.addr(nxt)
+    m = topo.mask(core, nxt)
+    tot = 0
+    for s, src, name in (("h1", T["HB"][:, 0:1024], "B3"), ("h0", T["HX"][:, :], "X1"), ("h2", T["HB"][:, 1024:2048], "B1")):
+        g.wait_ge(T.sem[s], cnt)
+        g.remote_dma(land[name], src, T.sem["a" + name], T.sem["sent"], pid, rid, m)
+        tot += len(topo.engines(core, nxt))
+    g.wait_ge(T.sem["sent"], tot)
+
+
+def emit_in_planned_order(nodes, Q, T):
+    succ = [[] for _ in nodes]
+    for i, nd in enumerate(nodes):
+        for p in nd["pre"]:
+            succ[p].append(i)
+    prio = [0.0] * len(nodes)
+    for i in range(len(nodes) - 1, -1, -1):
+        prio[i] = nodes[i]["cost"] + nodes[i]["lat"] + max([prio[s] for s in succ[i]] + [0.0])
+    left = [len(nd["pre"]) for nd in nodes]
+    at = [0.0] * len(nodes)
+    free = {}
+    ready = [i for i in range(len(nodes)) if left[i] == 0]
+    order = []
+    while ready:
+        st = {i: max(at[i], free.get(nodes[i]["q"], 0.0) if nodes[i]["q"] != "x" else 0.0) for i in ready}
+        i = min(ready, key=lambda k: (st[k], -prio[k]))
+        for k in ready:
+            if nodes[k]["q"] == nodes[i]["q"] != "x" and prio[k] > prio[i] and st[k] < st[i] + min(
+                    0.6 * nodes[i]["cost"], 0.5 * (prio[k] - prio[i])) + 1:
+                i = k
+        ready.remove(i)
+        nd = nodes[i]
+        free[nd["q"]] = st[i] + nd["cost"]
+        order.append(i)
+        for s in succ[i]:
+            done = st[i] + nd["cost"] + (nd["lat"] + HOP if nodes[s]["pre"][i] != 0 else 0.0)
+            at[s] = max(at[s], done)
+            left[s] -= 1
+            if left[s] == 0:
+                ready.append(s)
+    count, final = {}, {}
+    for i in order:
+        nd = nodes[i]
+        if nd["tok"] is None and nd["inc"]:
+            count[nd["q"]] = count.get(nd["q"], 0) + len(nd["emit"])
+            nd["tok"] = ("q" + nd["q"], count[nd["q"]])
+    waited = {q: {} for q in Q}
+
+    def wait(q, s, v):
+        if waited[q].get(s, 0) < v:
+            Q[q].wait_ge(T.sem[s], v)
+            waited[q][s] = v
+
+    for i in order:
+        nd = nodes[i]
+        if nd["tok"] is not None:
+            final[nd["tok"][0]] = max(final.get(nd["tok"][0], 0), nd["tok"][1])
+        if nd["q"] == "x":
+            continue
+        need = {}
+        for p in nd["pre"]:
+            if nd["pre"][p] == 1:
+                s, v = nodes[p]["tok"]
+                need[s] = max(need.get(s, 0), v)
+        for s in need:
+            wait(nd["q"], s, need[s])
+        for e in nd["emit"]:
+            h = e()
+            if nd["inc"]:
+                h.then_inc(T.sem[nd["tok"][0]], nd["inc"])
+    return final, wait
+
+
+def rank_program(g, core, T, topo):
+    rank = T.rank_of(core)
+    n = len(T.cores)
+    if rank is None:
+        for r in range(n):
+            if helper_of(T, topo, r) == core:
+                helper_program(g, core, T, topo, r)
+        return
+    nxt, prv = T.cores[(rank + 1) % n], T.cores[(rank - 1) % n]
+    hlp = helper_of(T, topo, rank)
+    rot_in = rank == 0
+    rot_out = rank == n - 1
+    Q = {"v": g.vector, "a": g.scalar, "t": g.tensor, "g": g, "s": g.sync}
+    nodes, log, last, sends = [], {}, {}, {}
+    nd = [0]
+    group = []
+    chain = [None]
+
+    def r(name, lo=0, hi=None, step=1, p=None):
+        t = T[name]
+        if hi is None:
+            hi = t.shape[1]
+        ps = slice(None) if p is None else slice(*p)
+        return (t[ps, lo:hi:step] if step != 1 else t[ps, lo:hi], [(name, lo, hi)], len(range(lo, hi, step)), name, "")
+
+    def r3(name, a0, a1, b0, b1):
+        w = T[name].shape[2]
+        return (T[name][:, a0:a1, b0:b1], [(name, a0 * w, a1 * w)], (a1 - a0) * (b1 - b0), name, "")
+
+    def row(name, k, b0, b1):
+        w = T[name].shape[2]
+        return (T[name][:, k, b0:b1], [(name, k * w + b0, k * w + b1)], b1 - b0, name, "")
+
+    def ind(win, off):
+        return (win[0].indirect(off[0]), win[1] + off[1], 16 * off[2], win[3], "i")
+
+    def dr(apx, name):
+        return (apx, [(name, 0, 1)], 0, name, "")
+
+    def sm(k, lo=0, hi=16):
+        return r("SM", 16 * k + lo, 16 * k + hi)
+
+    def su(k, w=16):
+        return r("SU", 16 * k, 16 * k + w)
+
+    def co(k):
+        return r("CO", k, k + 1)
+
+    def regs(xs, out=False):
+        rd, wr = [], []
+        for x in xs:
+            if isinstance(x, tuple):
+                if out:
+                    wr += x[1][:1]
+                    rd += x[1][1:]
+                else:
+                    rd += x[1]
+        return rd, wr
+
+    def ap(x):
+        return x[0] if isinstance(x, tuple) else x
+
+    def node(q, outs, ins, emit, cost, lat=0.0, inc=1, tok=None, extra=None):
+        rd2, wr = regs(outs, True)
+        rd = regs(ins)[0] + rd2
+        me = len(nodes)
+        pre = dict(extra or {})
+        for rs, w in ((rd, False), (wr, True)):
+            for name, lo, hi in rs:
+                psum = name.startswith("ps")
+                for lo2, hi2, k, w2 in log.get(name, []):
+                    q2 = nodes[k]["q"]
+                    if psum and q2 == q == "t":
+                        pre.setdefault(k, 0)
+                    elif (psum and q2 != q) or ((w or w2) and lo < hi2 and lo2 < hi):
+                        pre[k] = 1
+                    elif psum:
+                        pre.setdefault(k, 0)
+        if q in "gs":
+            if q in last:
+                pre.setdefault(last[q], 0)
+            last[q] = me
+        if chain[0] is not None and q in "va":
+            if q in chain[0]:
+                pre.setdefault(chain[0][q], 0)
+            chain[0][q] = me
+        nodes.append(dict(q=q, emit=emit, cost=cost, lat=lat, inc=inc, tok=tok, pre=pre))
+        for rs, w in ((wr, True), (rd, False)):
+            for name, lo, hi in rs:
+                old = log.get(name, [])
+                if name.startswith("ps"):
+                    old = [e for e in old if e[2] == me or (nodes[e[2]]["q"] == q != "t")]
+                if w:
+                    old = [e for e in old if not (lo <= e[0] and e[1] <= hi)]
+                log[name] = old + [(lo, hi, me, w)]
+        return me
+
+    def cost(o, ins, k=1.0):
+        if o[4]:
+            return 50 + o[2] * SC * CY
+        if ins[0][4]:
+            return 50 + o[2] * GA * CY
+        if k == 1.0 and all(SIZE[SCRATCH[x[3]][2]] == 2 for x in [o] + ins):
+            k = 0.5
+        return 30 + max(64, max(o[2], ins[0][2]) * k) * CY
+
+    def ts(o, i, s1, op0, s2=None, op1=None):
+        if op1 is None:
+            node("v", [o], [i, s1], [lambda: g.vector.tensor_scalar(o[0], i[0], ap(s1), None, op0)], cost(o, [i]))
+        else:
+            node("v", [o], [i, s1, s2], [lambda: g.vector.tensor_scalar(o[0], i[0], ap(s1), ap(s2), op0, op1)], cost(o, [i]))
+
+    def tt(o, a, b, f):
+        k = 1.01 if "ps" in (a[3][:2], b[3][:2]) else 2.0
+        node("v", [o], [a, b], [lambda: g.vector.tensor_tensor(o[0], a[0], b[0], f)], cost(o, [a, b], k))
+
+    def cp(o, i):
+        node("v", [o], [i], [lambda: g.vector.tensor_copy(o[0], i[0])], cost(o, [i]))
+
+    def ms(o, c):
+        node("v", [o], [], [lambda: g.vector.memset(o[0], c)], cost(o, [o]))
+
+    def scan(o, d0, d1, init, op0, op1):
+        node("v", [o], [d0, d1, init], [lambda: g.vector.tensor_tensor_scan(o[0], d0[0], d1[0], ap(init), op0, op1)], cost(o, [d0, d1]))
+
+    def act(o, i, f=AF.Identity, bias=0.0, scale=1.0, acc=None):
+        c = cost(o, [i], 1.01) + 30
+        if acc is None:
+            node("a", [o], [i, bias, scale], [lambda: g.scalar.activation(o[0], i[0], f, bias=ap(bias), scale=ap(scale))], c)
+        else:
+            node("a", [o, acc], [i, bias, scale],
+                 [lambda: g.scalar.activation(o[0], i[0], f, bias=ap(bias), scale=ap(scale), accum_out=acc[0])], c)
+
+    def mm(o, l, rh, start=True, stop=True):
+        group.append((o, l, rh, start, stop))
+
+    def go():
+        ms_ = list(group)
+        del group[:]
+        em = [(lambda m=m: g.tensor.matmul(m[0][0], m[1][0], m[2][0], m[3], m[4])) for m in ms_]
+        c = sum(max(64, m[2][2]) * SIZE[SCRATCH[m[1][3]][2]] ** 2 / 4 * PE for m in ms_)
+        node("t", [m[0] for m in ms_], [m[1] for m in ms_] + [m[2] for m in ms_], em, c)
+
+    def iota(o, pat, base=0, ch=0, fl=True):
+        if fl:
+            node("g", [o], [], [lambda: g.iota(o[0], pat, base, ch, allow_small_or_imprecise_dtypes=True)], 130 + 2 * o[2])
+        else:
+            node("g", [o], [], [lambda: g.iota(o[0], pat, base, ch)], 130 + 2 * o[2])
+
+    def diagonal(o, i, fill):
+        node("g", [o], [i], [lambda: g.affine_select(o[0], i[0], [[-1, 128]], A.not_equal, fill, 0, 1)], 430.0)
+
+    def dma(pairs, lat=2200.0, add=False):
+        s = "d%d" % nd[0]
+        nd[0] += 1
+        if add:
+            em = [(lambda a=a, b=b: g.dma_start(ap(a), ap(b), accum_op=A.add, max_dma_last_dim=8192)) for a, b in pairs]
+        else:
+            em = [(lambda a=a, b=b: g.sync.dma_start(ap(a), ap(b))) for a, b in pairs]
+        node("g" if add else "s", [a for a, _ in pairs], [b for _, b in pairs], em, 100.0 * len(pairs), lat, 16, (s, 16 * len(pairs)))
+
+    eng_n, eng_p = topo.engines(core, nxt), topo.engines(core, prv)
+    eng_h = [e for e in topo.engines(core, hlp) if e not in eng_n]
+    sent = [0]
+
+    def send(items):
+        def em():
+            if len(items) == 1:
+                c, en, o, s, name = items[0]
+                rid, pid, _ = topo.addr(c)
+                return g.remote_dma(o, s[0], T.sem[name], T.sem["sent"], pid, rid, _mask(en))
+            tr = []
+            for c, en, o, s, name in items:
+                rid, pid, _ = topo.addr(c)
+                tr.append(RemoteDMATransfer(dst_ids=[DstId(rid=rid, pnc=pid)], dma_engine_mask=_mask(en),
+                                            remote_sem=T.sem[name], src=s[0], dst=o))
+            return g.remote_dma_fused(tr, local_sem=T.sem["sent"])
+        k = node("g", [], [it[3] for it in items], [em], 1200.0, 0.0, 0)
+        for it in items:
+            sends[it[4]] = k
+        sent[0] += sum(len(it[1]) for it in items)
+
+    n_in = len(topo.engines(prv, core))
+    n_bk = len(topo.engines(nxt, core))
+    n_h = len(topo.engines(helper_of(T, topo, (rank - 1) % n), core))
+
+    def arrive(name, outs, count, like=None, lat=2500.0):
+        node("x", outs, [], [], 0.0, lat, 0, ("a" + name, count), {sends[like or "a" + name]: 0})
+
+    def arrive_turned(name, b, lo, hi, d, count, like=None, lat=2500.0):
+        if not rot_in:
+            arrive(name, [r(b, lo, hi)], count, like, lat)
+            return
+        arrive(name, [dr(d, "d" + name)], count, like, lat)
+        dma([(r(b, lo, hi, p=(16, 128)), dr(d[0:112, :], "d" + name)), (r(b, lo, hi, p=(0, 16)), dr(d[112:128, :], "d" + name))])
+
+    def load_g(b, lo, hi, src, rows, c0, c1, lat):
+        if rot_out:
+            k = 7 * rows
+            dma([(r(b, lo, hi, p=(16, 128)), src[0:k, c0:c1]), (r(b, lo, hi, p=(0, 16)), src[k:k + rows, c0:c1])], lat)
+        else:
+            dma([(r(b, lo, hi), src[:, c0:c1])], lat)
+
+    load_g("MP", 0, 256, T["mp"], 1, 0, V, 2500.0)
+    dma([(r("B", 0, 2048), T["nb"][:, 0:2048]), (r("B", 2048, V), T["nb"][:, 2048:V])], 11000.0)
+    load_g("XS", 0, 2064, T["x"], 16, 0, 2064, 13500.0)
+    load_g("XS", 2064, V, T["x"], 16, 2064, V, 16000.0)
+    dma([(r("XH", 0, V), T["x"][:, :])], 21000.0)
+    dma([(r("KC", 0, 256), T["ky"][:, :]), (r("KC", 256, 512), T["iv"][:, :])], 21500.0)
+
+    iota(r("PI", 0, 1), [[0, 1]], 0, 1, False)
+    iota(r("QN"), [[0, 16], [1, 16]])
+    iota(r("N256"), [[1, 256]])
+    iota(r("GN"), [[1, 8], [0, 16]])
+    iota(r("IDX2"), [[16, 8], [0, 2], [1, 16]])
+    iota(r3("J2", 0, 8, 0, 32), [[0, 16], [4096, 16]])
+    iota(r("SEI"), [[16, 8], [1, 2]], 12)
+    cP, cQ, cG, cE1, cE0, cU, cAW, cLT, cBit, cTB, c1e, c1o, c2e, c2o, c14, cVo, cBp, c23, cTmp, cR1, cR2 = range(21)
+    SK, AK = 24, 40
+    (sAW, sDW, sDA, sOW0, sOW2, sNOW, sS, sSC, sVF, sUF, sUG, sKC, sT2, sO1, sO2, sO3, sPRE, sRES, sWIN, sB8, sSEL,
+     sB8n, sZ, sA1, sA2, sA3, sA4, sA5, sA6, sPW) = range(30)
+    uLB, uLT, uM, uU, uV, uES, uUS, uG, uG2 = range(9)
+    ID, NID, ID75, ID25, IDf = r("ID", 0, 128), r("ID", 128, 256), r("ID", 256, 384), r("ID", 384, 512), r("IDf", 0, 128)
+    ts(r("PI", 1, 2), r("PI", 0, 1), 15, A.bitwise_and)
+    ts(r("PI", 2, 3), r("PI", 0, 1), 4, A.logical_shift_right)
+    ts(r("PI", 3, 4), r("PI", 0, 1), 4, A.logical_shift_right, 1, A.bitwise_and)
+    cp(r("CO", 0, 4), r("PI", 0, 4))
+    ms(r("ONE"), 1.0)
+    ms(r("CC", 0, 8), 0.0)
+    ms(r("P", 128, 136), 9999.0)
+    ts(co(cE0), co(cE1), -1.0, A.mult, 1.0, A.add)
+    ts(co(cLT), co(cQ), 16.0, A.mult)
+    ts(co(cU), co(cG), 16.0, A.mult, 15.0, A.add)
+    ts(co(cAW), co(cQ), 2.0, A.mult, 1.0, A.add)
+    ts(co(cBit), co(cQ), 11.5, A.is_lt)
+    ts(co(cBp), co(cQ), 2.0, A.mult, 4096.0, A.add)
+    ts(r("DM"), r("QN"), co(cQ), A.is_equal)
+    ts(su(uLT), r("N256", 0, 16), co(cLT), A.add)
+    ts(r("CO", SK, SK + 12), r("DM", 0, 12), -2.0, A.mult, 1.0, A.add)
+    ms(sm(sA1), 2.0)
+    ms(sm(sZ), 0.0)
+    scan(sm(sPW), sm(sA1), sm(sZ), 0.5, A.mult, A.add)
+    ts(r("CO", AK, AK + 12), sm(sPW, 0, 12), r("DM", 14, 15), A.mult)
+    ts(IDf, r("N256", 0, 128), co(cP), A.is_equal)
+    act(ID, IDf)
+    act(NID, IDf, scale=-1.0)
+    act(ID75, IDf, scale=0.75)
+    act(ID25, IDf, scale=0.25)
+    act(r("BKI", 0, 1), co(cBit))
+    for k in range(12):
+        for a in range(0, 1 << k, 512):
+            b = min(a + 512, 1 << k)
+            act(r("BKI", (1 << k) + a, (1 << k) + b), r("BKI", a, b), bias=co(AK + k), scale=co(SK + k))
+    ts(r("SAMEG"), r("GN"), co(cG), A.is_equal)
+    ts(r("WF"), r("QN", 0, 128), co(cQ), A.is_ge)
+    tt(r("TRI"), r("WF"), r("SAMEG"), A.mult)
+    ts(sm(sAW), r("N256", 0, 16), 32.0, A.mult, co(cAW), A.add)
+    ts(r("UB"), r("N256", 0, 144), co(cU), A.is_equal)
+    act(r("I2A"), r("N256"), bias=1.0, scale=2.0)
+    ts(r("B", V, V + 8), r("N256", 0, 8), 0.0, A.mult, co(cBp), A.add)
+    ts(r3("ROT", 0, 8, 0, 32), r("IDX2"), co(cP), A.is_equal)
+    for i in range(16):
+        act(r("S", 128 * i, 128 * i + 128), IDf, scale=r("DM", i, i + 1))
+    for t in range(RO):
+        act(r("JT", 128 * t, 128 * t + 128), r3("J2", 0, 8, 16 - t, 32 - t))
+    ts(co(cTmp), r("DM", 14, 15), 0.5, A.mult, co(cBp), A.add)
+    ts(co(cVo), co(cTmp), -2048.0, A.add)
+    act(r("FW", 0, 256), r("N256"), bias=co(cVo), scale=0.0)
+    act(r("F", FP, FD), r("FW", 0, 32))
+    act(r("GV", 0, 256), r("N256"), bias=4096.0, scale=0.0)
+    ms(r("XH", V, 4384), 0.0)
+    ts(r("B8s"), r("N256", 0, 8), co(cG), A.is_equal, 65536.0, A.mult)
+    ts(r("M12"), r("QN"), 12.0, A.is_equal)
+    ts(r("RST", 0, 128), r("QN", 0, 128), 0.0, A.is_equal, 67108864.0, A.mult)
+    ts(co(cTmp), r("DM", 13, 14), 1.0 / 256, A.mult)
+    act(r("STA"), r("N256"), scale=co(cTmp))
+    act(r("UBf"), r("UB"), scale=r("DM", 14, 15))
+    act(r("BKI", V, V + 16), r("N256", 0, 16))
+    cp(su(uLB), r("N256", 0, 16))
+    ts(sm(sB8, 0, 8), r("N256", 0, 8), co(cG), A.is_equal)
+    act(sm(sB8n, 0, 8), sm(sB8, 0, 8), scale=-8192.0)
+    ts(sm(sSEL), r("SEI"), co(cP), A.is_equal)
+    act(sm(sDW), sm(sAW), bias=DUMP - 0.5, scale=0.5)
+    for hh in range(2):
+        ts(sm(sDA, 8 * hh, 8 * hh + 8), sm(sZ, 0, 8), co(cP), A.add, DUMP + 128.0 * hh, A.add)
+    act(sm(sOW0), sm(sDA), bias=6144.0 + DUMP / 256, scale=-1.0 / 256)
+    ms(sm(sOW2), 0.0)
+    tt(co(cTB), co(cBit), r("DM", 14, 15), A.add)
+    ts(co(c1e), co(cBit), co(cE0), A.mult, 512.0, A.mult)
+    ts(co(c1o), co(cBit), co(cE1), A.mult, 512.0, A.mult)
+    tt(co(c23), r("DM", 12, 13), r("DM", 13, 14), A.add)
+    act(co(c14), r("DM", 14, 15), scale=1.0 / 8192)
+    ts(co(c2e), co(c23), co(cE0), A.mult, -1.0, A.mult)
+    ts(co(c2o), co(c23), co(cE1), A.mult, -1.0, A.mult)
+    ms(r("BG", 2048, 2056), 4096)
+    ms(r("BG", 4104, 4112), 4096)
+    ms(r("XG", V, 4384), 0.0)
+
+    def level1(cc):
+        for b in range(16):
+            act(r("JK", 128 * b, 128 * b + 128), cc, AF.Sign, bias=sm(sAW, b, b + 1), scale=-1.0, acc=sm(sS, b, b + 1))
+
+    def level2():
+        ts(su(uM), sm(sS), 0.5, A.mult, 64.0, A.add)
+        act(r("MF"), sm(sS), bias=1024.0, scale=8.0)
+        tt(r("CMP"), ind(r("P", 0, 136), su(uM)), r("I2A"), A.is_lt)
+        mm(r("ps1", 0, 16), ID, r("MF"), True, False)
+        for q in range(16):
+            mm(r("ps1", 0, 16), r("UB", 15 - q, 143 - q), r("CMP", q, 256, 16), False, q == 15)
+        go()
+
+    ts(r3("T1", 0, 16, 0, 16), r("MP"), co(cE0), A.mult)
+    ts(r3("T1", 0, 16, 16, 32), r("MP"), co(cE1), A.mult)
+    node("v", [r3("T2", 0, 16, 0, 32)], [r3("T1", 0, 16, 0, 32)],
+         [lambda: g.vector.transpose(T["T2"][:, :, :], T["T1"][:, :, :])], 550.0)
+    tt(r("T3"), r3("T2", 0, 16, 0, 16), r3("T2", 0, 16, 16, 32), A.add)
+    cp(r("WS"), ind(r("T3"), su(uLT)))
+    send([(nxt, eng_n, T["WR"][:, :], r("WS"), "aW")])
+    arrive("W", [r("WR")], n_in, lat=4000.0)
+    for k in range(1, 9):
+        diagonal(r("PD", 128 * (k - 1), 128 * k), r3("ROT", 0, 8, k, k + 16), -1.0)
+    for k in range(1, 8):
+        diagonal(row("CK", k - 1, 128, 256), r3("ROT", 0, 8, 16 - k, 32 - k), 1.0)
+    act(row("CK", 7, 128, 256), IDf)
+    for k in range(8):
+        act(row("CK", k, 0, 128), row("CK", k, 128, 256), scale=-1048576.0)
+    ts(r("IF"), r("WS", 0, 128), 4095.5, A.is_gt, 2.0, A.mult)
+    mm(r("ps0", 0, 128), r("SAMEG"), r("IF"))
+    go()
+    mm(r("ps1", 0, 128), r("TRI"), r("IF"))
+    go()
+    scan(r("CC", 1, 129), r("ONE", 0, 128), r("ps0", 0, 128), 0.0, A.mult, A.add)
+    tt(r("P", 0, 128), r("ps1", 0, 128), r("CC", 0, 128), A.add)
+    level1(r("CC", 1, 129))
+    level2()
+    cp(r("U0"), r("ps1", 0, 16))
+    cp(su(uG), r("ps1", 0, 16))
+    ts(sm(sA3), r("U0"), 2047.5, A.is_gt, 2048.0, A.mult)
+    tt(sm(sA4), sm(sA3), r("U0"), A.add)
+    act(r("Y0"), ind(r("XS", 0, 2064), su(uG)), AF.Copy)
+    if rot_out:
+        for c, sh in ((cR1, 16), (cR2, 112)):
+            ts(r("PI", 4, 5), r("PI", 0, 1), float(sh), A.add)
+            ts(r("PI", 5, 6), r("PI", 4, 5), 127, A.bitwise_and)
+            cp(co(c), r("PI", 5, 6))
+        ts(r("IDf", 128, 256), r("N256", 0, 128), co(cR1), A.is_equal)
+        ts(r("IDf", 256, 384), r("N256", 0, 128), co(cR2), A.is_equal)
+        act(r("IDR"), r("IDf", 128, 256))
+        mm(r("ps0", 0, 16), r("IDf", 256, 384), sm(sA4))
+        go()
+        cp(su(uG2), r("ps0", 0, 16))
+        cp(r("T3"), ind(r("B", 0, V + 8), su(uG2)))
+        mm(r("ps0", 0, 256), r("IDf", 128, 256), r("T3"))
+        go()
+        cp(r("W0"), r("ps0", 0, 256))
+    else:
+        cp(su(uG2), sm(sA4))
+        cp(r("W0"), ind(r("B", 0, V + 8), su(uG2)))
+    send([(nxt, eng_n, T["WL"][:, :], r("W0"), "aw")])
+    arrive("w", [r("WL")], n_in)
+    send([(hlp, eng_h, T["HB"][:, 0:1024], r("B", 3072, V), "h1")])
+    send([(nxt, eng_n, T["YA"][:, :], r("Y0"), "ay")])
+    arrive("y", [r("YA")], n_in)
+    ts(r("ZC"), r("MP"), 1.0 / 8192, A.mult)
+    send([(nxt, eng_n, T["UR"][:, :], r("U0"), "au")])
+    arrive("u", [r("UR")], n_in)
+    send([(nxt, eng_n, T["dZ"][:, :], r("ZC"), "aZ")])
+    arrive("Z", [dr(None, "dZ")], n_in)
+    land = landing(T, rot_out)
+    send([(nxt, eng_n, land["B2"], r("B", 2048, 3072), "aB2"), (hlp, eng_h, T["HX"][:, :], r("XS", 2048, V), "h0")])
+    send([(nxt, eng_n, land["X0"], r("XS", 0, 2048), "aX0")])
+    arrive("X0", [r("XG", 0, 2048)], n_in, lat=20000.0)
+    arrive("X1", [r("XG", 2048, V)], n_h, "h0", 24000.0)
+    cp(r("KF"), r("KC"))
+    dma([(r("BKI", 0, V, p=(12, 128, 16)), r("KF", 0, 256)), (r("BKI", 0, V, p=(13, 128, 16)), r("KF", 256, 512))])
+    for k in range(4):
+        ts(r("F", FN + 1024 * k, FN + 1024 * k + 1024), ind(r("B", 0, V + 8), r("WR", 64 * k, 64 * k + 64)), -2048.0, A.add)
+
+    def expand(o, src, mask):
+        tt(o, ind(src, su(uLB)), mask, A.mult)
+
+    def to_wrapped(col, e, rhs, add=None):
+        if add is not None:
+            mm(r("ps0", col, col + 16), IDf, add, True, False)
+        for hh in range(2):
+            mm(r("ps0", col + 8 * hh, col + 8 * hh + 8), r(e, 128 * hh, 128 * hh + 128), rhs, add is None, add is None or hh == 1)
+        go()
+
+    for t in range(RO):
+        lo = 2048 * (t % 2)
+        end = t == RO - 1
+        uf = r("UR") if t == 0 else sm(sUF)
+
+        def fg(c):
+            ts(r("FO", 1024 * c, 1024 * c + 1024), ind(r("F", FN, FD), r("WL", 64 * c, 64 * c + 64)), CR, A.add, CR, A.subtract)
+            for i in range(16):
+                j = (i - t) % 16
+                mm(r("ps0", 0, 64), r("S", 128 * i, 128 * i + 128), r("FO", 1024 * c + j, 1024 * c + 1024, 16), i == 0, i == 15)
+            go()
+
+        def ev(c):
+            ts(r("VO", 64 * c, 64 * c + 64), r("ps0", 0, 64), 2048.0, A.add)
+            cp(r("V16", 64 * c, 64 * c + 64), r("ps0", 0, 64))
+            for k in range(8):
+                mm(r("ps1", 64 * k, 64 * k + 64), r("PD", 128 * k, 128 * k + 128), r("V16", 64 * c, 64 * c + 64))
+            go()
+
+        def eq(c):
+            hh, o = c // 2, 64 * (c % 2)
+            ts((T["EQ"][:, 8 * hh:8 * hh + 8, o:o + 64], [("EQ", 4 * c, 4 * c + 1)], 512, "EQ", ""), r("ps1"), 0.0, A.is_equal)
+
+        def xg(c):
+            xo, xi = r("XO", 1024 * c, 1024 * c + 1024), ind(r("XH", 0, DUMP), r("VO", 64 * c, 64 * c + 64))
+            if c in XG_V:
+                cp(xo, xi)
+            else:
+                act(xo, xi, AF.Copy)
+
+        def ab(c, u):
+            hh, o = c // 2, 64 * (c % 2)
+            bank = "ps%d" % (2 + (2 * c + u) % 3)
+            for k in range(8):
+                mm(r(bank, 64 * k, 64 * k + 64), ID, r("XO", 1024 * c + 8 * u + k, 1024 * c + 1024, 16), True, False)
+                mm(r(bank, 64 * k, 64 * k + 64), NID, r("YA", 64 * c, 64 * c + 64), False, True)
+            go()
+            k = 16 * hh + 8 * u
+            act((T["AB"][:, k:k + 8, o:o + 64], [("AB", 8 * hh + 4 * u + c % 2, 8 * hh + 4 * u + c % 2 + 1)], 512, "AB", ""),
+                r(bank), AF.Abs)
+
+        def support(hh):
+            bank, a, b = "ps%d" % (6 + hh), 128 * hh, 128 * hh + 128
+            eqs = [(T["EQ"][:, 8 * hh + k, :], [("EQ", 8 * hh, 8 * hh + 8)], 128, "EQ", "") for k in range(8)]
+            for k in range(8):
+                mm(r("ps5", a, b), eqs[k], row("CK", k, 128, 256), k == 0, k == 7)
+            go()
+            if hh in PEN_V:
+                ts(r("PEN", a, b), r("ps5", a, b), 0.5, A.is_lt, 33554432.0, A.mult)
+            else:
+                act(r("PEN", a, b), r("ps5", a, b), AF.Relu, bias=33554432.0, scale=-33554432.0)
+            for k in range(8):
+                mm(r(bank, 0, 128), eqs[k], row("CK", k, 0, 128), k == 0, False)
+            mm(r(bank, 0, 128), r("V16", a, b), ID, False, False)
+            mm(r(bank, 0, 128), r("ONE", 0, 128, p=(0, 1)), r("JT", 128 * t, 128 * t + 128, p=(0, 1)), False, False)
+            go()
+            mm(r(bank, 0, 128), ID, r("PEN", a, b), False, False)
+            go()
+
+        def best(hh):
+            bank, a, b = "ps%d" % (6 + hh), 128 * hh, 128 * hh + 128
+            for u in range(2):
+                for i in range(8 * u, 8 * u + 8):
+                    mm(r(bank, i, 128, 16), (T["AB"][:, 16 * hh + i, :], [("AB", 8 * hh + 4 * u, 8 * hh + 4 * u + 2)], 128, "AB", ""),
+                       r("B8s"), False, i == 15)
+                go()
+            scan(r("KS", a, b), r("RST", 0, 128), r(bank, 0, 128), 0.0, A.add, A.min)
+
+        def features(_):
+            if t > 0:
+                cp(ind(r("XG"), r("LU", 16 * t - 16, 16 * t)), r("XU", 256 * t - 256, 256 * t))
+                act(r("YA"), ind(r("XG", lo, lo + 2064), su(uU)), AF.Copy)
+
+        def numbers(_):
+            if t > 0:
+                act(r("EU"), ind(r("BKI", lo, lo + 2064), su(uU)), AF.Copy)
+
+        def keys(_):
+            if t > 0:
+                cp(ind(r("BKI"), r("VS", 16 * t - 16, 16 * t)), r("NEW"))
+
+        s0 = 2048 - lo
+        if not end:
+            for a in range(s0, s0 + 2048, 512):
+                act(r("FL", a, a + 512), r("F", FN + a, FN + a + 512), AF.Sign, bias=-2047.75)
+        chain[0] = {}
+        step = dict(g=features, u=numbers, k=keys, f=fg, e=ev, q=eq, x=xg, s=support, b=best,
+                    a=lambda c: ab(c, 0), c=lambda c: ab(c, 1))
+        for w in ORDER.split():
+            step[w[0]](int(w[1]))
+        chain[0] = None
+        if t == 0:
+            dma([(r("F", FN, FP, p=(14, 128, 16)), dr(T["dZ"][:, :], "dZ"))], 2800.0, True)
+            for k in (2, 3):
+                arrive_turned("B%d" % k, "BG", 1024 * k + 8, 1024 * k + 1032, T["dB"][k], n_h if k % 2 else n_in,
+                              "h1" if k % 2 else None, 20000.0)
+            cp(su(uU), uf)
+            act(r("EU"), ind(r("BKI", lo, lo + 2064), su(uU)), AF.Copy)
+        if end:
+            arrive("M", [dr(None, "dM")], n_bk, lat=8000.0)
+            dma([(r("F", FN, FP, p=(14, 128, 16)), dr(T["dM"][:, :], "dM"))])
+        act(sm(sUG), uf, bias=float(lo))
+
+        sY, sV, sC = r("SI", 0, 16), r("SI", 16, 32), r("SI", 32, 48)
+        ts(sY, r("KS", 15, 256, 16), 2048.0, A.add, CAP, A.min)
+        ts(sV, sY, 4095, A.bitwise_and)
+        ts(sC, sY, 16, A.arith_shift_right)
+        expand(r("E1"), sV, r("DM"))
+        to_wrapped(0, "E1", sm(sB8, 0, 8))
+        ts(sm(sSC), sC, -16.0, A.add)
+        expand(r("E2"), sm(sSC), r("M12"))
+        cp(su(uV), r("ps0", 0, 16))
+        cp(sm(sVF), r("ps0", 0, 16))
+        act(r("G1"), ind(r("BKI", 0, V), su(uV)), AF.Copy)
+        if end:
+            send([(prv, eng_p, T["GV"][:, 256:512], r("G1"), "aG")])
+            arrive("G", [r("GV", 256, 512)], n_bk)
+        mm(r("ps1", 0, 256), ID, r("STA"), True, False)
+        for hh in range(2):
+            mm(r("ps1", 128 * hh, 128 * hh + 128), r("E2", 128 * hh, 128 * hh + 128), ID, False, hh == 1)
+        go()
+        nv = 2 * RED_V
+        tt(sm(sNOW, nv, 16), sm(sSC, nv, 16), sm(sOW0, nv, 16), A.subtract)
+        tt(sm(sOW2, 0, nv), sm(sOW0, 0, nv), sm(sSC, 0, nv), A.subtract)
+        ts(r("TB"), r("G1"), co(cTB), A.mult)
+        act(r("LE"), r("G1"), bias=co(c2e), scale=co(c1e))
+        act(r("LO"), r("G1"), bias=co(c2o), scale=co(c1o))
+        for hh in range(2):
+            mm(r("ps0", 32 + 16 * hh, 48 + 16 * hh), r("G1", 128 * hh, 128 * hh + 128), sm(sSEL))
+        go()
+        tt(r("R"), r("ps1", 0, 256), r("TB"), A.add)
+        ts(sm(sKC), r("ps0", 32, 64, 2), 220.0, A.min)
+        tt(sm(sO1), r("ps0", 33, 64, 2), sm(sDA), A.subtract)
+        ts(sm(sO2), r("ps0", 33, 64, 2), 4095.5, A.is_lt)
+        tt(sm(sT2), sm(sSC), sm(sKC), A.is_lt)
+        tt(sm(sO3), sm(sO1), sm(sO2), A.mult)
+        tt(sm(sPRE), sm(sO3), sm(sT2), A.mult)
+        expand(r("E3"), sm(sPRE), r("DM"))
+        expand(r("E4"), sm(sT2), r("DM"))
+
+        todo = sorted(range(8), key=lambda k: (k if k < RED_V else (k - RED_V - 0.5) * RED_V / (8.0 - RED_V)))
+        for x, k in enumerate(todo):
+            gp, hh, bank = k % 4, k // 4, ("ps2", "ps3", "ps4", "ps6", "ps7")[x % 5]
+            p = (32 * gp, 32 * gp + 32)
+            for e in range(2):
+                mm(r(bank, 256 * e, 256 * e + 256), r("LO" if e else "LE", 128 * hh, 128 * hh + 128, p=p), r("R", p=p))
+                go()
+            for e in range(2):
+                col = 2 * k + e
+                src, res = r(bank, 256 * e, 256 * e + 256), sm(sRES, col, col + 1)
+                if k < RED_V:
+                    node("v", [res], [src], [lambda res=res, src=src: g.vector.tensor_reduce(res[0], src[0], AxisListType.X, A.max)], 290.0)
+                else:
+                    act(r("JK", 256 * col, 256 * col + 256), src, AF.Relu, bias=sm(sNOW, col, col + 1), acc=res)
+        mm(r("ps1", 256, 512), r("UBf", 2, 130), r("EU"), True, False)
+        mm(r("ps1", 256, 512), IDf, r("TB"), False, False)
+        for hh in range(2):
+            mm(r("ps1", 256 + 128 * hh, 384 + 128 * hh), r("E2", 128 * hh, 128 * hh + 128), ID, False, hh == 1)
+        go()
+        act(r("NEW"), r("ps1", 256, 512))
+        vs = r("VS", 16 * t, 16 * t + 16)
+        tt(sm(sWIN), sm(sRES), sm(sOW2), A.is_le)
+        expand(r("E5"), sm(sWIN), r("E3"))
+        to_wrapped(64, "E5", sm(sB8, 0, 8), sm(sDW))
+        cp(su(uES), r("ps0", 64, 80))
+        expand(r("E6"), sm(sWIN), r("E4"))
+        to_wrapped(80, "E6", sm(sB8n, 0, 8), sm(sDW))
+        tt(sm(sA5), r("ps0", 80, 96), sm(sUG), A.max)
+        tt(sm(sA6), r("ps0", 80, 96), sm(sVF), A.max)
+        cp(su(uUS), sm(sA5))
+        cp(vs, sm(sA6))
+        if end:
+            send([(prv, eng_p, T["ML"][:, :], su(uES, 32), "aE")])
+            arrive("E", [r("ML")], n_bk)
+            cp(ind(r("BKI"), vs), r("NEW"))
+            dma([(T["yk"][:, :], r("BKI", 0, V, p=(12, 128, 16)))])
+            cp(ind(r("F", FN, FE), r("ML", 0, 16)), r("GV", 0, 256))
+            cp(ind(r("F", FN, FE), r("ML", 16, 32)), r("GV", 256, 512))
+            if rot_out:
+                dma([(T["ym"][0:7, :], r("F", FN, FP, p=(30, 128, 16))), (T["ym"][7:8, :], r("F", FN, FP, p=(14, 15)))])
+            else:
+                dma([(T["ym"][:, :], r("F", FN, FP, p=(14, 128, 16)))])
+            break
+
+        nx = r("NX", 256 * t, 256 * t + 256)
+        act(r("XT"), ind(r("XH", 0, V), su(uV)), bias=-0.5)
+        mm(r("ps5", 256, 512), ID75, r("XT"), True, False)
+        mm(r("ps5", 256, 512), ID25, r("YA"), False, True)
+        go()
+        ts(nx, r("ps5", 256, 512), CR, A.add, CR, A.subtract)
+        nxo, vso = nx, vs
+        if rot_out:
+            nxo, vso = r("NR", 256 * t, 256 * t + 256), r("VR", 16 * t, 16 * t + 16)
+            mm(r("ps5", 0, 256), r("IDR"), nx)
+            go()
+            act(nxo, r("ps5", 0, 256))
+            mm(r("ps0", 96, 112), r("IDf", 128, 256), sm(sA6))
+            go()
+            cp(vso, r("ps0", 96, 112))
+        send([(nxt, eng_n, T["XU"][:, 256 * t:256 * t + 256], nxo, "aN%d" % t)])
+        send([(nxt, eng_n, T["LU"][:, 16 * t:16 * t + 16], vso, "aL%d" % t)])
+        if t == 0:
+            send([(nxt, eng_n, land["B0"], r("B", 0, 1024), "aB0"), (hlp, eng_h, T["HB"][:, 1024:2048], r("B", 1024, 2048), "h2")])
+        act(r("FB"), r("G1"), bias=-2048.0, scale=co(c14))
+        tt(r("FW", 256, 512), ind(r("B", 0, V), su(uV)), r("FB"), A.add)
+        cp(ind(r("FL"), su(uES)), r("ONE", 0, 256))
+        scan(r("CUM"), r("ONE"), r("FL", s0, s0 + 2048), 0.0, A.add, A.add)
+        level1(r("CUM", 15, 2048, 16))
+        for q in range(16):
+            mm(r("ps2", 0, 128), r("S", 128 * q, 128 * q + 128), r("CUM", q, 2048, 16), q == 0, q == 15)
+        go()
+        cp(r("P", 0, 128), r("ps2", 0, 128))
+        cp(ind(r("F", FN, FE), su(uES)), r("FW", 0, 256))
+        cp(ind(r("F", FN, FE), su(uUS)), r("FW", 256, 512))
+        cp(ind(r("XH"), vs), nx)
+        level2()
+        arrive("N%d" % t, [r("XU", 256 * t, 256 * t + 256)], n_in, lat=3500.0)
+        arrive("L%d" % t, [r("LU", 16 * t, 16 * t + 16)], n_in, lat=3500.0)
+        if t == 0:
+            for k in (0, 1):
+                arrive_turned("B%d" % k, "BG", 1024 * k, 1024 * k + 1024, T["dB"][k], n_h if k % 2 else n_in,
+                              "h2" if k % 2 else None, 20000.0)
+        cp(su(uU), r("ps1", 0, 16))
+        cp(sm(sUF), r("ps1", 0, 16))
+        b0 = 2056 if t % 2 == 0 else 0
+        cp(r("WL"), ind(r("BG", b0, b0 + 2056), su(uU)))
+        if t == RO - 2:
+            dma([(r("FC"), r("F", FN, FP, p=(14, 128, 16)))])
+            act(r("FR", 0, 256), r("FC"), bias=CR)
+            act(r("FR", 256, 512), r("FR", 0, 256), bias=-CR)
+            tt(r("MO", 0, 256), r("FC"), r("FR", 256, 512), A.subtract)
+            act(r("MO", 256, 512), r("MO", 0, 256), scale=8192.0)
+            send([(prv, eng_p, T["dM"][:, :], r("MO", 256, 512), "aM")])
+
+    final, wait = emit_in_planned_order(nodes, Q, T)
+    final["sent"] = sent[0]
+    for s in final:
+        wait("g", s, final[s])

@@ -3,14 +3,15 @@ from concourse.mybir import AluOpType as A, AxisListType, ActivationFunctionType
 
 V = 4096
 RO = 4
-FN, FP, FD, FE = 256, 4352, 4384, 4640
+FN, FP, FD, FE = 256, 4352, 4384, 4896
 DUMP = 4128
 CR = 12582912.0
-CAP = 241.0 * 65536
-XG_V = (3,)
-PEN_V = (1,)
-RED_V = 4
-ORDER = "f0 g0 e0 u0 x0 f1 q0 e1 a0 c0 x1 f2 q1 e2 x2 s0 f3 q2 e3 a1 c1 x3 q3 a2 c2 s1 b0 k0 a3 c3 b1"
+CAP = 1040.0 * 65536
+PEN = 134217728.0
+OPT = dict(XG_V=(3,), PEN_V=(1,), RED_V=(1, 4), Z_A=(4, 0), FB_A=((0, 1024), (1024, 1920)), FB_V=((1920, 4096),),
+           ORDER="p0 f0 g0 e0 d0 x0 f1 p1 q0 e1 d1 x1 a0 c0 f2 q1 e2 d2 x2 s0 a1 c1 f3 q2 e3 d3 x3 a2 c2 q3 b0 s1 a3 c3 k0 b1",
+           ORDER2="c t m p1 p2 p3 h f p4 p0 s z p5 p6 p7 x y w a u l n e",
+           LAST="c h p4 p0 p5 p1 p6 p2 p7 p3 t a n l")
 CY, PE, GA, SC, HOP = 1.0, 0.5, 1.5, 3.5, 80.0
 
 f32, bf, f16, i32, u16 = "float32", "bfloat16", "float16", "int32", "uint16"
@@ -21,38 +22,41 @@ def _sb(n, dt):
 
 
 SCRATCH = {
-    "B": _sb(4104, i32), "F": _sb(FE, f32), "BG": _sb(4112, i32), "XH": _sb(4384, bf), "XS": _sb(4096, bf),
-    "XG": _sb(4384, bf), "BKI": _sb(4384, f32), "FL": _sb(4384, bf),
+    "B": _sb(4104, i32), "BF": _sb(4104, f32), "F": _sb(FE, f32), "BG": _sb(4112, i32), "XH": _sb(4384, bf),
+    "XS": _sb(4096, bf), "XG": _sb(4384, bf), "BKI": _sb(4384, f32),
     "FO": _sb(4096, f16), "XO": _sb(4096, bf), "AB": _sb([32, 128], bf), "EQ": _sb([16, 128], bf),
-    "VO": _sb(256, u16), "V16": _sb(256, f16), "WL": _sb(256, u16), "YA": _sb(256, bf),
-    "PI": _sb(8, i32), "CO": _sb(64, f32), "N256": _sb(256, f32), "QN": _sb(256, f32), "GN": _sb(128, f32),
-    "IDX2": _sb(256, f32), "J2": _sb([8, 32], f32), "SEI": _sb(16, f32),
-    "DM": _sb(256, f32), "M12": _sb(256, f32), "RST": _sb(256, f32), "I2A": _sb(256, f32), "STA": _sb(256, bf),
-    "UB": _sb(144, bf), "UBf": _sb(144, f32), "SAMEG": _sb(128, bf), "TRI": _sb(128, bf),
-    "ID": _sb(512, bf), "IDf": _sb(384, f32), "S": _sb(2048, bf), "ROT": _sb([8, 32], bf),
-    "PD": _sb(1024, bf), "CK": _sb([8, 256], bf), "JT": _sb(512, bf), "ONE": _sb(2048, bf),
-    "B8s": _sb(8, bf), "SM": _sb(16 * 32, f32), "SI": _sb(64, i32), "SU": _sb(16 * 12, u16), "MF": _sb(16, bf),
+    "VO": _sb(256, u16), "V16": _sb(256, f16), "WL": _sb(272, u16), "YA": _sb(256, bf),
+    "PI": _sb(8, i32), "CO": _sb(64, f32), "N256": _sb(256, f32), "QN": _sb(256, f32),
+    "NB": _sb(256, bf), "NBH": _sb(256, bf), "NH": _sb(256, f32),
+    "J2": _sb([8, 32], f32), "SEI": _sb(24, f32), "SEL": _sb(24, f32), "KO": _sb(48, bf),
+    "DM": _sb(256, f32), "RST": _sb(128, f32), "STA": _sb(256, bf),
+    "UB": _sb(144, bf), "UH": _sb(144, bf), "TRI": _sb(128, bf), "UPR": _sb(128, bf),
+    "TRC": _sb(128, bf), "MB": _sb(128, bf), "MU": _sb(384, bf),
+    "ID": _sb(512, bf), "IDf": _sb(256, f32), "S": _sb(2048, bf), "ROT": _sb([8, 32], bf),
+    "PD": _sb(1024, bf), "CK": _sb([8, 256], bf), "JT": _sb(512, bf), "ONE": _sb(256, bf), "ZERO": _sb(128, bf),
+    "B8": _sb(64, bf), "SM": _sb(16 * 24, f32), "SB": _sb(80, bf), "SI": _sb(64, i32), "SU": _sb(16 * 8, u16),
     "MP": _sb(256, i32), "T1": _sb([16, 32], f32), "T2": _sb([16, 32], f32), "T3": _sb(256, f32), "WS": _sb(256, u16),
-    "WF": _sb(128, f32), "IF": _sb(128, bf), "CC": _sb(136, f32), "ZC": _sb(256, f32), "W0": _sb(256, u16),
-    "Y0": _sb(256, bf), "U0": _sb(16, f32), "WR": _sb(256, u16), "UR": _sb(16, f32),
-    "KC": _sb(512, i32), "KF": _sb(512, f32),
-    "CUM": _sb(2048, bf), "P": _sb(136, f32), "CMP": _sb(256, bf), "JK": _sb(4096, bf),
-    "PEN": _sb(256, bf), "KS": _sb(256, f32),
-    "E1": _sb(256, f32), "E2": _sb(256, bf), "E3": _sb(256, f32), "E4": _sb(256, f32), "E5": _sb(256, f32),
-    "E6": _sb(256, f32), "EU": _sb(256, f32),
-    "G1": _sb(256, f32), "TB": _sb(256, f32), "R": _sb(256, bf), "LE": _sb(256, bf), "LO": _sb(256, bf),
-    "NEW": _sb(256, f32), "FB": _sb(256, f32), "FW": _sb(512, f32), "XT": _sb(256, bf),
-    "NX": _sb(768, bf), "VS": _sb(64, u16), "XU": _sb(768, bf), "LU": _sb(48, u16),
-    "FC": _sb(256, f32), "FR": _sb(512, f32), "MO": _sb(512, f32), "GV": _sb(512, f32), "ML": _sb(32, u16),
-    "HX": _sb(2048, bf), "HB": _sb(2048, i32), "NR": _sb(768, bf), "VR": _sb(48, u16), "IDR": _sb(128, bf),
+    "IF": _sb(128, bf), "ZC": _sb(256, f32), "ZN": _sb(256, f32), "W0": _sb(272, u16),
+    "Y0": _sb(256, bf), "WR": _sb(256, u16),
+    "KC": _sb(1024, i32), "KF": _sb(768, f32),
+    "OH": _sb(2048, bf), "OQ": _sb(256, bf), "FT": _sb(128, bf), "QB": _sb(144, bf), "Z": _sb([16, 128], bf),
+    "P": _sb(136, f32), "CMP": _sb(256, bf), "JK": _sb(4096, bf),
+    "PEN": _sb(256, bf), "SUP": _sb(256, bf), "KS": _sb(256, f32),
+    "E1": _sb(256, f32), "E2": _sb(256, bf), "E5": _sb(256, bf), "EU": _sb(256, bf),
+    "G1": _sb(256, f32), "R": _sb(256, bf), "LE": _sb(256, bf), "LO": _sb(256, bf),
+    "NEW": _sb(256, f32), "FW": _sb(512, f32), "XT": _sb(256, bf),
+    "VAL": _sb(96, f32), "DW3": _sb(48, f32), "LF": _sb(48, f32), "LS": _sb(192, u16),
+    "NX": _sb(768, bf), "XU": _sb(768, bf), "LU": _sb(48, u16),
+    "FC": _sb(256, f32), "FR": _sb(512, f32), "MO": _sb(512, f32), "GV": _sb(512, f32), "GO": _sb(256, f32),
+    "ML": _sb(32, u16), "NR": _sb(768, bf), "VR": _sb(48, u16), "IDR": _sb(128, bf),
     "dZ": ("dram", [128, 256], f32), "dM": ("dram", [128, 256], f32), "dB": ("dram", [4, 128, 1024], i32),
 }
 for _k in range(8):
     SCRATCH["ps%d" % _k] = ("psum", [128, 512], f32)
 SIZE = {f32: 4, i32: 4, bf: 2, f16: 2, u16: 2}
 
-MSG = ["W", "w", "y", "u", "Z", "X0", "X1", "B0", "B1", "B2", "B3", "N0", "N1", "N2", "L0", "L1", "L2", "M", "G", "E"]
-SEMAPHORES = (["qv", "qa", "qt", "qg", "sent", "h0", "h1", "h2"] + ["a" + m for m in MSG]
+MSG = ["W", "w", "y", "Z", "X0", "X1", "B0", "B1", "B2", "B3", "N0", "N1", "N2", "L0", "L1", "L2", "M", "G", "E"]
+SEMAPHORES = (["qv", "qa", "qt", "qg", "sent", "sx", "go", "h0", "h1", "h2"] + ["a" + m for m in MSG]
               + ["d%d" % k for k in range(30)])
 
 
@@ -87,7 +91,7 @@ def helper_program(g, core, T, topo, r):
     rid, pid, _ = topo.addr(nxt)
     m = topo.mask(core, nxt)
     tot = 0
-    for s, src, name in (("h1", T["HB"][:, 0:1024], "B3"), ("h0", T["HX"][:, :], "X1"), ("h2", T["HB"][:, 1024:2048], "B1")):
+    for s, src, name in (("h1", T["BG"][:, 0:1024], "B3"), ("h0", T["XG"][:, 0:2048], "X1"), ("h2", T["BG"][:, 1024:2048], "B1")):
         g.wait_ge(T.sem[s], cnt)
         g.remote_dma(land[name], src, T.sem["a" + name], T.sem["sent"], pid, rid, m)
         tot += len(topo.engines(core, nxt))
@@ -101,7 +105,7 @@ def emit_in_planned_order(nodes, Q, T):
             succ[p].append(i)
     prio = [0.0] * len(nodes)
     for i in range(len(nodes) - 1, -1, -1):
-        prio[i] = nodes[i]["cost"] + nodes[i]["lat"] + max([prio[s] for s in succ[i]] + [0.0])
+        prio[i] = nodes[i]["cost"] + nodes[i]["lat"] + max([prio[s] + HOP for s in succ[i]] + [0.0])
     left = [len(nd["pre"]) for nd in nodes]
     at = [0.0] * len(nodes)
     free = {}
@@ -119,7 +123,7 @@ def emit_in_planned_order(nodes, Q, T):
         free[nd["q"]] = st[i] + nd["cost"]
         order.append(i)
         for s in succ[i]:
-            done = st[i] + nd["cost"] + (nd["lat"] + HOP if nodes[s]["pre"][i] != 0 else 0.0)
+            done = st[i] + nd["cost"] + (nd["lat"] + HOP if nodes[s]["pre"][i] != 0 or nd["q"] == "x" else 0.0)
             at[s] = max(at[s], done)
             left[s] -= 1
             if left[s] == 0:
@@ -199,6 +203,9 @@ def rank_program(g, core, T, topo):
     def sm(k, lo=0, hi=16):
         return r("SM", 16 * k + lo, 16 * k + hi)
 
+    def sb(k, lo=0, hi=16):
+        return r("SB", 16 * k + lo, 16 * k + hi)
+
     def su(k, w=16):
         return r("SU", 16 * k, 16 * k + w)
 
@@ -219,7 +226,7 @@ def rank_program(g, core, T, topo):
     def ap(x):
         return x[0] if isinstance(x, tuple) else x
 
-    def node(q, outs, ins, emit, cost, lat=0.0, inc=1, tok=None, extra=None):
+    def node(q, outs, ins, emit, cost, lat=0.0, inc=1, tok=None, extra=None, keep=True):
         rd2, wr = regs(outs, True)
         rd = regs(ins)[0] + rd2
         me = len(nodes)
@@ -245,7 +252,7 @@ def rank_program(g, core, T, topo):
             chain[0][q] = me
         nodes.append(dict(q=q, emit=emit, cost=cost, lat=lat, inc=inc, tok=tok, pre=pre))
         for rs, w in ((wr, True), (rd, False)):
-            for name, lo, hi in rs:
+            for name, lo, hi in (rs if keep else []):
                 old = log.get(name, [])
                 if name.startswith("ps"):
                     old = [e for e in old if e[2] == me or (nodes[e[2]]["q"] == q != "t")]
@@ -282,6 +289,9 @@ def rank_program(g, core, T, topo):
     def scan(o, d0, d1, init, op0, op1):
         node("v", [o], [d0, d1, init], [lambda: g.vector.tensor_tensor_scan(o[0], d0[0], d1[0], ap(init), op0, op1)], cost(o, [d0, d1]))
 
+    def red(o, i, f):
+        node("v", [o], [i], [lambda: g.vector.tensor_reduce(o[0], i[0], AxisListType.X, f)], cost(o, [i], 1.01))
+
     def act(o, i, f=AF.Identity, bias=0.0, scale=1.0, acc=None):
         c = cost(o, [i], 1.01) + 30
         if acc is None:
@@ -306,38 +316,42 @@ def rank_program(g, core, T, topo):
         else:
             node("g", [o], [], [lambda: g.iota(o[0], pat, base, ch)], 130 + 2 * o[2])
 
-    def diagonal(o, i, fill):
-        node("g", [o], [i], [lambda: g.affine_select(o[0], i[0], [[-1, 128]], A.not_equal, fill, 0, 1)], 430.0)
+    def select(o, i, pat, f, fill, base, ch):
+        node("g", [o], [i], [lambda: g.affine_select(o[0], i[0], pat, f, fill, base, ch)], 170 + 2 * o[2])
 
-    def dma(pairs, lat=2200.0, add=False):
+    def diagonal(o, i, fill):
+        select(o, i, [[-1, 128]], A.not_equal, fill, 0, 1)
+
+    def dma(pairs, lat=2200.0, add=False, extra=None):
         s = "d%d" % nd[0]
         nd[0] += 1
         if add:
             em = [(lambda a=a, b=b: g.dma_start(ap(a), ap(b), accum_op=A.add, max_dma_last_dim=8192)) for a, b in pairs]
         else:
             em = [(lambda a=a, b=b: g.sync.dma_start(ap(a), ap(b))) for a, b in pairs]
-        node("g" if add else "s", [a for a, _ in pairs], [b for _, b in pairs], em, 100.0 * len(pairs), lat, 16, (s, 16 * len(pairs)))
+        node("g" if add else "s", [a for a, _ in pairs], [b for _, b in pairs], em, 100.0 * len(pairs), lat, 16,
+             (s, 16 * len(pairs)), extra)
 
     eng_n, eng_p = topo.engines(core, nxt), topo.engines(core, prv)
     eng_h = [e for e in topo.engines(core, hlp) if e not in eng_n]
-    sent = [0]
+    sent = {"sent": 0, "sx": 0}
 
-    def send(items):
+    def send(items, local="sent", c=1200.0):
         def em():
             if len(items) == 1:
-                c, en, o, s, name = items[0]
-                rid, pid, _ = topo.addr(c)
-                return g.remote_dma(o, s[0], T.sem[name], T.sem["sent"], pid, rid, _mask(en))
+                d, en, o, s, name = items[0]
+                rid, pid, _ = topo.addr(d)
+                return g.remote_dma(o, s[0], T.sem[name], T.sem[local], pid, rid, _mask(en))
             tr = []
-            for c, en, o, s, name in items:
-                rid, pid, _ = topo.addr(c)
+            for d, en, o, s, name in items:
+                rid, pid, _ = topo.addr(d)
                 tr.append(RemoteDMATransfer(dst_ids=[DstId(rid=rid, pnc=pid)], dma_engine_mask=_mask(en),
                                             remote_sem=T.sem[name], src=s[0], dst=o))
-            return g.remote_dma_fused(tr, local_sem=T.sem["sent"])
-        k = node("g", [], [it[3] for it in items], [em], 1200.0, 0.0, 0)
+            return g.remote_dma_fused(tr, local_sem=T.sem[local])
+        k = node("g", [], [it[3] for it in items], [em], c, 0.0, 0, keep=False)
         for it in items:
             sends[it[4]] = k
-        sent[0] += sum(len(it[1]) for it in items)
+        sent[local] += sum(len(it[1]) for it in items)
 
     n_in = len(topo.engines(prv, core))
     n_bk = len(topo.engines(nxt, core))
@@ -353,202 +367,275 @@ def rank_program(g, core, T, topo):
         arrive(name, [dr(d, "d" + name)], count, like, lat)
         dma([(r(b, lo, hi, p=(16, 128)), dr(d[0:112, :], "d" + name)), (r(b, lo, hi, p=(0, 16)), dr(d[112:128, :], "d" + name))])
 
-    def load_g(b, lo, hi, src, rows, c0, c1, lat):
+    def load_g(b, lo, hi, src, rows, c0, c1, lat, extra=None):
         if rot_out:
             k = 7 * rows
-            dma([(r(b, lo, hi, p=(16, 128)), src[0:k, c0:c1]), (r(b, lo, hi, p=(0, 16)), src[k:k + rows, c0:c1])], lat)
+            dma([(r(b, lo, hi, p=(16, 128)), src[0:k, c0:c1]), (r(b, lo, hi, p=(0, 16)), src[k:k + rows, c0:c1])], lat, extra=extra)
         else:
-            dma([(r(b, lo, hi), src[:, c0:c1])], lat)
+            dma([(r(b, lo, hi), src[:, c0:c1])], lat, extra=extra)
 
-    load_g("MP", 0, 256, T["mp"], 1, 0, V, 2500.0)
-    dma([(r("B", 0, 2048), T["nb"][:, 0:2048]), (r("B", 2048, V), T["nb"][:, 2048:V])], 11000.0)
-    load_g("XS", 0, 2064, T["x"], 16, 0, 2064, 13500.0)
-    load_g("XS", 2064, V, T["x"], 16, 2064, V, 16000.0)
-    dma([(r("XH", 0, V), T["x"][:, :])], 21000.0)
-    dma([(r("KC", 0, 256), T["ky"][:, :]), (r("KC", 256, 512), T["iv"][:, :])], 21500.0)
-
-    iota(r("PI", 0, 1), [[0, 1]], 0, 1, False)
-    iota(r("QN"), [[0, 16], [1, 16]])
-    iota(r("N256"), [[1, 256]])
-    iota(r("GN"), [[1, 8], [0, 16]])
-    iota(r("IDX2"), [[16, 8], [0, 2], [1, 16]])
-    iota(r3("J2", 0, 8, 0, 32), [[0, 16], [4096, 16]])
-    iota(r("SEI"), [[16, 8], [1, 2]], 12)
-    cP, cQ, cG, cE1, cE0, cU, cAW, cLT, cBit, cTB, c1e, c1o, c2e, c2o, c14, cVo, cBp, c23, cTmp, cR1, cR2 = range(21)
-    SK, AK = 24, 40
-    (sAW, sDW, sDA, sOW0, sOW2, sNOW, sS, sSC, sVF, sUF, sUG, sKC, sT2, sO1, sO2, sO3, sPRE, sRES, sWIN, sB8, sSEL,
-     sB8n, sZ, sA1, sA2, sA3, sA4, sA5, sA6, sPW) = range(30)
-    uLB, uLT, uM, uU, uV, uES, uUS, uG, uG2 = range(9)
+    (cP, cQ, cG, cE1, cE0, cU, cLT, cBit, cBp, cVo, cHi, cH1, cL1, cL2, cO1, cO2, cMB, cPW, cW14, cW15, cWV,
+     cUH, cNB, cZN, cST, cLo, cOff, cA, cB, cC) = range(30)
+    SK = 32
+    (sOW0, sOW1, sOW2, sOW3, sNOW, sSC, sT2, sLO, sRES, sACC, sB8, sZ, sA1, sA2, sA3, sA4, sPW, sU0, sF8) = range(19)
+    bCC, bHX, bN8, bOFF = range(4)
+    uLB, uLT, uM, uV, uG2 = range(5)
+    uU = r("WL", 256, 272)
     ID, NID, ID75, ID25, IDf = r("ID", 0, 128), r("ID", 128, 256), r("ID", 256, 384), r("ID", 384, 512), r("IDf", 0, 128)
+    B8, B8s, B8n = r("B8", 0, 8), r("B8", 16, 24), r("B8", 32, 40)
+    one1 = r("ONE", 0, 128, p=(0, 1))
+    found = r("ps5", 272, 288)
+    xs = "XS" if rot_out else "XH"
+    land = landing(T, rot_out)
+
+    def fill(o, c):
+        act(o, r("N256", 0, o[2]), bias=c, scale=0.0)
+
+    def gate(k):
+        return {node("g", [], [], [lambda: g.sem_inc(T.sem["go"], 1)], 30.0, 0.0, 0, ("go", k)): 1}
+
+    def between(o, lo_, hi_):
+        select(o, r("ONE", 0, o[2]), lo_[0], A.is_ge, 0.0, lo_[1], lo_[2])
+        select(o, o, hi_[0], A.is_ge, 0.0, hi_[1], hi_[2])
+
+    def counts():
+        mm(r("ps5", 256, 264), r("QB", 1, 129), B8)
+        mm(r("ps5", 384, 512), r("TRI"), r("QB", 1, 129), True, False)
+        mm(r("ps5", 384, 512), r("UPR"), r("QB", 0, 128), False, True)
+        go()
+        cp(sb(bCC, 0, 8), r("ps5", 256, 264))
+        cp(r("P", 0, 128), r("ps5", 384, 512))
+
+    def level1(z_=1):
+        for k in range(8):
+            z = (T["Z"][:, :, 16 * k:16 * k + 16], [("Z", k, k + 1)], 256, "Z", "")
+            if k < 8 - OPT["Z_A"][z_]:
+                ts(z, r("NB"), sb(bCC, k, k + 1), A.is_lt, 2.0, A.mult)
+            else:
+                act(z, r("NH"), AF.Sign, bias=sb(bCC, k, k + 1), scale=-1.0)
+        column(z_, True)
+
+    def column(z_, stop):
+        mm(found, ID, sb(bOFF + z_), True, False)
+        for b in range(16):
+            mm(r("ps5", 272 + b, 273 + b), (T["Z"][:, b, :], [("Z", 0, 8)], 128, "Z", ""), sb(bN8, 0, 1), False, stop and b == 15)
+        go()
+
+    def level2(z_=1):
+        ts(su(uM), found, 1.0 / 16, A.mult, 128.0, A.add)
+        column(z_, False)
+        tt(r("CMP"), ind(r("P", 0, 136), su(uM)), r("N256"), A.is_le)
+        for q in range(16):
+            mm(found, r("UB", 15 - q, 143 - q), r("CMP", q, 256, 16), False, q == 15)
+        go()
+
+    def as_float(k):
+        ts(r("BF", 1024 * k, 1024 * k + 1024), r("B", 1024 * k, 1024 * k + 1024), -2048.0, A.add)
+
+    def codes(k0, k1):
+        for k in range(k0, k1):
+            for a in range(0, 1 << k, 1024):
+                b = min(a + 1024, 1 << k)
+                act(r("BKI", (1 << k) + a, (1 << k) + b), r("BKI", a, b), scale=co(SK + k))
+
+    chain[0] = {}
+    load_g("MP", 0, 256, T["mp"], 1, 0, V, 2000.0)
+    for k in range(4):
+        dma([(r("B", 1024 * k, 1024 * k + 1024), T["nb"][:, 1024 * k:1024 * k + 1024])], 3500.0 + 1900.0 * k)
+    dma([(r("KC", 0, 256), T["ky"][:, :]), (r("KC", 256, 512), T["iv"][:, :])], 10000.0)
+    iota(r("PI", 0, 1), [[0, 1]], 0, 1, False)
+    iota(r("N256"), [[1, 256]])
+    iota(r("QN"), [[0, 16], [1, 16]])
+    ms(r("ONE"), 1.0)
+    between(r("TRI"), ([[-16, 8], [0, 16]], 0, 1), ([[16, 8], [1, 16]], 0, -1))
+    between(r("UPR"), ([[-16, 8], [-1, 16]], -1, 1), ([[16, 8], [0, 16]], 15, -1))
+    select(r3("ROT", 0, 8, 0, 32), r("ONE"), [[-16, 8], [0, 2], [-1, 16]], A.is_equal, 0.0, 0, 1)
     ts(r("PI", 1, 2), r("PI", 0, 1), 15, A.bitwise_and)
     ts(r("PI", 2, 3), r("PI", 0, 1), 4, A.logical_shift_right)
     ts(r("PI", 3, 4), r("PI", 0, 1), 4, A.logical_shift_right, 1, A.bitwise_and)
     cp(r("CO", 0, 4), r("PI", 0, 4))
-    ms(r("ONE"), 1.0)
-    ms(r("CC", 0, 8), 0.0)
-    ms(r("P", 128, 136), 9999.0)
-    ts(co(cE0), co(cE1), -1.0, A.mult, 1.0, A.add)
-    ts(co(cLT), co(cQ), 16.0, A.mult)
-    ts(co(cU), co(cG), 16.0, A.mult, 15.0, A.add)
-    ts(co(cAW), co(cQ), 2.0, A.mult, 1.0, A.add)
-    ts(co(cBit), co(cQ), 11.5, A.is_lt)
-    ts(co(cBp), co(cQ), 2.0, A.mult, 4096.0, A.add)
-    ts(r("DM"), r("QN"), co(cQ), A.is_equal)
-    ts(su(uLT), r("N256", 0, 16), co(cLT), A.add)
-    ts(r("CO", SK, SK + 12), r("DM", 0, 12), -2.0, A.mult, 1.0, A.add)
-    ms(sm(sA1), 2.0)
-    ms(sm(sZ), 0.0)
-    scan(sm(sPW), sm(sA1), sm(sZ), 0.5, A.mult, A.add)
-    ts(r("CO", AK, AK + 12), sm(sPW, 0, 12), r("DM", 14, 15), A.mult)
+    ms(r("QB", 0, 16), 0.0)
+    act(co(cE0), co(cE1), bias=1.0, scale=-1.0)
+    act(co(cLT), co(cQ), scale=16.0)
+    act(co(cU), co(cG), bias=15.0, scale=16.0)
+    act(co(cBp), co(cQ), bias=4096.0, scale=2.0)
     ts(IDf, r("N256", 0, 128), co(cP), A.is_equal)
-    act(ID, IDf)
-    act(NID, IDf, scale=-1.0)
-    act(ID75, IDf, scale=0.75)
-    act(ID25, IDf, scale=0.25)
-    act(r("BKI", 0, 1), co(cBit))
-    for k in range(12):
-        for a in range(0, 1 << k, 512):
-            b = min(a + 512, 1 << k)
-            act(r("BKI", (1 << k) + a, (1 << k) + b), r("BKI", a, b), bias=co(AK + k), scale=co(SK + k))
-    ts(r("SAMEG"), r("GN"), co(cG), A.is_equal)
-    ts(r("WF"), r("QN", 0, 128), co(cQ), A.is_ge)
-    tt(r("TRI"), r("WF"), r("SAMEG"), A.mult)
-    ts(sm(sAW), r("N256", 0, 16), 32.0, A.mult, co(cAW), A.add)
+    ts(B8, r("N256", 0, 8), co(cG), A.is_equal)
+    ts(su(uLT), r("N256", 0, 16), co(cLT), A.add)
+    for k in range(2):
+        if OPT["Z_A"][k]:
+            ts(co(cOff), co(cG), 7.5 - OPT["Z_A"][k], A.is_gt, -1024.0, A.mult)
+            fill(sb(bOFF + k), co(cOff))
+        else:
+            ms(sb(bOFF + k), 0.0)
+    ts(co(cBit), co(cQ), 11.5, A.is_lt)
+    ts(r("DM"), r("QN"), co(cQ), A.is_equal)
     ts(r("UB"), r("N256", 0, 144), co(cU), A.is_equal)
-    act(r("I2A"), r("N256"), bias=1.0, scale=2.0)
-    ts(r("B", V, V + 8), r("N256", 0, 8), 0.0, A.mult, co(cBp), A.add)
-    ts(r3("ROT", 0, 8, 0, 32), r("IDX2"), co(cP), A.is_equal)
-    for i in range(16):
-        act(r("S", 128 * i, 128 * i + 128), IDf, scale=r("DM", i, i + 1))
-    for t in range(RO):
-        act(r("JT", 128 * t, 128 * t + 128), r3("J2", 0, 8, 16 - t, 32 - t))
-    ts(co(cTmp), r("DM", 14, 15), 0.5, A.mult, co(cBp), A.add)
-    ts(co(cVo), co(cTmp), -2048.0, A.add)
-    act(r("FW", 0, 256), r("N256"), bias=co(cVo), scale=0.0)
-    act(r("F", FP, FD), r("FW", 0, 32))
-    act(r("GV", 0, 256), r("N256"), bias=4096.0, scale=0.0)
-    ms(r("XH", V, 4384), 0.0)
-    ts(r("B8s"), r("N256", 0, 8), co(cG), A.is_equal, 65536.0, A.mult)
-    ts(r("M12"), r("QN"), 12.0, A.is_equal)
-    ts(r("RST", 0, 128), r("QN", 0, 128), 0.0, A.is_equal, 67108864.0, A.mult)
-    ts(co(cTmp), r("DM", 13, 14), 1.0 / 256, A.mult)
-    act(r("STA"), r("N256"), scale=co(cTmp))
-    act(r("UBf"), r("UB"), scale=r("DM", 14, 15))
-    act(r("BKI", V, V + 16), r("N256", 0, 16))
-    cp(su(uLB), r("N256", 0, 16))
-    ts(sm(sB8, 0, 8), r("N256", 0, 8), co(cG), A.is_equal)
-    act(sm(sB8n, 0, 8), sm(sB8, 0, 8), scale=-8192.0)
-    ts(sm(sSEL), r("SEI"), co(cP), A.is_equal)
-    act(sm(sDW), sm(sAW), bias=DUMP - 0.5, scale=0.5)
-    for hh in range(2):
-        ts(sm(sDA, 8 * hh, 8 * hh + 8), sm(sZ, 0, 8), co(cP), A.add, DUMP + 128.0 * hh, A.add)
-    act(sm(sOW0), sm(sDA), bias=6144.0 + DUMP / 256, scale=-1.0 / 256)
-    ms(sm(sOW2), 0.0)
-    tt(co(cTB), co(cBit), r("DM", 14, 15), A.add)
-    ts(co(c1e), co(cBit), co(cE0), A.mult, 512.0, A.mult)
-    ts(co(c1o), co(cBit), co(cE1), A.mult, 512.0, A.mult)
-    tt(co(c23), r("DM", 12, 13), r("DM", 13, 14), A.add)
-    act(co(c14), r("DM", 14, 15), scale=1.0 / 8192)
-    ts(co(c2e), co(c23), co(cE0), A.mult, -1.0, A.mult)
-    ts(co(c2o), co(c23), co(cE1), A.mult, -1.0, A.mult)
-    ms(r("BG", 2048, 2056), 4096)
-    ms(r("BG", 4104, 4112), 4096)
-    ms(r("XG", V, 4384), 0.0)
-
-    def level1(cc):
-        for b in range(16):
-            act(r("JK", 128 * b, 128 * b + 128), cc, AF.Sign, bias=sm(sAW, b, b + 1), scale=-1.0, acc=sm(sS, b, b + 1))
-
-    def level2():
-        ts(su(uM), sm(sS), 0.5, A.mult, 64.0, A.add)
-        act(r("MF"), sm(sS), bias=1024.0, scale=8.0)
-        tt(r("CMP"), ind(r("P", 0, 136), su(uM)), r("I2A"), A.is_lt)
-        mm(r("ps1", 0, 16), ID, r("MF"), True, False)
-        for q in range(16):
-            mm(r("ps1", 0, 16), r("UB", 15 - q, 143 - q), r("CMP", q, 256, 16), False, q == 15)
-        go()
-
+    act(r("NB"), r("N256"))
+    act(ID, IDf)
+    fill(r("P", 128, 136), 9999.0)
+    fill(sb(bN8, 0, 2), -8.0)
+    act(r("NH"), r("N256"), bias=0.5)
     ts(r3("T1", 0, 16, 0, 16), r("MP"), co(cE0), A.mult)
     ts(r3("T1", 0, 16, 16, 32), r("MP"), co(cE1), A.mult)
     node("v", [r3("T2", 0, 16, 0, 32)], [r3("T1", 0, 16, 0, 32)],
          [lambda: g.vector.transpose(T["T2"][:, :, :], T["T1"][:, :, :])], 550.0)
     tt(r("T3"), r3("T2", 0, 16, 0, 16), r3("T2", 0, 16, 16, 32), A.add)
     cp(r("WS"), ind(r("T3"), su(uLT)))
-    send([(nxt, eng_n, T["WR"][:, :], r("WS"), "aW")])
-    arrive("W", [r("WR")], n_in, lat=4000.0)
+    send([(nxt, eng_n, T["WR"][:, :], r("WS"), "aW")], c=3000.0)
+    arrive("W", [r("WR")], n_in, lat=3000.0)
+    load_g(xs, 0, 2064 if rot_out else V, T["x"], 16, 0, 2064 if rot_out else V, 6000.0, gate(1))
+    act(co(cVo), co(cBp), bias=-2048.0)
+    fill(r("BF", V, V + 8), co(cVo))
+    act(r("CO", SK, SK + 12), r("DM", 0, 12), bias=1.0, scale=-2.0)
+    act(r("BKI", 0, 1), co(cBit))
+    codes(0, 10)
+    if rot_out:
+        act(r("IDf", 128, 256), IDf)
+        act(r("IDR"), r("IDf", 112, 240))
+
+    ts(r("IF"), r("WS", 0, 128), 4095.5, A.is_gt)
+    scan(r("QB", 1, 129), r("ONE", 0, 128), r("IF"), 0.0, A.mult, A.add)
     for k in range(1, 9):
         diagonal(r("PD", 128 * (k - 1), 128 * k), r3("ROT", 0, 8, k, k + 16), -1.0)
-    for k in range(1, 8):
-        diagonal(row("CK", k - 1, 128, 256), r3("ROT", 0, 8, 16 - k, 32 - k), 1.0)
-    act(row("CK", 7, 128, 256), IDf)
-    for k in range(8):
-        act(row("CK", k, 0, 128), row("CK", k, 128, 256), scale=-1048576.0)
-    ts(r("IF"), r("WS", 0, 128), 4095.5, A.is_gt, 2.0, A.mult)
-    mm(r("ps0", 0, 128), r("SAMEG"), r("IF"))
-    go()
-    mm(r("ps1", 0, 128), r("TRI"), r("IF"))
-    go()
-    scan(r("CC", 1, 129), r("ONE", 0, 128), r("ps0", 0, 128), 0.0, A.mult, A.add)
-    tt(r("P", 0, 128), r("ps1", 0, 128), r("CC", 0, 128), A.add)
-    level1(r("CC", 1, 129))
-    level2()
-    cp(r("U0"), r("ps1", 0, 16))
-    cp(su(uG), r("ps1", 0, 16))
-    ts(sm(sA3), r("U0"), 2047.5, A.is_gt, 2048.0, A.mult)
-    tt(sm(sA4), sm(sA3), r("U0"), A.add)
-    act(r("Y0"), ind(r("XS", 0, 2064), su(uG)), AF.Copy)
+    counts()
+    level1(0)
+    as_float(0)
+    codes(10, 12)
+    act(r("BKI", V, V + 16), r("N256", 0, 16))
+    for i in range(16):
+        act(r("S", 128 * i, 128 * i + 128), IDf, scale=r("DM", i, i + 1))
+    level2(0)
+    as_float(1)
+    ts(r("W0", 256, 272), found, 2048.0, A.add)
+    ts(sm(sA3), found, -0.5, A.is_gt, 2048.0, A.mult)
+    ts(sm(sU0), found, 2048.0, A.add)
+    ts(r("B", V, V + 8), r("N256", 0, 8), 0.0, A.mult, co(cBp), A.add)
+    tt(sm(sA4), sm(sA3), sm(sU0), A.add)
     if rot_out:
-        for c, sh in ((cR1, 16), (cR2, 112)):
-            ts(r("PI", 4, 5), r("PI", 0, 1), float(sh), A.add)
-            ts(r("PI", 5, 6), r("PI", 4, 5), 127, A.bitwise_and)
-            cp(co(c), r("PI", 5, 6))
-        ts(r("IDf", 128, 256), r("N256", 0, 128), co(cR1), A.is_equal)
-        ts(r("IDf", 256, 384), r("N256", 0, 128), co(cR2), A.is_equal)
-        act(r("IDR"), r("IDf", 128, 256))
-        mm(r("ps0", 0, 16), r("IDf", 256, 384), sm(sA4))
+        mm(r("ps0", 0, 16), r("IDf", 16, 144), sm(sA4))
         go()
+        as_float(2)
         cp(su(uG2), r("ps0", 0, 16))
         cp(r("T3"), ind(r("B", 0, V + 8), su(uG2)))
-        mm(r("ps0", 0, 256), r("IDf", 128, 256), r("T3"))
+        mm(r("ps0", 0, 256), r("IDf", 112, 240), r("T3"))
         go()
-        cp(r("W0"), r("ps0", 0, 256))
+        as_float(3)
+        cp(r("W0", 0, 256), r("ps0", 0, 256))
     else:
         cp(su(uG2), sm(sA4))
-        cp(r("W0"), ind(r("B", 0, V + 8), su(uG2)))
+        as_float(2)
+        cp(r("W0", 0, 256), ind(r("B", 0, V + 8), su(uG2)))
+        as_float(3)
     send([(nxt, eng_n, T["WL"][:, :], r("W0"), "aw")])
     arrive("w", [r("WL")], n_in)
-    send([(hlp, eng_h, T["HB"][:, 0:1024], r("B", 3072, V), "h1")])
+    if rot_out:
+        dma([(r("XH", 0, V), T["x"][:, :])], 5500.0, extra=gate(2))
+        load_g("XS", 2064, V, T["x"], 16, 2064, V, 7500.0)
+    for k in range(1, 8):
+        diagonal(row("CK", k - 1, 128, 256), r3("ROT", 0, 8, 16 - k, 32 - k), 1.0)
+
+    for a, b in OPT["FB_A"]:
+        act(r("F", FN + a, FN + b), ind(r("BF", 0, V + 8), r("WR", a // 16, b // 16)), AF.Copy)
+        if a == 0:
+            act(r("Y0"), ind(r(xs, 0, 2064), r("W0", 256, 272)), AF.Copy)
+    for a, b in OPT["FB_V"]:
+        ts(r("F", FN + a, FN + b), ind(r("B", 0, V + 8), r("WR", a // 16, b // 16)), -2048.0, A.add)
+    fill(r("F", FP, FD), co(cVo))
     send([(nxt, eng_n, T["YA"][:, :], r("Y0"), "ay")])
     arrive("y", [r("YA")], n_in)
     ts(r("ZC"), r("MP"), 1.0 / 8192, A.mult)
-    send([(nxt, eng_n, T["UR"][:, :], r("U0"), "au")])
-    arrive("u", [r("UR")], n_in)
     send([(nxt, eng_n, T["dZ"][:, :], r("ZC"), "aZ")])
-    arrive("Z", [dr(None, "dZ")], n_in)
-    land = landing(T, rot_out)
-    send([(nxt, eng_n, land["B2"], r("B", 2048, 3072), "aB2"), (hlp, eng_h, T["HX"][:, :], r("XS", 2048, V), "h0")])
-    send([(nxt, eng_n, land["X0"], r("XS", 0, 2048), "aX0")])
-    arrive("X0", [r("XG", 0, 2048)], n_in, lat=20000.0)
-    arrive("X1", [r("XG", 2048, V)], n_h, "h0", 24000.0)
-    cp(r("KF"), r("KC"))
-    dma([(r("BKI", 0, V, p=(12, 128, 16)), r("KF", 0, 256)), (r("BKI", 0, V, p=(13, 128, 16)), r("KF", 256, 512))])
-    for k in range(4):
-        ts(r("F", FN + 1024 * k, FN + 1024 * k + 1024), ind(r("B", 0, V + 8), r("WR", 64 * k, 64 * k + 64)), -2048.0, A.add)
+    arrive("Z", [dr(None, "dZ")], n_in, lat=8000.0)
+    act(co(cZN), co(cQ), scale=256.0 / 8192)
+    act(r("ZN"), r("N256"), bias=co(cZN), scale=1.0 / 8192)
+    dma([(r("BF", 0, V, p=(14, 128, 16)), r("ZN"))], 4000.0, True)
+    ts(r("KC", 512, 768), r("KC", 256, 512), 4, A.logical_shift_right)
+    ts(r("KC", 768, 1024), r("KC", 256, 512), 4096 + 15, A.bitwise_and)
+    cp(r("KF", 0, 256), r("KC", 0, 256))
+    cp(r("KF", 256, 768), r("KC", 512, 1024))
+    dma([(r("BKI", 0, V, p=(13 + k, 128, 16)), r("KF", 256 * k, 256 * k + 256)) for k in range(3)], 4000.0)
+    send([(nxt, eng_n, land["B2"], r("B", 2048, 3072), "aB2"), (hlp, eng_h, T["BG"][:, 0:1024], r("B", 3072, V), "h1")])
+    send([(nxt, eng_n, land["X0"], r(xs, 0, 2048), "aX0"), (hlp, eng_h, T["XG"][:, 0:2048], r(xs, 2048, V), "h0")], "sx")
+    send([(hlp, eng_h, T["BG"][:, 1024:2048], r("B", 1024, 2048), "h2")])
+    arrive("X0", [r("XG", 0, 2048)], n_in, lat=12000.0)
+    arrive("X1", [r("XG", 2048, V)], n_h, "h0", 14000.0)
+    iota(r3("J2", 0, 8, 0, 32), [[0, 16], [4096, 16]])
+    iota(r("SEI"), [[16, 8], [1, 3]], 13)
 
-    def expand(o, src, mask):
-        tt(o, ind(src, su(uLB)), mask, A.mult)
+    act(NID, IDf, scale=-1.0)
+    fill(r("XH", V, DUMP), 0.0)
+    chain[0] = None
+    act(row("CK", 7, 128, 256), IDf)
+    for k in range(8):
+        act(row("CK", k, 0, 128), row("CK", k, 128, 256), scale=-1048576.0)
+    act(B8s, B8, scale=65536.0)
+    for t in range(RO):
+        act(r("JT", 128 * t, 128 * t + 128), r3("J2", 0, 8, 16 - t, 32 - t))
+    fill(r("FW", 0, 256), co(cVo))
+    fill(r("ZERO"), 0.0)
+    act(B8n, B8, scale=-8192.0)
+    act(sm(sB8, 0, 8), B8)
+    act(sm(sF8, 0, 8), B8, scale=r("DM", 0, 1))
+    ts(r("RST"), r("QN", 0, 128), 0.0, A.is_equal, 4 * PEN, A.mult)
+    act(ID75, IDf, scale=0.75)
+    act(ID25, IDf, scale=0.25)
+    ts(r("TRC"), r("N256", 0, 128), co(cP), A.is_ge)
+    act(r("NBH"), r("N256"), bias=-127.5)
+    fill(r("GV", 0, 256), 4096.0)
+    fill(r("E2"), 0.0)
+    fill(r("KO"), 0.0)
+    fill(r("KO", 1, 48, 3), -127.5)
+    act(co(cST), r("DM", 12, 13), scale=1.0 / 256)
+    act(r("STA"), r("N256"), scale=co(cST))
+    cp(su(uLB), r("N256", 0, 16))
+    ts(r("SEL"), r("SEI"), co(cP), A.is_equal)
+    act(co(cLo), co(cQ), bias=float(DUMP))
+    act(r("DW3", 0, 32), r("N256", 0, 32), bias=co(cLo), scale=16.0)
+    act(r("DW3", 32, 48), r("N256", 0, 16), bias=co(cLo), scale=16.0)
+    act(co(cA), co(cP), bias=6144.0, scale=-1.0 / 256)
+    act(co(cB), co(cP), bias=6143.5, scale=-1.0 / 256)
+    fill(sm(sOW0, 0, 8), co(cA))
+    fill(sm(sOW0, 8, 16), co(cB))
+    act(sm(sOW1), sm(sOW0), bias=-1.0)
+    fill(sm(sOW2), -1.0)
+    act(co(cHi), r("DM", 14, 15), bias=r("DM", 15, 16))
+    act(co(cH1), co(cHi), bias=-1.0)
+    act(co(cL1), co(cBit), bias=co(cHi), scale=512.0)
+    act(co(cL2), co(cBit), bias=co(cH1))
+    act(co(cO1), co(cL1), scale=co(cE1))
+    act(co(cO2), co(cL2), scale=co(cE1))
+    act(co(cMB), co(cBit), scale=1.0 / 512)
+    act(r("MB"), IDf, scale=co(cMB))
+    fill(sm(sA1), 2.0)
+    fill(sm(sZ), 0.0)
+    scan(sm(sPW), sm(sA1), sm(sZ), 0.5, A.mult, A.add)
+    tt(sm(sA2), sm(sPW), r("DM", 0, 16), A.mult)
+    red(co(cPW), sm(sA2, 0, 12), A.add)
+    red(co(cC), sm(sA2, 0, 4), A.add)
+    act(co(cW15), co(cC), scale=-0.5)
+    act(co(cA), co(cC), scale=1.0 / 32)
+    act(co(cW14), co(cPW), bias=co(cA), scale=-1.0 / 32)
+    act(co(cWV), co(cPW), scale=-1.0 / 1024)
+    act(r("MU", 0, 128), r("UB", 1, 129), scale=co(cW14))
+    act(r("MU", 128, 256), r("UB", 0, 128), scale=co(cW15))
+    act(r("MU", 256, 384), r("UB", 1, 129), scale=co(cWV))
+    act(co(cUH), r("DM", 14, 15), bias=r("DM", 15, 16), scale=16.0)
+    act(r("UH"), r("UB"), scale=co(cUH))
+    act(co(cB), r("DM", 15, 16), scale=7.5)
+    act(co(cNB), r("DM", 14, 15), bias=co(cB), scale=127.5)
+    ms(r("BG", 2048, 2056), 4096)
+    ms(r("BG", 4104, 4112), 4096)
+    fill(r("XG", V, V + 16), 0.0)
 
-    def to_wrapped(col, e, rhs, add=None):
-        if add is not None:
-            mm(r("ps0", col, col + 16), IDf, add, True, False)
-        for hh in range(2):
-            mm(r("ps0", col + 8 * hh, col + 8 * hh + 8), r(e, 128 * hh, 128 * hh + 128), rhs, add is None, add is None or hh == 1)
-        go()
+    def expand(o, src, mask, f=A.mult):
+        tt(o, ind(src, su(uLB)), mask, f)
 
     for t in range(RO):
         lo = 2048 * (t % 2)
+        s0 = 2048 - lo
         end = t == RO - 1
-        uf = r("UR") if t == 0 else sm(sUF)
+        val = 48 * (t % 2)
 
         def fg(c):
             ts(r("FO", 1024 * c, 1024 * c + 1024), ind(r("F", FN, FD), r("WL", 64 * c, 64 * c + 64)), CR, A.add, CR, A.subtract)
@@ -560,6 +647,8 @@ def rank_program(g, core, T, topo):
         def ev(c):
             ts(r("VO", 64 * c, 64 * c + 64), r("ps0", 0, 64), 2048.0, A.add)
             cp(r("V16", 64 * c, 64 * c + 64), r("ps0", 0, 64))
+
+        def turned(c):
             for k in range(8):
                 mm(r("ps1", 64 * k, 64 * k + 64), r("PD", 128 * k, 128 * k + 128), r("V16", 64 * c, 64 * c + 64))
             go()
@@ -570,7 +659,7 @@ def rank_program(g, core, T, topo):
 
         def xg(c):
             xo, xi = r("XO", 1024 * c, 1024 * c + 1024), ind(r("XH", 0, DUMP), r("VO", 64 * c, 64 * c + 64))
-            if c in XG_V:
+            if c in OPT["XG_V"]:
                 cp(xo, xi)
             else:
                 act(xo, xi, AF.Copy)
@@ -590,17 +679,17 @@ def rank_program(g, core, T, topo):
             bank, a, b = "ps%d" % (6 + hh), 128 * hh, 128 * hh + 128
             eqs = [(T["EQ"][:, 8 * hh + k, :], [("EQ", 8 * hh, 8 * hh + 8)], 128, "EQ", "") for k in range(8)]
             for k in range(8):
-                mm(r("ps5", a, b), eqs[k], row("CK", k, 128, 256), k == 0, k == 7)
+                mm(r(bank, 0, 128), eqs[k], row("CK", k, 0, 128), k == 0, k == 7)
             go()
-            if hh in PEN_V:
-                ts(r("PEN", a, b), r("ps5", a, b), 0.5, A.is_lt, 33554432.0, A.mult)
+            if hh in OPT["PEN_V"]:
+                ts(r("PEN", a, b), r(bank, 0, 128), -0.5, A.is_gt, PEN, A.mult)
+                cp(r("SUP", a, b), r(bank, 0, 128))
             else:
-                act(r("PEN", a, b), r("ps5", a, b), AF.Relu, bias=33554432.0, scale=-33554432.0)
-            for k in range(8):
-                mm(r(bank, 0, 128), eqs[k], row("CK", k, 0, 128), k == 0, False)
-            mm(r(bank, 0, 128), r("V16", a, b), ID, False, False)
-            mm(r(bank, 0, 128), r("ONE", 0, 128, p=(0, 1)), r("JT", 128 * t, 128 * t + 128, p=(0, 1)), False, False)
-            go()
+                act(r("PEN", a, b), r(bank, 0, 128), AF.Relu, bias=PEN, scale=128.0)
+                act(r("SUP", a, b), r(bank, 0, 128))
+            mm(r(bank, 0, 128), r("V16", a, b), ID, True, False)
+            mm(r(bank, 0, 128), one1, r("JT", 128 * t, 128 * t + 128, p=(0, 1)), False, False)
+            mm(r(bank, 0, 128), ID, r("SUP", a, b), False, False)
             mm(r(bank, 0, 128), ID, r("PEN", a, b), False, False)
             go()
 
@@ -609,177 +698,234 @@ def rank_program(g, core, T, topo):
             for u in range(2):
                 for i in range(8 * u, 8 * u + 8):
                     mm(r(bank, i, 128, 16), (T["AB"][:, 16 * hh + i, :], [("AB", 8 * hh + 4 * u, 8 * hh + 4 * u + 2)], 128, "AB", ""),
-                       r("B8s"), False, i == 15)
+                       B8s, False, i == 15)
                 go()
-            scan(r("KS", a, b), r("RST", 0, 128), r(bank, 0, 128), 0.0, A.add, A.min)
+            scan(r("KS", a, b), r("RST"), r(bank, 0, 128), 0.0, A.add, A.min)
 
         def features(_):
             if t > 0:
                 cp(ind(r("XG"), r("LU", 16 * t - 16, 16 * t)), r("XU", 256 * t - 256, 256 * t))
-                act(r("YA"), ind(r("XG", lo, lo + 2064), su(uU)), AF.Copy)
-
-        def numbers(_):
-            if t > 0:
-                act(r("EU"), ind(r("BKI", lo, lo + 2064), su(uU)), AF.Copy)
+                act(r("YA"), ind(r("XG", lo, lo + 2064), uU), AF.Copy)
 
         def keys(_):
             if t > 0:
-                cp(ind(r("BKI"), r("VS", 16 * t - 16, 16 * t)), r("NEW"))
+                cp(ind(r("BKI"), r("LS", 48 * t - 16, 48 * t)), r("NEW"))
 
-        s0 = 2048 - lo
-        if not end:
-            for a in range(s0, s0 + 2048, 512):
-                act(r("FL", a, a + 512), r("F", FN + a, FN + a + 512), AF.Sign, bias=-2047.75)
+        def before(h):
+            if not end:
+                if h == 0:
+                    mm(r("ps5", 0, 128), one1, r("ZERO", p=(0, 1)), True, False)
+                for q in range(8 * h, 8 * h + 8):
+                    mm(r("ps5", q, 128, 16), r("F", FN + s0 + q, FN + s0 + 2048, 16), sm(sF8, 0, 8), False, False)
+                go()
+
+        if t == 0:
+            ts(r("VAL", 16, 32), uU, 0.0, A.add)
+            act(r("EU"), ind(r("BKI", 0, 2064), uU), AF.Copy)
         chain[0] = {}
-        step = dict(g=features, u=numbers, k=keys, f=fg, e=ev, q=eq, x=xg, s=support, b=best,
+        step = dict(g=features, k=keys, p=before, f=fg, e=ev, d=turned, q=eq, x=xg, s=support, b=best,
                     a=lambda c: ab(c, 0), c=lambda c: ab(c, 1))
-        for w in ORDER.split():
+        for w in OPT["ORDER"].split():
             step[w[0]](int(w[1]))
         chain[0] = None
         if t == 0:
             dma([(r("F", FN, FP, p=(14, 128, 16)), dr(T["dZ"][:, :], "dZ"))], 2800.0, True)
             for k in (2, 3):
                 arrive_turned("B%d" % k, "BG", 1024 * k + 8, 1024 * k + 1032, T["dB"][k], n_h if k % 2 else n_in,
-                              "h1" if k % 2 else None, 20000.0)
-            cp(su(uU), uf)
-            act(r("EU"), ind(r("BKI", lo, lo + 2064), su(uU)), AF.Copy)
+                              "h1" if k % 2 else None, 12000.0)
         if end:
             arrive("M", [dr(None, "dM")], n_bk, lat=8000.0)
             dma([(r("F", FN, FP, p=(14, 128, 16)), dr(T["dM"][:, :], "dM"))])
-        act(sm(sUG), uf, bias=float(lo))
 
         sY, sV, sC = r("SI", 0, 16), r("SI", 16, 32), r("SI", 32, 48)
-        ts(sY, r("KS", 15, 256, 16), 2048.0, A.add, CAP, A.min)
-        ts(sV, sY, 4095, A.bitwise_and)
-        ts(sC, sY, 16, A.arith_shift_right)
-        expand(r("E1"), sV, r("DM"))
-        to_wrapped(0, "E1", sm(sB8, 0, 8))
-        ts(sm(sSC), sC, -16.0, A.add)
-        expand(r("E2"), sm(sSC), r("M12"))
-        cp(su(uV), r("ps0", 0, 16))
-        cp(sm(sVF), r("ps0", 0, 16))
-        act(r("G1"), ind(r("BKI", 0, V), su(uV)), AF.Copy)
-        if end:
-            send([(prv, eng_p, T["GV"][:, 256:512], r("G1"), "aG")])
-            arrive("G", [r("GV", 256, 512)], n_bk)
-        mm(r("ps1", 0, 256), ID, r("STA"), True, False)
-        for hh in range(2):
-            mm(r("ps1", 128 * hh, 128 * hh + 128), r("E2", 128 * hh, 128 * hh + 128), ID, False, hh == 1)
-        go()
-        nv = 2 * RED_V
-        tt(sm(sNOW, nv, 16), sm(sSC, nv, 16), sm(sOW0, nv, 16), A.subtract)
-        tt(sm(sOW2, 0, nv), sm(sOW0, 0, nv), sm(sSC, 0, nv), A.subtract)
-        ts(r("TB"), r("G1"), co(cTB), A.mult)
-        act(r("LE"), r("G1"), bias=co(c2e), scale=co(c1e))
-        act(r("LO"), r("G1"), bias=co(c2o), scale=co(c1o))
-        for hh in range(2):
-            mm(r("ps0", 32 + 16 * hh, 48 + 16 * hh), r("G1", 128 * hh, 128 * hh + 128), sm(sSEL))
-        go()
-        tt(r("R"), r("ps1", 0, 256), r("TB"), A.add)
-        ts(sm(sKC), r("ps0", 32, 64, 2), 220.0, A.min)
-        tt(sm(sO1), r("ps0", 33, 64, 2), sm(sDA), A.subtract)
-        ts(sm(sO2), r("ps0", 33, 64, 2), 4095.5, A.is_lt)
-        tt(sm(sT2), sm(sSC), sm(sKC), A.is_lt)
-        tt(sm(sO3), sm(sO1), sm(sO2), A.mult)
-        tt(sm(sPRE), sm(sO3), sm(sT2), A.mult)
-        expand(r("E3"), sm(sPRE), r("DM"))
-        expand(r("E4"), sm(sT2), r("DM"))
+        red_v = OPT["RED_V"][end]
+        nv = 2 * red_v
+        vs = r("LS", 48 * t + 32, 48 * t + 48)
+        nx = r("NX", 256 * (t % 3), 256 * (t % 3) + 256)
+        banks = ["ps2", "ps3", "ps4", "ps7"]
 
-        todo = sorted(range(8), key=lambda k: (k if k < RED_V else (k - RED_V - 0.5) * RED_V / (8.0 - RED_V)))
-        for x, k in enumerate(todo):
-            gp, hh, bank = k % 4, k // 4, ("ps2", "ps3", "ps4", "ps6", "ps7")[x % 5]
-            p = (32 * gp, 32 * gp + 32)
+        def choice():
+            ts(sY, r("KS", 15, 256, 16), 2048.0, A.add, CAP, A.min)
+            ts(sV, sY, 4095, A.bitwise_and)
+            expand(r("E1"), sV, r("DM"))
+            for hh in range(2):
+                mm(r("ps0", 8 * hh, 8 * hh + 8), r("E1", 128 * hh, 128 * hh + 128), sm(sB8, 0, 8))
+            go()
+            ts(sC, sY, 16, A.arith_shift_right)
+            ts(r("E2", 13, 256, 16), sC, -16.0, A.add)
+            cp(su(uV), r("ps0", 0, 16))
+            act(r("G1"), ind(r("BKI", 0, V), su(uV)), AF.Copy)
+            ts(sm(sSC), sC, -16.0, A.add)
+            cp(r("VAL", val + 32, val + 48), r("ps0", 0, 16))
+            if nv < 16:
+                tt(sm(sNOW, nv, 16), sm(sSC, nv, 16), sm(sOW0, nv, 16), A.subtract)
+            if nv:
+                tt(sm(sOW2, 0, nv), sm(sOW1, 0, nv), sm(sSC, 0, nv), A.subtract)
+            act(r("LE"), r("G1"), bias=co(cL2), scale=co(cL1))
+            mm(r("ps6", 0, 48), one1, r("KO", p=(0, 1)), True, False)
+            for hh in range(2):
+                mm(r("ps6", 24 * hh, 24 * hh + 24), r("G1", 128 * hh, 128 * hh + 128), r("SEL"), False, hh == 1)
+            go()
+            mm(r("ps1", 0, 256), ID, r("STA"), True, False)
+            for hh in range(2):
+                mm(r("ps1", 128 * hh, 128 * hh + 128), r("E2", 128 * hh, 128 * hh + 128), ID, False, False)
+            go()
+            mm(r("ps1", 0, 256), r("MB"), r("LE"), False, True)
+            go()
+            act(r("R"), r("ps1", 0, 256))
+            act(r("LO"), r("G1"), bias=co(cO2), scale=co(cO1))
+            tt(sm(sT2), sm(sSC), r("ps6", 0, 48, 3), A.is_lt)
+
+        def marks():
+            tt(sb(bHX), sm(sT2), r("ps6", 1, 48, 3), A.mult)
+            cp(sm(sLO), r("ps6", 2, 48, 3))
+            for k in range(16):
+                ts(r("OH", 128 * k, 128 * k + 128), r("NBH", s0 // 16, s0 // 16 + 128), sb(bHX, k, k + 1), A.is_equal, 8192.0, A.mult)
+                if k == 0:
+                    expand(r("OQ"), sm(sLO), r("QN"), A.is_equal)
+                if k % 4 == 3:
+                    for m in range(k - 3, k + 1):
+                        mm(r("ps5", 16 * (m % 8), 16 * (m % 8) + 16), r("OH", 128 * m, 128 * m + 128), r("OQ", 16 * m, 16 * m + 16), False, m == 15)
+                    go()
+
+        def holders():
+            tt(sm(sOW3), sm(sOW2), sm(sT2), A.add)
+            for q in range(16):
+                mm(r("ps6", 64, 80), r("UH", 15 - q, 143 - q), r("LE", q, 256, 16), q == 0, q == 15)
+            go()
+            tt(r("VAL", val, val + 16), r("ps6", 64, 80), r("DW3", 0, 16), A.min)
+
+        def flags():
+            ts(r("FT"), r("ps5", 0, 128), 2047.5, A.is_gt)
+            mm(r("ps5", 128, 256), r("FT"), r("TRC"))
+            go()
+            cp(r("QB", 1, 129), r("ps5", 128, 256))
+
+        def pairs(k):
+            gp, hh, bank = k % 4, k // 4, banks.pop(0)
+            banks.append(bank)
             for e in range(2):
+                p = (32 * gp, 32 * gp + (32 if e else 16))
                 mm(r(bank, 256 * e, 256 * e + 256), r("LO" if e else "LE", 128 * hh, 128 * hh + 128, p=p), r("R", p=p))
                 go()
             for e in range(2):
                 col = 2 * k + e
                 src, res = r(bank, 256 * e, 256 * e + 256), sm(sRES, col, col + 1)
-                if k < RED_V:
-                    node("v", [res], [src], [lambda res=res, src=src: g.vector.tensor_reduce(res[0], src[0], AxisListType.X, A.max)], 290.0)
+                if k < red_v:
+                    red(res, src, A.max)
                 else:
                     act(r("JK", 256 * col, 256 * col + 256), src, AF.Relu, bias=sm(sNOW, col, col + 1), acc=res)
-        mm(r("ps1", 256, 512), r("UBf", 2, 130), r("EU"), True, False)
-        mm(r("ps1", 256, 512), IDf, r("TB"), False, False)
-        for hh in range(2):
-            mm(r("ps1", 256 + 128 * hh, 384 + 128 * hh), r("E2", 128 * hh, 128 * hh + 128), ID, False, hh == 1)
-        go()
-        act(r("NEW"), r("ps1", 256, 512))
-        vs = r("VS", 16 * t, 16 * t + 16)
-        tt(sm(sWIN), sm(sRES), sm(sOW2), A.is_le)
-        expand(r("E5"), sm(sWIN), r("E3"))
-        to_wrapped(64, "E5", sm(sB8, 0, 8), sm(sDW))
-        cp(su(uES), r("ps0", 64, 80))
-        expand(r("E6"), sm(sWIN), r("E4"))
-        to_wrapped(80, "E6", sm(sB8n, 0, 8), sm(sDW))
-        tt(sm(sA5), r("ps0", 80, 96), sm(sUG), A.max)
-        tt(sm(sA6), r("ps0", 80, 96), sm(sVF), A.max)
-        cp(su(uUS), sm(sA5))
-        cp(vs, sm(sA6))
+
+        def newkeys():
+            mm(r("ps1", 256, 512), r("MU", 0, 128), r("EU"), True, False)
+            mm(r("ps1", 256, 512), r("MU", 128, 256), r("EU"), False, False)
+            mm(r("ps1", 256, 512), r("MB"), r("LE"), False, False)
+            for hh in range(2):
+                mm(r("ps1", 256 + 128 * hh, 384 + 128 * hh), r("E2", 128 * hh, 128 * hh + 128), ID, False, hh == 1)
+            go()
+            act(r("NEW"), r("ps1", 256, 512), bias=co(cNB))
+
+        def theirs():
+            if end:
+                mm(r("ps0", 256, 512), r("MU", 256, 384), r("LE"))
+                go()
+                act(r("GO"), r("ps0", 256, 512), bias=2047.5)
+                send([(prv, eng_p, T["GV"][:, 256:512], r("GO"), "aG")])
+                arrive("G", [r("GV", 256, 512)], n_bk)
+            else:
+                act(r("XT"), ind(r("XH", 0, V), su(uV)), bias=-0.5)
+                mm(r("ps0", 256, 512), ID75, r("XT"), True, False)
+                mm(r("ps0", 256, 512), ID25, r("YA"), False, True)
+                go()
+
+        def mixed():
+            ts(nx, r("ps0", 256, 512), CR, A.add, CR, A.subtract)
+            nxo = nx
+            if rot_out:
+                nxo = r("NR", 256 * t, 256 * t + 256)
+                mm(r("ps6", 256, 512), r("IDR"), nx)
+                go()
+                act(nxo, r("ps6", 256, 512))
+            send([(nxt, eng_n, T["XU"][:, 256 * t:256 * t + 256], nxo, "aN%d" % t)])
+
+        def columns():
+            act(r("FW", 256, 512), ind(r("BF", 0, V), su(uV)), AF.Copy)
+
+        def accepted():
+            mm(r("ps0", 64, 112), IDf, r("DW3"), True, False)
+            go()
+            tt(sm(sACC), sm(sRES), sm(sOW3), A.is_le)
+            expand(r("E5"), sm(sACC), r("DM"))
+            for k in range(6):
+                mm(r("ps0", 64 + 8 * k, 72 + 8 * k), r("E5", 128 * (k % 2), 128 * (k % 2) + 128), B8n, False, k == 5)
+            go()
+
+        def lists():
+            tt(r("LF"), r("ps0", 64, 112), r("VAL", val, val + 48), A.max)
+            cp(r("LS", 48 * t, 48 * t + 48), r("LF"))
+            if end:
+                send([(prv, eng_p, T["ML"][:, :], r("LS", 48 * t, 48 * t + 32), "aE")])
+                return
+            vso = vs
+            if rot_out:
+                vso = r("VR", 16 * t, 16 * t + 16)
+                mm(r("ps6", 96, 112), r("IDf", 112, 240), r("LF", 32, 48))
+                go()
+                cp(vso, r("ps6", 96, 112))
+            send([(nxt, eng_n, T["LU"][:, 16 * t:16 * t + 16], vso, "aL%d" % t)])
+            if t == 0:
+                send([(nxt, eng_n, land["B0"], r("B", 0, 1024), "aB0")])
+
+        def askers():
+            ts(uU, found, 2048.0, A.add)
+            if t == 1:
+                arrive_turned("B1", "BG", 1024, 2048, T["dB"][1], n_h, "h2", 12000.0)
+                arrive_turned("B0", "BG", 0, 1024, T["dB"][0], n_in, None, 8000.0)
+            b0 = 2056 if t % 2 == 0 else 0
+            cp(r("WL", 0, 256), ind(r("BG", b0, b0 + 2056), uU))
+
+        def numbers():
+            act(r("VAL", 64 - val, 80 - val), found, bias=2048.0 + s0)
+            act(r("EU"), ind(r("BKI", s0, s0 + 2064), uU), AF.Copy)
+
+        chain[0] = {}
+        step = dict(c=choice, m=marks, h=holders, f=flags, n=newkeys, t=theirs, x=mixed, w=columns, a=accepted, l=lists,
+                    u=askers, e=numbers, s=counts, z=level1, y=level2)
+        for w in OPT["LAST" if end else "ORDER2"].split():
+            if w[0] == "p":
+                pairs(int(w[1]))
+            else:
+                step[w]()
         if end:
-            send([(prv, eng_p, T["ML"][:, :], su(uES, 32), "aE")])
             arrive("E", [r("ML")], n_bk)
             cp(ind(r("BKI"), vs), r("NEW"))
-            dma([(T["yk"][:, :], r("BKI", 0, V, p=(12, 128, 16)))])
-            cp(ind(r("F", FN, FE), r("ML", 0, 16)), r("GV", 0, 256))
-            cp(ind(r("F", FN, FE), r("ML", 16, 32)), r("GV", 256, 512))
+            dma([(T["yk"][:, :], r("BKI", 0, V, p=(13, 128, 16)))])
+            cp(ind(r("F", FN, FE), r("ML")), r("GV"))
             if rot_out:
                 dma([(T["ym"][0:7, :], r("F", FN, FP, p=(30, 128, 16))), (T["ym"][7:8, :], r("F", FN, FP, p=(14, 15)))])
             else:
                 dma([(T["ym"][:, :], r("F", FN, FP, p=(14, 128, 16)))])
             break
-
-        nx = r("NX", 256 * t, 256 * t + 256)
-        act(r("XT"), ind(r("XH", 0, V), su(uV)), bias=-0.5)
-        mm(r("ps5", 256, 512), ID75, r("XT"), True, False)
-        mm(r("ps5", 256, 512), ID25, r("YA"), False, True)
-        go()
-        ts(nx, r("ps5", 256, 512), CR, A.add, CR, A.subtract)
-        nxo, vso = nx, vs
-        if rot_out:
-            nxo, vso = r("NR", 256 * t, 256 * t + 256), r("VR", 16 * t, 16 * t + 16)
-            mm(r("ps5", 0, 256), r("IDR"), nx)
-            go()
-            act(nxo, r("ps5", 0, 256))
-            mm(r("ps0", 96, 112), r("IDf", 128, 256), sm(sA6))
-            go()
-            cp(vso, r("ps0", 96, 112))
-        send([(nxt, eng_n, T["XU"][:, 256 * t:256 * t + 256], nxo, "aN%d" % t)])
-        send([(nxt, eng_n, T["LU"][:, 16 * t:16 * t + 16], vso, "aL%d" % t)])
+        cp(ind(r("F", FN, FE), r("LS", 48 * t + 16, 48 * t + 32)), r("FW", 256, 512))
+        fo, fi = ind(r("F", FN, FE), r("LS", 48 * t, 48 * t + 16)), r("FW", 0, 256)
+        node("a", [fo], [fi], [lambda fo=fo, fi=fi: g.scalar.activation(fo[0], fi[0], AF.Silu)], cost(fo, [fi]))
         if t == 0:
-            send([(nxt, eng_n, land["B0"], r("B", 0, 1024), "aB0"), (hlp, eng_h, T["HB"][:, 1024:2048], r("B", 1024, 2048), "h2")])
-        act(r("FB"), r("G1"), bias=-2048.0, scale=co(c14))
-        tt(r("FW", 256, 512), ind(r("B", 0, V), su(uV)), r("FB"), A.add)
-        cp(ind(r("FL"), su(uES)), r("ONE", 0, 256))
-        scan(r("CUM"), r("ONE"), r("FL", s0, s0 + 2048), 0.0, A.add, A.add)
-        level1(r("CUM", 15, 2048, 16))
-        for q in range(16):
-            mm(r("ps2", 0, 128), r("S", 128 * q, 128 * q + 128), r("CUM", q, 2048, 16), q == 0, q == 15)
-        go()
-        cp(r("P", 0, 128), r("ps2", 0, 128))
-        cp(ind(r("F", FN, FE), su(uES)), r("FW", 0, 256))
-        cp(ind(r("F", FN, FE), su(uUS)), r("FW", 256, 512))
+            node("x", [], [r("XH")], [], 0.0, 0.0, 0, ("sx", sent["sx"]), {sends["aX0"]: 0})
         cp(ind(r("XH"), vs), nx)
-        level2()
+        chain[0] = None
         arrive("N%d" % t, [r("XU", 256 * t, 256 * t + 256)], n_in, lat=3500.0)
-        arrive("L%d" % t, [r("LU", 16 * t, 16 * t + 16)], n_in, lat=3500.0)
-        if t == 0:
-            for k in (0, 1):
-                arrive_turned("B%d" % k, "BG", 1024 * k, 1024 * k + 1024, T["dB"][k], n_h if k % 2 else n_in,
-                              "h2" if k % 2 else None, 20000.0)
-        cp(su(uU), r("ps1", 0, 16))
-        cp(sm(sUF), r("ps1", 0, 16))
-        b0 = 2056 if t % 2 == 0 else 0
-        cp(r("WL"), ind(r("BG", b0, b0 + 2056), su(uU)))
+        arrive("L%d" % t, [r("LU", 16 * t, 16 * t + 16)], n_in, lat=3000.0)
         if t == RO - 2:
             dma([(r("FC"), r("F", FN, FP, p=(14, 128, 16)))])
             act(r("FR", 0, 256), r("FC"), bias=CR)
             act(r("FR", 256, 512), r("FR", 0, 256), bias=-CR)
             tt(r("MO", 0, 256), r("FC"), r("FR", 256, 512), A.subtract)
-            act(r("MO", 256, 512), r("MO", 0, 256), scale=8192.0)
+            ts(r("FR", 0, 256), r("FC"), 2047.75, A.is_gt, 0.5, A.mult)
+            tt(r("FR", 256, 512), r("MO", 0, 256), r("FR", 0, 256), A.max)
+            act(r("MO", 256, 512), r("FR", 256, 512), scale=8192.0)
             send([(prv, eng_p, T["dM"][:, :], r("MO", 256, 512), "aM")])
 
     final, wait = emit_in_planned_order(nodes, Q, T)
-    final["sent"] = sent[0]
+    final.update(sent)
     for s in final:
         wait("g", s, final[s])

@@ -8,11 +8,11 @@ DUMP = 4128
 CR = 12582912.0
 CAP = 1040.0 * 65536
 PEN = 134217728.0
-OPT = dict(XG_V=(3,), PEN_V=(1,), RED_V=(1, 4), Z_A=(4, 0), FB_A=((0, 1024), (1024, 1920)), FB_V=((1920, 4096),),
-           ORDER="p0 f0 g0 e0 d0 x0 f1 p1 q0 e1 d1 x1 a0 c0 f2 q1 e2 d2 x2 s0 a1 c1 f3 q2 e3 d3 x3 a2 c2 q3 b0 s1 a3 c3 k0 b1",
-           ORDER2="c t m p1 p2 p3 h f p4 p0 s z p5 p6 p7 x y w a u l n e",
-           LAST="c h p4 p0 p5 p1 p6 p2 p7 p3 t a n l")
-CY, PE, GA, SC, HOP = 1.0, 0.5, 1.5, 3.5, 80.0
+OPT = dict(XG_V=(3,), PEN_V=(1,), RED_V=(0, 4), Z_A=(4, 0), FB_A=((0, 1024), (1024, 2304)), FB_V=((2304, 4096),),
+           ORDER="p0 f0 g0 p1 i0 f1 e0 x0 f2 d0 i1 y1 y0 a0 e1 i2 f3 e2 c0 d1 y2 x1 a1 A0 C0 x2 i3 q0 y4 y3 q1 s0 d2 e3 A1 d3 c1 C1 x3 a2 q2 r0 y5 b0 A2 c2 C2 q3 K0 a3 k0 s1 c3 B0 A3 r1 b1 C3 B1",
+           ORDER2="c p3 p2 t m0 p0 m1 p4 m2 m3 p5 f x Q p1 s p7 r p6 h z H d a y l w q g u n o e",
+           LAST="c p4 p0 p5 t p1 p6 p3 p2 p7 h H d a n l")
+CY, PE, GA, SC, HOP = 0.83, 0.47, 1.56, 3.8, 120.0
 
 f32, bf, f16, i32, u16 = "float32", "bfloat16", "float16", "int32", "uint16"
 
@@ -23,21 +23,21 @@ def _sb(n, dt):
 
 SCRATCH = {
     "B": _sb(4104, i32), "BF": _sb(4104, f32), "F": _sb(FE, f32), "BG": _sb(4112, i32), "XH": _sb(4384, bf),
-    "XS": _sb(4096, bf), "XG": _sb(4384, bf), "BKI": _sb(4384, f32),
+    "BKI": _sb(4384, f32),
     "FO": _sb(4096, f16), "XO": _sb(4096, bf), "AB": _sb([32, 128], bf), "EQ": _sb([16, 128], bf),
-    "VO": _sb(256, u16), "V16": _sb(256, f16), "WL": _sb(272, u16), "YA": _sb(256, bf),
+    "VO": _sb(256, u16), "V16": _sb(256, f16), "WL": _sb(272, u16), "YA": _sb(1024, bf),
     "PI": _sb(8, i32), "CO": _sb(64, f32), "N256": _sb(256, f32), "QN": _sb(256, f32),
-    "NB": _sb(256, bf), "NBH": _sb(256, bf), "NH": _sb(256, f32),
-    "J2": _sb([8, 32], f32), "SEI": _sb(24, f32), "SEL": _sb(24, f32), "KO": _sb(48, bf),
+    "NB": _sb(256, bf), "DMN": _sb(256, f32), "NH": _sb(256, f32),
+    "J2": _sb([8, 32], f32), "SEI": _sb(24, f32), "SEL": _sb(24, f32), "HL": _sb(48, bf),
     "DM": _sb(256, f32), "RST": _sb(128, f32), "STA": _sb(256, bf),
     "UB": _sb(144, bf), "UH": _sb(144, bf), "TRI": _sb(128, bf), "UPR": _sb(128, bf),
     "TRC": _sb(128, bf), "MB": _sb(128, bf), "MU": _sb(384, bf),
-    "ID": _sb(512, bf), "IDf": _sb(256, f32), "S": _sb(2048, bf), "ROT": _sb([8, 32], bf),
-    "PD": _sb(1024, bf), "CK": _sb([8, 256], bf), "JT": _sb(512, bf), "ONE": _sb(256, bf), "ZERO": _sb(128, bf),
-    "B8": _sb(64, bf), "SM": _sb(16 * 24, f32), "SB": _sb(80, bf), "SI": _sb(64, i32), "SU": _sb(16 * 8, u16),
+    "ID": _sb(512, bf), "IDf": _sb(256, f32), "S": _sb(2048, bf), "ROT": _sb([8, 32], bf), "RON": _sb([8, 32], bf),
+    "PD": _sb(1024, bf), "CK": _sb(1024, bf), "JT": _sb(512, bf), "ONE": _sb(256, bf), "ZERO": _sb(128, bf),
+    "B8": _sb(64, bf), "SM": _sb(16 * 24, f32), "SB": _sb(96, bf), "SI": _sb(64, i32), "SU": _sb(16 * 8, u16),
     "MP": _sb(256, i32), "T1": _sb([16, 32], f32), "T2": _sb([16, 32], f32), "T3": _sb(256, f32), "WS": _sb(256, u16),
     "IF": _sb(128, bf), "ZC": _sb(256, f32), "ZN": _sb(256, f32), "W0": _sb(272, u16),
-    "Y0": _sb(256, bf), "WR": _sb(256, u16),
+    "Y0": _sb(1024, bf), "UQ": _sb(48, u16), "UO": _sb(48, u16), "WR": _sb(256, u16),
     "KC": _sb(1024, i32), "KF": _sb(768, f32),
     "OH": _sb(2048, bf), "OQ": _sb(256, bf), "FT": _sb(128, bf), "QB": _sb(144, bf), "Z": _sb([16, 128], bf),
     "P": _sb(136, f32), "CMP": _sb(256, bf), "JK": _sb(4096, bf),
@@ -45,18 +45,17 @@ SCRATCH = {
     "E1": _sb(256, f32), "E2": _sb(256, bf), "E5": _sb(256, bf), "EU": _sb(256, bf),
     "G1": _sb(256, f32), "R": _sb(256, bf), "LE": _sb(256, bf), "LO": _sb(256, bf),
     "NEW": _sb(256, f32), "FW": _sb(512, f32), "XT": _sb(256, bf),
-    "VAL": _sb(96, f32), "DW3": _sb(48, f32), "LF": _sb(48, f32), "LS": _sb(192, u16),
-    "NX": _sb(768, bf), "XU": _sb(768, bf), "LU": _sb(48, u16),
-    "FC": _sb(256, f32), "FR": _sb(512, f32), "MO": _sb(512, f32), "GV": _sb(512, f32), "GO": _sb(256, f32),
-    "ML": _sb(32, u16), "NR": _sb(768, bf), "VR": _sb(48, u16), "IDR": _sb(128, bf),
+    "VAL": _sb(96, f32), "DW3": _sb(48, f32), "LF": _sb(48, f32), "LS": _sb(192, u16), "NX": _sb(768, bf),
+    "FC": _sb(256, f32), "FR": _sb(512, f32), "MO": _sb(256, f32), "GV": _sb(512, f32), "GO": _sb(256, f32),
+    "ML": _sb(32, u16),
     "dZ": ("dram", [128, 256], f32), "dM": ("dram", [128, 256], f32), "dB": ("dram", [4, 128, 1024], i32),
 }
 for _k in range(8):
     SCRATCH["ps%d" % _k] = ("psum", [128, 512], f32)
 SIZE = {f32: 4, i32: 4, bf: 2, f16: 2, u16: 2}
 
-MSG = ["W", "w", "y", "Z", "X0", "X1", "B0", "B1", "B2", "B3", "N0", "N1", "N2", "L0", "L1", "L2", "M", "G", "E"]
-SEMAPHORES = (["qv", "qa", "qt", "qg", "sent", "sx", "go", "h0", "h1", "h2"] + ["a" + m for m in MSG]
+MSG = ["W", "w", "Y0", "Y1", "Y2", "Y3", "Z", "B0", "B1", "B2", "B3", "U1", "U2", "U3", "M", "G", "E"]
+SEMAPHORES = (["qv", "qa", "qt", "qg", "sent", "h1", "h2"] + ["a" + m for m in MSG]
               + ["d%d" % k for k in range(30)])
 
 
@@ -76,7 +75,7 @@ def helper_of(T, topo, r):
 
 
 def landing(T, rot):
-    d = {"X0": T["XG"][:, 0:2048], "X1": T["XG"][:, 2048:4096]}
+    d = {}
     for k in range(4):
         lo = 1024 * k + (8 if k >= 2 else 0)
         d["B%d" % k] = T["dB"][k] if rot else T["BG"][:, lo:lo + 1024]
@@ -91,7 +90,7 @@ def helper_program(g, core, T, topo, r):
     rid, pid, _ = topo.addr(nxt)
     m = topo.mask(core, nxt)
     tot = 0
-    for s, src, name in (("h1", T["BG"][:, 0:1024], "B3"), ("h0", T["XG"][:, 0:2048], "X1"), ("h2", T["BG"][:, 1024:2048], "B1")):
+    for s, src, name in (("h1", T["BG"][:, 0:1024], "B3"), ("h2", T["BG"][:, 1024:2048], "B1")):
         g.wait_ge(T.sem[s], cnt)
         g.remote_dma(land[name], src, T.sem["a" + name], T.sem["sent"], pid, rid, m)
         tot += len(topo.engines(core, nxt))
@@ -190,10 +189,6 @@ def rank_program(g, core, T, topo):
         w = T[name].shape[2]
         return (T[name][:, a0:a1, b0:b1], [(name, a0 * w, a1 * w)], (a1 - a0) * (b1 - b0), name, "")
 
-    def row(name, k, b0, b1):
-        w = T[name].shape[2]
-        return (T[name][:, k, b0:b1], [(name, k * w + b0, k * w + b1)], b1 - b0, name, "")
-
     def ind(win, off):
         return (win[0].indirect(off[0]), win[1] + off[1], 16 * off[2], win[3], "i")
 
@@ -246,7 +241,7 @@ def rank_program(g, core, T, topo):
             if q in last:
                 pre.setdefault(last[q], 0)
             last[q] = me
-        if chain[0] is not None and q in "va":
+        if chain[0] is not None and q in chain[0].get("on", "va"):
             if q in chain[0]:
                 pre.setdefault(chain[0][q], 0)
             chain[0][q] = me
@@ -322,7 +317,7 @@ def rank_program(g, core, T, topo):
     def diagonal(o, i, fill):
         select(o, i, [[-1, 128]], A.not_equal, fill, 0, 1)
 
-    def dma(pairs, lat=2200.0, add=False, extra=None):
+    def dma(pairs, lat=2200.0, add=False):
         s = "d%d" % nd[0]
         nd[0] += 1
         if add:
@@ -330,28 +325,28 @@ def rank_program(g, core, T, topo):
         else:
             em = [(lambda a=a, b=b: g.sync.dma_start(ap(a), ap(b))) for a, b in pairs]
         node("g" if add else "s", [a for a, _ in pairs], [b for _, b in pairs], em, 100.0 * len(pairs), lat, 16,
-             (s, 16 * len(pairs)), extra)
+             (s, 16 * len(pairs)))
 
     eng_n, eng_p = topo.engines(core, nxt), topo.engines(core, prv)
     eng_h = [e for e in topo.engines(core, hlp) if e not in eng_n]
-    sent = {"sent": 0, "sx": 0}
+    sent = [0]
 
-    def send(items, local="sent", c=1200.0):
+    def send(items, c=1200.0):
         def em():
             if len(items) == 1:
                 d, en, o, s, name = items[0]
                 rid, pid, _ = topo.addr(d)
-                return g.remote_dma(o, s[0], T.sem[name], T.sem[local], pid, rid, _mask(en))
+                return g.remote_dma(o, s[0], T.sem[name], T.sem["sent"], pid, rid, _mask(en))
             tr = []
             for d, en, o, s, name in items:
                 rid, pid, _ = topo.addr(d)
                 tr.append(RemoteDMATransfer(dst_ids=[DstId(rid=rid, pnc=pid)], dma_engine_mask=_mask(en),
                                             remote_sem=T.sem[name], src=s[0], dst=o))
-            return g.remote_dma_fused(tr, local_sem=T.sem[local])
+            return g.remote_dma_fused(tr, local_sem=T.sem["sent"])
         k = node("g", [], [it[3] for it in items], [em], c, 0.0, 0, keep=False)
         for it in items:
             sends[it[4]] = k
-        sent[local] += sum(len(it[1]) for it in items)
+        sent[0] += sum(len(it[1]) for it in items)
 
     n_in = len(topo.engines(prv, core))
     n_bk = len(topo.engines(nxt, core))
@@ -367,32 +362,22 @@ def rank_program(g, core, T, topo):
         arrive(name, [dr(d, "d" + name)], count, like, lat)
         dma([(r(b, lo, hi, p=(16, 128)), dr(d[0:112, :], "d" + name)), (r(b, lo, hi, p=(0, 16)), dr(d[112:128, :], "d" + name))])
 
-    def load_g(b, lo, hi, src, rows, c0, c1, lat, extra=None):
-        if rot_out:
-            k = 7 * rows
-            dma([(r(b, lo, hi, p=(16, 128)), src[0:k, c0:c1]), (r(b, lo, hi, p=(0, 16)), src[k:k + rows, c0:c1])], lat, extra=extra)
-        else:
-            dma([(r(b, lo, hi), src[:, c0:c1])], lat, extra=extra)
-
-    (cP, cQ, cG, cE1, cE0, cU, cLT, cBit, cBp, cVo, cHi, cH1, cL1, cL2, cO1, cO2, cMB, cPW, cW14, cW15, cWV,
-     cUH, cNB, cZN, cST, cLo, cOff, cA, cB, cC) = range(30)
+    (cP, cQ, cG, cE1, cE0, cU, cLT, cBit, cBp, cVo, cHi, cH1, cL1, cL2, cO1, cO2, cMB, cPW, cW14,
+     cUH, cNB, cZN, cST, cLo, cOff, cA, cB, cC) = range(28)
     SK = 32
-    (sOW0, sOW1, sOW2, sOW3, sNOW, sSC, sT2, sLO, sRES, sACC, sB8, sZ, sA1, sA2, sA3, sA4, sPW, sU0, sF8) = range(19)
-    bCC, bHX, bN8, bOFF = range(4)
-    uLB, uLT, uM, uV, uG2 = range(5)
+    sOW0, sOW1, sOW2, sNOW, sRES, sACC, sB8, sZ, sA1, sA2, sA3, sA4, sPW, sU0, sF8 = range(15)
+    bCC, bT2, bN8, bMF, bOFF = range(5)
+    uLB, uLT, uM, uV, uG2, uL3 = range(6)
     uU = r("WL", 256, 272)
     ID, NID, ID75, ID25, IDf = r("ID", 0, 128), r("ID", 128, 256), r("ID", 256, 384), r("ID", 384, 512), r("IDf", 0, 128)
+    FWD, BACK = r("IDf", 112, 240), r("IDf", 16, 144)
     B8, B8s, B8n = r("B8", 0, 8), r("B8", 16, 24), r("B8", 32, 40)
     one1 = r("ONE", 0, 128, p=(0, 1))
-    found = r("ps5", 272, 288)
-    xs = "XS" if rot_out else "XH"
+    found = r("ps6", 272, 288)
     land = landing(T, rot_out)
 
     def fill(o, c):
         act(o, r("N256", 0, o[2]), bias=c, scale=0.0)
-
-    def gate(k):
-        return {node("g", [], [], [lambda: g.sem_inc(T.sem["go"], 1)], 30.0, 0.0, 0, ("go", k)): 1}
 
     def between(o, lo_, hi_):
         select(o, r("ONE", 0, o[2]), lo_[0], A.is_ge, 0.0, lo_[1], lo_[2])
@@ -400,11 +385,14 @@ def rank_program(g, core, T, topo):
 
     def counts():
         mm(r("ps5", 256, 264), r("QB", 1, 129), B8)
-        mm(r("ps5", 384, 512), r("TRI"), r("QB", 1, 129), True, False)
-        mm(r("ps5", 384, 512), r("UPR"), r("QB", 0, 128), False, True)
+        go()
+        mm(r("ps1", 128, 256), r("TRI"), r("QB", 1, 129), True, False)
+        mm(r("ps1", 128, 256), r("UPR"), r("QB", 0, 128), False, True)
         go()
         cp(sb(bCC, 0, 8), r("ps5", 256, 264))
-        cp(r("P", 0, 128), r("ps5", 384, 512))
+
+    def prefix():
+        cp(r("P", 0, 128), r("ps1", 128, 256))
 
     def level1(z_=1):
         for k in range(8):
@@ -413,21 +401,25 @@ def rank_program(g, core, T, topo):
                 ts(z, r("NB"), sb(bCC, k, k + 1), A.is_lt, 2.0, A.mult)
             else:
                 act(z, r("NH"), AF.Sign, bias=sb(bCC, k, k + 1), scale=-1.0)
-        column(z_, True)
-
-    def column(z_, stop):
-        mm(found, ID, sb(bOFF + z_), True, False)
+        mm(r("ps5", 272, 288), ID, sb(bOFF + z_), True, False)
         for b in range(16):
-            mm(r("ps5", 272 + b, 273 + b), (T["Z"][:, b, :], [("Z", 0, 8)], 128, "Z", ""), sb(bN8, 0, 1), False, stop and b == 15)
+            mm(r("ps5", 272 + b, 273 + b), (T["Z"][:, b, :], [("Z", 0, 8)], 128, "Z", ""), sb(bN8, 0, 1), False, b == 15)
         go()
 
-    def level2(z_=1):
-        ts(su(uM), found, 1.0 / 16, A.mult, 128.0, A.add)
-        column(z_, False)
+    def level2(copy=act):
+        ts(su(uM), r("ps5", 272, 288), 1.0 / 16, A.mult, 128.0, A.add)
+        copy(sb(bMF), r("ps5", 272, 288))
+        mm(found, ID, sb(bMF), True, False)
         tt(r("CMP"), ind(r("P", 0, 136), su(uM)), r("N256"), A.is_le)
         for q in range(16):
             mm(found, r("UB", 15 - q, 143 - q), r("CMP", q, 256, 16), False, q == 15)
         go()
+
+    def features(t, win, lst):
+        y = r("Y0", 256 * t, 256 * t + 256)
+        act(y, ind(win, lst), AF.Copy)
+        send([(nxt, eng_n, T["YA"][:, 256 * t:256 * t + 256], y, "aY%d" % t)])
+        arrive("Y%d" % t, [r("YA", 256 * t, 256 * t + 256)], n_in)
 
     def as_float(k):
         ts(r("BF", 1024 * k, 1024 * k + 1024), r("B", 1024 * k, 1024 * k + 1024), -2048.0, A.add)
@@ -439,14 +431,19 @@ def rank_program(g, core, T, topo):
                 act(r("BKI", (1 << k) + a, (1 << k) + b), r("BKI", a, b), scale=co(SK + k))
 
     chain[0] = {}
-    load_g("MP", 0, 256, T["mp"], 1, 0, V, 2000.0)
+    if rot_out:
+        dma([(r("MP", p=(16, 128)), T["mp"][0:7, :]), (r("MP", p=(0, 16)), T["mp"][7:8, :])], 2000.0)
+    else:
+        dma([(r("MP"), T["mp"][:, :])], 2000.0)
     for k in range(4):
         dma([(r("B", 1024 * k, 1024 * k + 1024), T["nb"][:, 1024 * k:1024 * k + 1024])], 3500.0 + 1900.0 * k)
+    dma([(r("XH", 0, V), T["x"][:, :])], 13500.0)
     dma([(r("KC", 0, 256), T["ky"][:, :]), (r("KC", 256, 512), T["iv"][:, :])], 10000.0)
     iota(r("PI", 0, 1), [[0, 1]], 0, 1, False)
     iota(r("N256"), [[1, 256]])
     iota(r("QN"), [[0, 16], [1, 16]])
     ms(r("ONE"), 1.0)
+    ms(r("ZERO"), 0.0)
     between(r("TRI"), ([[-16, 8], [0, 16]], 0, 1), ([[16, 8], [1, 16]], 0, -1))
     between(r("UPR"), ([[-16, 8], [-1, 16]], -1, 1), ([[16, 8], [0, 16]], 15, -1))
     select(r3("ROT", 0, 8, 0, 32), r("ONE"), [[-16, 8], [0, 2], [-1, 16]], A.is_equal, 0.0, 0, 1)
@@ -484,15 +481,15 @@ def rank_program(g, core, T, topo):
     cp(r("WS"), ind(r("T3"), su(uLT)))
     send([(nxt, eng_n, T["WR"][:, :], r("WS"), "aW")], c=3000.0)
     arrive("W", [r("WR")], n_in, lat=3000.0)
-    load_g(xs, 0, 2064 if rot_out else V, T["x"], 16, 0, 2064 if rot_out else V, 6000.0, gate(1))
     act(co(cVo), co(cBp), bias=-2048.0)
     fill(r("BF", V, V + 8), co(cVo))
     act(r("CO", SK, SK + 12), r("DM", 0, 12), bias=1.0, scale=-2.0)
     act(r("BKI", 0, 1), co(cBit))
-    codes(0, 10)
-    if rot_out:
+    for i in range(9):
+        codes(i, i + 1)
+        act(r("S", 128 * i, 128 * i + 128), IDf, scale=r("DM", i, i + 1))
+    if rot_out or rot_in:
         act(r("IDf", 128, 256), IDf)
-        act(r("IDR"), r("IDf", 112, 240))
 
     ts(r("IF"), r("WS", 0, 128), 4095.5, A.is_gt)
     scan(r("QB", 1, 129), r("ONE", 0, 128), r("IF"), 0.0, A.mult, A.add)
@@ -500,12 +497,26 @@ def rank_program(g, core, T, topo):
         diagonal(r("PD", 128 * (k - 1), 128 * k), r3("ROT", 0, 8, k, k + 16), -1.0)
     counts()
     level1(0)
+    prefix()
     as_float(0)
-    codes(10, 12)
-    act(r("BKI", V, V + 16), r("N256", 0, 16))
-    for i in range(16):
+    codes(9, 11)
+    for i in range(9, 16):
         act(r("S", 128 * i, 128 * i + 128), IDf, scale=r("DM", i, i + 1))
-    level2(0)
+    act(NID, FWD if rot_in else IDf, scale=-1.0)
+    if rot_in:
+        act(ID25, FWD, scale=0.25)
+    act(r3("RON", 0, 8, 0, 32), r3("ROT", 0, 8, 0, 32), scale=-1048576.0)
+    act(B8s, B8, scale=65536.0)
+    act(B8n, B8, scale=-8192.0)
+    act(sm(sB8, 0, 8), B8)
+    act(co(cA), r("DM", 0, 1), scale=1.0 / 8192)
+    act(sm(sF8, 0, 8), B8, scale=co(cA))
+    act(co(cHi), r("DM", 14, 15), bias=r("DM", 15, 16))
+    act(co(cUH), r("DM", 14, 15), bias=r("DM", 15, 16), scale=16.0)
+    act(co(cMB), co(cBit), scale=1.0 / 512)
+    act(co(cST), r("DM", 12, 13), scale=1.0 / 256)
+    act(co(cLo), co(cQ), bias=float(DUMP))
+    level2(cp)
     as_float(1)
     ts(r("W0", 256, 272), found, 2048.0, A.add)
     ts(sm(sA3), found, -0.5, A.is_gt, 2048.0, A.mult)
@@ -513,12 +524,12 @@ def rank_program(g, core, T, topo):
     ts(r("B", V, V + 8), r("N256", 0, 8), 0.0, A.mult, co(cBp), A.add)
     tt(sm(sA4), sm(sA3), sm(sU0), A.add)
     if rot_out:
-        mm(r("ps0", 0, 16), r("IDf", 16, 144), sm(sA4))
+        mm(r("ps0", 0, 16), BACK, sm(sA4))
         go()
         as_float(2)
         cp(su(uG2), r("ps0", 0, 16))
         cp(r("T3"), ind(r("B", 0, V + 8), su(uG2)))
-        mm(r("ps0", 0, 256), r("IDf", 112, 240), r("T3"))
+        mm(r("ps0", 0, 256), FWD, r("T3"))
         go()
         as_float(3)
         cp(r("W0", 0, 256), r("ps0", 0, 256))
@@ -529,21 +540,15 @@ def rank_program(g, core, T, topo):
         as_float(3)
     send([(nxt, eng_n, T["WL"][:, :], r("W0"), "aw")])
     arrive("w", [r("WL")], n_in)
-    if rot_out:
-        dma([(r("XH", 0, V), T["x"][:, :])], 5500.0, extra=gate(2))
-        load_g("XS", 2064, V, T["x"], 16, 2064, V, 7500.0)
-    for k in range(1, 8):
-        diagonal(row("CK", k - 1, 128, 256), r3("ROT", 0, 8, 16 - k, 32 - k), 1.0)
+    iota(r3("J2", 0, 8, 0, 32), [[0, 16], [4096, 16]])
+    iota(r("XH", V, DUMP), [[0, 32]])
 
     for a, b in OPT["FB_A"]:
         act(r("F", FN + a, FN + b), ind(r("BF", 0, V + 8), r("WR", a // 16, b // 16)), AF.Copy)
-        if a == 0:
-            act(r("Y0"), ind(r(xs, 0, 2064), r("W0", 256, 272)), AF.Copy)
     for a, b in OPT["FB_V"]:
         ts(r("F", FN + a, FN + b), ind(r("B", 0, V + 8), r("WR", a // 16, b // 16)), -2048.0, A.add)
     fill(r("F", FP, FD), co(cVo))
-    send([(nxt, eng_n, T["YA"][:, :], r("Y0"), "ay")])
-    arrive("y", [r("YA")], n_in)
+    features(0, r("XH", 0, DUMP), su(uG2))
     ts(r("ZC"), r("MP"), 1.0 / 8192, A.mult)
     send([(nxt, eng_n, T["dZ"][:, :], r("ZC"), "aZ")])
     arrive("Z", [dr(None, "dZ")], n_in, lat=8000.0)
@@ -554,79 +559,54 @@ def rank_program(g, core, T, topo):
     ts(r("KC", 768, 1024), r("KC", 256, 512), 4096 + 15, A.bitwise_and)
     cp(r("KF", 0, 256), r("KC", 0, 256))
     cp(r("KF", 256, 768), r("KC", 512, 1024))
-    dma([(r("BKI", 0, V, p=(13 + k, 128, 16)), r("KF", 256 * k, 256 * k + 256)) for k in range(3)], 4000.0)
     send([(nxt, eng_n, land["B2"], r("B", 2048, 3072), "aB2"), (hlp, eng_h, T["BG"][:, 0:1024], r("B", 3072, V), "h1")])
-    send([(nxt, eng_n, land["X0"], r(xs, 0, 2048), "aX0"), (hlp, eng_h, T["XG"][:, 0:2048], r(xs, 2048, V), "h0")], "sx")
     send([(hlp, eng_h, T["BG"][:, 1024:2048], r("B", 1024, 2048), "h2")])
-    arrive("X0", [r("XG", 0, 2048)], n_in, lat=12000.0)
-    arrive("X1", [r("XG", 2048, V)], n_h, "h0", 14000.0)
-    iota(r3("J2", 0, 8, 0, 32), [[0, 16], [4096, 16]])
-    iota(r("SEI"), [[16, 8], [1, 3]], 13)
 
-    act(NID, IDf, scale=-1.0)
-    fill(r("XH", V, DUMP), 0.0)
+    codes(11, 12)
+    act(r("BKI", V, V + 16), r("N256", 0, 16))
+    dma([(r("BKI", 0, V, p=(13 + k, 128, 16)), r("KF", 256 * k, 256 * k + 256)) for k in range(3)], 4000.0)
+    for k in range(1, 8):
+        diagonal(r("CK", 128 * k - 128, 128 * k), r3("RON", 0, 8, 16 - k, 32 - k), -1048576.0)
+    for o, c in ((r("CK", 896, 1024), -1048576.0), (ID75, 0.75)) + (() if rot_in else ((ID25, 0.25),)):
+        diagonal(o, r("ZERO"), c)
+    iota(r("SEI"), [[16, 8], [1, 3]], 13)
+    iota(r("E2"), [[0, 256]])
+    iota(sm(sOW0), [[-128, 2], [0, 8]], 6143 * 256, -1)
+    iota(r("BG", 2048, 2056), [[0, 8]], 4096, 0, False)
+    iota(r("BG", 4104, 4112), [[0, 8]], 4096, 0, False)
+    iota(r("GV", 0, 256), [[0, 256]], 4096)
+    keep = chain[0]
     chain[0] = None
-    act(row("CK", 7, 128, 256), IDf)
-    for k in range(8):
-        act(row("CK", k, 0, 128), row("CK", k, 128, 256), scale=-1048576.0)
-    act(B8s, B8, scale=65536.0)
-    for t in range(RO):
-        act(r("JT", 128 * t, 128 * t + 128), r3("J2", 0, 8, 16 - t, 32 - t))
-    fill(r("FW", 0, 256), co(cVo))
-    fill(r("ZERO"), 0.0)
-    act(B8n, B8, scale=-8192.0)
-    act(sm(sB8, 0, 8), B8)
-    act(sm(sF8, 0, 8), B8, scale=r("DM", 0, 1))
-    ts(r("RST"), r("QN", 0, 128), 0.0, A.is_equal, 4 * PEN, A.mult)
-    act(ID75, IDf, scale=0.75)
-    act(ID25, IDf, scale=0.25)
-    ts(r("TRC"), r("N256", 0, 128), co(cP), A.is_ge)
-    act(r("NBH"), r("N256"), bias=-127.5)
-    fill(r("GV", 0, 256), 4096.0)
-    fill(r("E2"), 0.0)
-    fill(r("KO"), 0.0)
-    fill(r("KO", 1, 48, 3), -127.5)
-    act(co(cST), r("DM", 12, 13), scale=1.0 / 256)
-    act(r("STA"), r("N256"), scale=co(cST))
-    cp(su(uLB), r("N256", 0, 16))
-    ts(r("SEL"), r("SEI"), co(cP), A.is_equal)
-    act(co(cLo), co(cQ), bias=float(DUMP))
-    act(r("DW3", 0, 32), r("N256", 0, 32), bias=co(cLo), scale=16.0)
-    act(r("DW3", 32, 48), r("N256", 0, 16), bias=co(cLo), scale=16.0)
-    act(co(cA), co(cP), bias=6144.0, scale=-1.0 / 256)
-    act(co(cB), co(cP), bias=6143.5, scale=-1.0 / 256)
-    fill(sm(sOW0, 0, 8), co(cA))
-    fill(sm(sOW0, 8, 16), co(cB))
-    act(sm(sOW1), sm(sOW0), bias=-1.0)
-    fill(sm(sOW2), -1.0)
-    act(co(cHi), r("DM", 14, 15), bias=r("DM", 15, 16))
     act(co(cH1), co(cHi), bias=-1.0)
     act(co(cL1), co(cBit), bias=co(cHi), scale=512.0)
+    act(r("UH"), r("UB"), scale=co(cUH))
     act(co(cL2), co(cBit), bias=co(cH1))
     act(co(cO1), co(cL1), scale=co(cE1))
-    act(co(cO2), co(cL2), scale=co(cE1))
-    act(co(cMB), co(cBit), scale=1.0 / 512)
     act(r("MB"), IDf, scale=co(cMB))
-    fill(sm(sA1), 2.0)
-    fill(sm(sZ), 0.0)
-    scan(sm(sPW), sm(sA1), sm(sZ), 0.5, A.mult, A.add)
-    tt(sm(sA2), sm(sPW), r("DM", 0, 16), A.mult)
-    red(co(cPW), sm(sA2, 0, 12), A.add)
-    red(co(cC), sm(sA2, 0, 4), A.add)
-    act(co(cW15), co(cC), scale=-0.5)
-    act(co(cA), co(cC), scale=1.0 / 32)
-    act(co(cW14), co(cPW), bias=co(cA), scale=-1.0 / 32)
-    act(co(cWV), co(cPW), scale=-1.0 / 1024)
-    act(r("MU", 0, 128), r("UB", 1, 129), scale=co(cW14))
-    act(r("MU", 128, 256), r("UB", 0, 128), scale=co(cW15))
-    act(r("MU", 256, 384), r("UB", 1, 129), scale=co(cWV))
-    act(co(cUH), r("DM", 14, 15), bias=r("DM", 15, 16), scale=16.0)
-    act(r("UH"), r("UB"), scale=co(cUH))
-    act(co(cB), r("DM", 15, 16), scale=7.5)
-    act(co(cNB), r("DM", 14, 15), bias=co(cB), scale=127.5)
-    ms(r("BG", 2048, 2056), 4096)
-    ms(r("BG", 4104, 4112), 4096)
-    fill(r("XG", V, V + 16), 0.0)
+    act(co(cO2), co(cL2), scale=co(cE1))
+    act(r("DW3", 0, 32), r("N256", 0, 32), bias=co(cLo), scale=16.0)
+    act(r("DW3", 32, 48), r("N256", 0, 16), bias=co(cLo), scale=16.0)
+    act(r("STA"), r("N256"), scale=co(cST))
+    act(r("DMN"), r("DM"), bias=-1.0, scale=1.001)
+
+    def constants():
+        ts(r("TRC"), r("N256", 0, 128), co(cP), A.is_ge)
+        cp(su(uLB), r("N256", 0, 16))
+        ts(su(uL3), r("N256", 0, 16), 3.0, A.mult, 2.0, A.add)
+        ts(r("SEL"), r("SEI"), co(cP), A.is_equal)
+        ts(sm(sOW1), sm(sOW0), 1.0 / 256, A.mult)
+        ms(sm(sA1), 2.0)
+        ms(sm(sZ), 0.0)
+        scan(sm(sPW), sm(sA1), sm(sZ), 0.5, A.mult, A.add)
+        tt(sm(sA2), sm(sPW), r("DM", 0, 16), A.mult)
+        ts(co(cB), r("DM", 15, 16), 7.5, A.mult)
+        red(co(cPW), sm(sA2, 0, 12), A.add)
+        red(co(cC), sm(sA2, 0, 4), A.add)
+        ts(co(cNB), r("DM", 14, 15), 127.5, A.mult, co(cB), A.add)
+        ts(co(cW14), co(cC), co(cPW), A.subtract, 1.0 / 32, A.mult)
+        ts(r("MU", 128, 256), r("UB", 0, 128), co(cC), A.mult, -0.5, A.mult)
+        ts(r("MU", 256, 384), r("UB", 1, 129), co(cPW), A.mult, -1.0 / 1024, A.mult)
+        ts(r("MU", 0, 128), r("UB", 1, 129), co(cW14), A.mult)
 
     def expand(o, src, mask, f=A.mult):
         tt(o, ind(src, su(uLB)), mask, f)
@@ -636,26 +616,30 @@ def rank_program(g, core, T, topo):
         s0 = 2048 - lo
         end = t == RO - 1
         val = 48 * (t % 2)
+        early = []
 
         def fg(c):
             ts(r("FO", 1024 * c, 1024 * c + 1024), ind(r("F", FN, FD), r("WL", 64 * c, 64 * c + 64)), CR, A.add, CR, A.subtract)
+
+        def pick(c):
             for i in range(16):
                 j = (i - t) % 16
-                mm(r("ps0", 0, 64), r("S", 128 * i, 128 * i + 128), r("FO", 1024 * c + j, 1024 * c + 1024, 16), i == 0, i == 15)
+                mm(r("ps0", 64 * c, 64 * c + 64), r("S", 128 * i, 128 * i + 128), r("FO", 1024 * c + j, 1024 * c + 1024, 16), i == 0, i == 15)
             go()
 
         def ev(c):
-            ts(r("VO", 64 * c, 64 * c + 64), r("ps0", 0, 64), 2048.0, A.add)
-            cp(r("V16", 64 * c, 64 * c + 64), r("ps0", 0, 64))
+            ts(r("VO", 64 * c, 64 * c + 64), r("ps0", 64 * c, 64 * c + 64), 2048.0, A.add)
+            cp(r("V16", 64 * c, 64 * c + 64), r("ps0", 64 * c, 64 * c + 64))
 
         def turned(c):
             for k in range(8):
-                mm(r("ps1", 64 * k, 64 * k + 64), r("PD", 128 * k, 128 * k + 128), r("V16", 64 * c, 64 * c + 64))
+                mm(r("ps7" if c % 2 else "ps1", 64 * k, 64 * k + 64), r("PD", 128 * k, 128 * k + 128), r("V16", 64 * c, 64 * c + 64))
             go()
 
         def eq(c):
             hh, o = c // 2, 64 * (c % 2)
-            ts((T["EQ"][:, 8 * hh:8 * hh + 8, o:o + 64], [("EQ", 4 * c, 4 * c + 1)], 512, "EQ", ""), r("ps1"), 0.0, A.is_equal)
+            ts((T["EQ"][:, 8 * hh:8 * hh + 8, o:o + 64], [("EQ", 4 * c, 4 * c + 1)], 512, "EQ", ""),
+               r("ps7" if c % 2 else "ps1"), 0.0, A.is_equal)
 
         def xg(c):
             xo, xi = r("XO", 1024 * c, 1024 * c + 1024), ind(r("XH", 0, DUMP), r("VO", 64 * c, 64 * c + 64))
@@ -664,13 +648,24 @@ def rank_program(g, core, T, topo):
             else:
                 act(xo, xi, AF.Copy)
 
-        def ab(c, u):
-            hh, o = c // 2, 64 * (c % 2)
+        def mine(c, u):
+            early.append((c, u))
             bank = "ps%d" % (2 + (2 * c + u) % 3)
             for k in range(8):
-                mm(r(bank, 64 * k, 64 * k + 64), ID, r("XO", 1024 * c + 8 * u + k, 1024 * c + 1024, 16), True, False)
-                mm(r(bank, 64 * k, 64 * k + 64), NID, r("YA", 64 * c, 64 * c + 64), False, True)
+                mm(r(bank, 64 * k, 64 * k + 64), NID, r("YA", 256 * t + 64 * c, 256 * t + 64 * c + 64), k == 0, False)
             go()
+
+        def ab(c, u):
+            bank = "ps%d" % (2 + (2 * c + u) % 3)
+            if (c, u) not in early:
+                mine(c, u)
+            for k in range(8):
+                mm(r(bank, 64 * k, 64 * k + 64), ID, r("XO", 1024 * c + 8 * u + k, 1024 * c + 1024, 16), False, k == 7)
+            go()
+
+        def size(c, u):
+            hh, o = c // 2, 64 * (c % 2)
+            bank = "ps%d" % (2 + (2 * c + u) % 3)
             k = 16 * hh + 8 * u
             act((T["AB"][:, k:k + 8, o:o + 64], [("AB", 8 * hh + 4 * u + c % 2, 8 * hh + 4 * u + c % 2 + 1)], 512, "AB", ""),
                 r(bank), AF.Abs)
@@ -679,7 +674,7 @@ def rank_program(g, core, T, topo):
             bank, a, b = "ps%d" % (6 + hh), 128 * hh, 128 * hh + 128
             eqs = [(T["EQ"][:, 8 * hh + k, :], [("EQ", 8 * hh, 8 * hh + 8)], 128, "EQ", "") for k in range(8)]
             for k in range(8):
-                mm(r(bank, 0, 128), eqs[k], row("CK", k, 0, 128), k == 0, k == 7)
+                mm(r(bank, 0, 128), eqs[k], r("CK", 128 * k, 128 * k + 128), k == 0, k == 7)
             go()
             if hh in OPT["PEN_V"]:
                 ts(r("PEN", a, b), r(bank, 0, 128), -0.5, A.is_gt, PEN, A.mult)
@@ -687,25 +682,28 @@ def rank_program(g, core, T, topo):
             else:
                 act(r("PEN", a, b), r(bank, 0, 128), AF.Relu, bias=PEN, scale=128.0)
                 act(r("SUP", a, b), r(bank, 0, 128))
+
+        def rest(hh):
+            bank, a, b = "ps%d" % (6 + hh), 128 * hh, 128 * hh + 128
             mm(r(bank, 0, 128), r("V16", a, b), ID, True, False)
             mm(r(bank, 0, 128), one1, r("JT", 128 * t, 128 * t + 128, p=(0, 1)), False, False)
             mm(r(bank, 0, 128), ID, r("SUP", a, b), False, False)
             mm(r(bank, 0, 128), ID, r("PEN", a, b), False, False)
             go()
 
-        def best(hh):
+        def best(hh, u):
             bank, a, b = "ps%d" % (6 + hh), 128 * hh, 128 * hh + 128
-            for u in range(2):
-                for i in range(8 * u, 8 * u + 8):
-                    mm(r(bank, i, 128, 16), (T["AB"][:, 16 * hh + i, :], [("AB", 8 * hh + 4 * u, 8 * hh + 4 * u + 2)], 128, "AB", ""),
-                       B8s, False, i == 15)
-                go()
-            scan(r("KS", a, b), r("RST"), r(bank, 0, 128), 0.0, A.add, A.min)
+            for i in range(8 * u, 8 * u + 8):
+                mm(r(bank, i, 128, 16), (T["AB"][:, 16 * hh + i, :], [("AB", 8 * hh + 4 * u, 8 * hh + 4 * u + 2)], 128, "AB", ""),
+                   B8s, False, i == 15)
+            go()
+            if u:
+                scan(r("KS", a, b), r("RST"), r(bank, 0, 128), 0.0, A.max, A.min)
 
-        def features(_):
+        def asked(_):
             if t > 0:
-                cp(ind(r("XG"), r("LU", 16 * t - 16, 16 * t)), r("XU", 256 * t - 256, 256 * t))
-                act(r("YA"), ind(r("XG", lo, lo + 2064), uU), AF.Copy)
+                arrive("U%d" % t, [r("UQ", 16 * t - 16, 16 * t)], n_bk)
+                features(t, r("XH", lo, lo + 2064), r("UQ", 16 * t - 16, 16 * t))
 
         def keys(_):
             if t > 0:
@@ -720,13 +718,15 @@ def rank_program(g, core, T, topo):
                 go()
 
         if t == 0:
-            ts(r("VAL", 16, 32), uU, 0.0, A.add)
-            act(r("EU"), ind(r("BKI", 0, 2064), uU), AF.Copy)
-        chain[0] = {}
-        step = dict(g=features, k=keys, p=before, f=fg, e=ev, d=turned, q=eq, x=xg, s=support, b=best,
-                    a=lambda c: ab(c, 0), c=lambda c: ab(c, 1))
+            act(r("JT", 0, 128), r3("J2", 0, 8, 16, 32))
+            ts(r("RST"), r("QN", 0, 128), -2 * CAP, A.mult, CAP - 2048.0, A.add)
+        chain[0] = dict(keep, on="vat")
+        step = dict(K=lambda _: t or constants(), g=asked, k=keys, p=before, f=fg, i=pick, e=ev, d=turned, q=eq, x=xg,
+                    s=support, r=rest, y=lambda u: mine(u // 2, u % 2), a=lambda c: ab(c, 0), c=lambda c: ab(c, 1),
+                    A=lambda c: size(c, 0), C=lambda c: size(c, 1), b=lambda h: best(h, 0), B=lambda h: best(h, 1))
         for w in OPT["ORDER"].split():
             step[w[0]](int(w[1]))
+        keep = chain[0]
         chain[0] = None
         if t == 0:
             dma([(r("F", FN, FP, p=(14, 128, 16)), dr(T["dZ"][:, :], "dZ"))], 2800.0, True)
@@ -734,37 +734,46 @@ def rank_program(g, core, T, topo):
                 arrive_turned("B%d" % k, "BG", 1024 * k + 8, 1024 * k + 1032, T["dB"][k], n_h if k % 2 else n_in,
                               "h1" if k % 2 else None, 12000.0)
         if end:
-            arrive("M", [dr(None, "dM")], n_bk, lat=8000.0)
-            dma([(r("F", FN, FP, p=(14, 128, 16)), dr(T["dM"][:, :], "dM"))])
+            chain[0] = keep
+            act(r("FR", 0, 256), r("FC"), bias=CR)
+            act(r("FR", 256, 512), r("FR", 0, 256), AF.Relu, bias=CR + 2047.0, scale=-1.0)
+            chain[0] = None
 
         sY, sV, sC = r("SI", 0, 16), r("SI", 16, 32), r("SI", 32, 48)
+        score = r("E2", 13, 256, 16)
         red_v = OPT["RED_V"][end]
         nv = 2 * red_v
         vs = r("LS", 48 * t + 32, 48 * t + 48)
         nx = r("NX", 256 * (t % 3), 256 * (t % 3) + 256)
+        uo = r("UO", 16 * (t % 3), 16 * (t % 3) + 16)
+        mine_u = uU if rot_in else uo
         banks = ["ps2", "ps3", "ps4", "ps7"]
 
         def choice():
-            ts(sY, r("KS", 15, 256, 16), 2048.0, A.add, CAP, A.min)
+            if t == 0:
+                act(r("FW", 0, 256), r("N256"), AF.Silu, bias=co(cVo), scale=0.0)
+                ts(r("VAL", 16, 32), uU, 0.0, A.add)
+                act(r("EU"), ind(r("BKI", 0, 2064), uU), AF.Copy)
+            ts(sY, r("KS", 15, 256, 16), 2048.0, A.add)
             ts(sV, sY, 4095, A.bitwise_and)
             expand(r("E1"), sV, r("DM"))
             for hh in range(2):
                 mm(r("ps0", 8 * hh, 8 * hh + 8), r("E1", 128 * hh, 128 * hh + 128), sm(sB8, 0, 8))
             go()
             ts(sC, sY, 16, A.arith_shift_right)
-            ts(r("E2", 13, 256, 16), sC, -16.0, A.add)
+            ts(score, sC, -16.0, A.add)
             cp(su(uV), r("ps0", 0, 16))
             act(r("G1"), ind(r("BKI", 0, V), su(uV)), AF.Copy)
-            ts(sm(sSC), sC, -16.0, A.add)
-            cp(r("VAL", val + 32, val + 48), r("ps0", 0, 16))
-            if nv < 16:
-                tt(sm(sNOW, nv, 16), sm(sSC, nv, 16), sm(sOW0, nv, 16), A.subtract)
-            if nv:
-                tt(sm(sOW2, 0, nv), sm(sOW1, 0, nv), sm(sSC, 0, nv), A.subtract)
+            tt(sm(sOW2), score, sm(sOW1), A.subtract)
             act(r("LE"), r("G1"), bias=co(cL2), scale=co(cL1))
-            mm(r("ps6", 0, 48), one1, r("KO", p=(0, 1)), True, False)
+            act(r("LO"), r("G1"), bias=co(cO2), scale=co(cO1))
+            if not end:
+                ts(r("XT"), ind(r("XH", 0, V), su(uV)), -0.5, A.add)
+            else:
+                tt(r("FR", 0, 256), r("FC"), r("FR", 256, 512), A.add)
+                ts(r("FC"), r("FR", 0, 256), -2047.0, A.add, 0.5, A.min)
             for hh in range(2):
-                mm(r("ps6", 24 * hh, 24 * hh + 24), r("G1", 128 * hh, 128 * hh + 128), r("SEL"), False, hh == 1)
+                mm(r("ps6", 24 * hh, 24 * hh + 24), r("G1", 128 * hh, 128 * hh + 128), r("SEL"))
             go()
             mm(r("ps1", 0, 256), ID, r("STA"), True, False)
             for hh in range(2):
@@ -773,32 +782,41 @@ def rank_program(g, core, T, topo):
             mm(r("ps1", 0, 256), r("MB"), r("LE"), False, True)
             go()
             act(r("R"), r("ps1", 0, 256))
-            act(r("LO"), r("G1"), bias=co(cO2), scale=co(cO1))
-            tt(sm(sT2), sm(sSC), r("ps6", 0, 48, 3), A.is_lt)
+            act(r("VAL", val + 32, val + 48), r("ps0", 0, 16))
+            if end:
+                act(r("MO"), r("FC"), scale=8192.0)
+                send([(prv, eng_p, T["dM"][:, :], r("MO"), "aM")])
+                arrive("M", [dr(None, "dM")], n_bk, lat=3000.0)
+                dma([(r("F", FN, FP, p=(14, 128, 16)), dr(T["dM"][:, :], "dM"))])
+            tt(sb(bT2), score, r("ps6", 0, 48, 3), A.is_lt)
+            if not end:
+                cp(r("HL"), r("ps6", 0, 48))
+            tt(sm(sNOW), sm(sOW2), sb(bT2), A.subtract)
 
-        def marks():
-            tt(sb(bHX), sm(sT2), r("ps6", 1, 48, 3), A.mult)
-            cp(sm(sLO), r("ps6", 2, 48, 3))
-            for k in range(16):
-                ts(r("OH", 128 * k, 128 * k + 128), r("NBH", s0 // 16, s0 // 16 + 128), sb(bHX, k, k + 1), A.is_equal, 8192.0, A.mult)
+        def marks(part):
+            for k in range(4 * part, 4 * part + 4):
+                ts(r("OH", 128 * k, 128 * k + 128), r("NB", s0 // 16, s0 // 16 + 128), r("HL", 3 * k + 1, 3 * k + 2), A.is_equal,
+                   sb(bT2, k, k + 1), A.mult)
                 if k == 0:
-                    expand(r("OQ"), sm(sLO), r("QN"), A.is_equal)
-                if k % 4 == 3:
-                    for m in range(k - 3, k + 1):
-                        mm(r("ps5", 16 * (m % 8), 16 * (m % 8) + 16), r("OH", 128 * m, 128 * m + 128), r("OQ", 16 * m, 16 * m + 16), False, m == 15)
-                    go()
+                    tt(r("OQ"), ind(r("HL"), su(uL3)), r("QN"), A.is_equal)
+            for m in range(4 * part, 4 * part + 4):
+                mm(r("ps5", 16 * (m % 8), 16 * (m % 8) + 16), r("OH", 128 * m, 128 * m + 128), r("OQ", 16 * m, 16 * m + 16), False, m == 15)
+            go()
 
         def holders():
-            tt(sm(sOW3), sm(sOW2), sm(sT2), A.add)
             for q in range(16):
-                mm(r("ps6", 64, 80), r("UH", 15 - q, 143 - q), r("LE", q, 256, 16), q == 0, q == 15)
+                mm(r("ps0", 128, 144), r("UH", 15 - q, 143 - q), r("LE", q, 256, 16), q == 0, q == 15)
             go()
-            tt(r("VAL", val, val + 16), r("ps6", 64, 80), r("DW3", 0, 16), A.min)
+
+        def held():
+            tt(r("VAL", val, val + 16), r("ps0", 128, 144), r("DW3", 0, 16), A.min)
 
         def flags():
-            ts(r("FT"), r("ps5", 0, 128), 2047.5, A.is_gt)
+            ts(r("FT"), r("ps5", 0, 128), 2047.5 / 8192, A.is_gt)
             mm(r("ps5", 128, 256), r("FT"), r("TRC"))
             go()
+
+        def places():
             cp(r("QB", 1, 129), r("ps5", 128, 256))
 
         def pairs(k):
@@ -812,7 +830,7 @@ def rank_program(g, core, T, topo):
                 col = 2 * k + e
                 src, res = r(bank, 256 * e, 256 * e + 256), sm(sRES, col, col + 1)
                 if k < red_v:
-                    red(res, src, A.max)
+                    red(sm(sACC, col, col + 1), src, A.max)
                 else:
                     act(r("JK", 256 * col, 256 * col + 256), src, AF.Relu, bias=sm(sNOW, col, col + 1), acc=res)
 
@@ -833,29 +851,24 @@ def rank_program(g, core, T, topo):
                 send([(prv, eng_p, T["GV"][:, 256:512], r("GO"), "aG")])
                 arrive("G", [r("GV", 256, 512)], n_bk)
             else:
-                act(r("XT"), ind(r("XH", 0, V), su(uV)), bias=-0.5)
                 mm(r("ps0", 256, 512), ID75, r("XT"), True, False)
-                mm(r("ps0", 256, 512), ID25, r("YA"), False, True)
+                mm(r("ps0", 256, 512), ID25, r("YA", 256 * t, 256 * t + 256), False, True)
                 go()
 
         def mixed():
             ts(nx, r("ps0", 256, 512), CR, A.add, CR, A.subtract)
-            nxo = nx
-            if rot_out:
-                nxo = r("NR", 256 * t, 256 * t + 256)
-                mm(r("ps6", 256, 512), r("IDR"), nx)
-                go()
-                act(nxo, r("ps6", 256, 512))
-            send([(nxt, eng_n, T["XU"][:, 256 * t:256 * t + 256], nxo, "aN%d" % t)])
 
         def columns():
             act(r("FW", 256, 512), ind(r("BF", 0, V), su(uV)), AF.Copy)
 
-        def accepted():
+        def dumps():
             mm(r("ps0", 64, 112), IDf, r("DW3"), True, False)
             go()
-            tt(sm(sACC), sm(sRES), sm(sOW3), A.is_le)
-            expand(r("E5"), sm(sACC), r("DM"))
+
+        def accepted():
+            if nv:
+                tt(sm(sRES, 0, nv), sm(sACC, 0, nv), sm(sNOW, 0, nv), A.add)
+            expand(r("E5"), sm(sRES), r("DMN"), A.is_lt)
             for k in range(6):
                 mm(r("ps0", 64 + 8 * k, 72 + 8 * k), r("E5", 128 * (k % 2), 128 * (k % 2) + 128), B8n, False, k == 5)
             go()
@@ -865,35 +878,48 @@ def rank_program(g, core, T, topo):
             cp(r("LS", 48 * t, 48 * t + 48), r("LF"))
             if end:
                 send([(prv, eng_p, T["ML"][:, :], r("LS", 48 * t, 48 * t + 32), "aE")])
-                return
-            vso = vs
-            if rot_out:
-                vso = r("VR", 16 * t, 16 * t + 16)
-                mm(r("ps6", 96, 112), r("IDf", 112, 240), r("LF", 32, 48))
+
+        def changes():
+            cp(ind(r("F", FN, FE), r("LS", 48 * t + 16, 48 * t + 32)), r("FW", 256, 512))
+            fo, fi = ind(r("F", FN, FE), r("LS", 48 * t, 48 * t + 16)), r("FW", 0, 256)
+            node("a", [fo], [fi], [lambda: g.scalar.activation(fo[0], fi[0], AF.Silu)], cost(fo, [fi]))
+
+        def own():
+            cp(ind(r("XH"), vs), nx)
+
+        def request():
+            ts(mine_u, found, 2048.0, A.add)
+            if rot_in:
+                act(sm(sU0), found, bias=2048.0)
+                mm(r("ps1", 0, 16), BACK, sm(sU0))
                 go()
-                cp(vso, r("ps6", 96, 112))
-            send([(nxt, eng_n, T["LU"][:, 16 * t:16 * t + 16], vso, "aL%d" % t)])
-            if t == 0:
-                send([(nxt, eng_n, land["B0"], r("B", 0, 1024), "aB0")])
+            else:
+                send([(prv, eng_p, T["UQ"][:, 16 * t:16 * t + 16], uo, "aU%d" % (t + 1))])
 
         def askers():
-            ts(uU, found, 2048.0, A.add)
             if t == 1:
                 arrive_turned("B1", "BG", 1024, 2048, T["dB"][1], n_h, "h2", 12000.0)
                 arrive_turned("B0", "BG", 0, 1024, T["dB"][0], n_in, None, 8000.0)
+            if rot_in:
+                cp(uo, r("ps1", 0, 16))
+                send([(prv, eng_p, T["UQ"][:, 16 * t:16 * t + 16], uo, "aU%d" % (t + 1))])
             b0 = 2056 if t % 2 == 0 else 0
-            cp(r("WL", 0, 256), ind(r("BG", b0, b0 + 2056), uU))
+            cp(r("WL", 0, 256), ind(r("BG", b0, b0 + 2056), mine_u))
+            if t == 0:
+                send([(nxt, eng_n, land["B0"], r("B", 0, 1024), "aB0")])
 
         def numbers():
             act(r("VAL", 64 - val, 80 - val), found, bias=2048.0 + s0)
-            act(r("EU"), ind(r("BKI", s0, s0 + 2064), uU), AF.Copy)
+            act(r("EU"), ind(r("BKI", s0, s0 + 2064), mine_u), AF.Copy)
+            act(r("JT", 128 * t + 128, 128 * t + 256), r3("J2", 0, 8, 15 - t, 31 - t))
 
-        chain[0] = {}
-        step = dict(c=choice, m=marks, h=holders, f=flags, n=newkeys, t=theirs, x=mixed, w=columns, a=accepted, l=lists,
-                    u=askers, e=numbers, s=counts, z=level1, y=level2)
+        chain[0] = dict(keep, on="vat")
+        step = dict(c=choice, h=holders, H=held, f=flags, Q=places, s=counts, r=prefix, z=level1, y=level2, q=request,
+                    u=askers, e=numbers, t=theirs, x=mixed, w=columns, n=newkeys, d=dumps, a=accepted, l=lists,
+                    g=changes, o=own)
         for w in OPT["LAST" if end else "ORDER2"].split():
-            if w[0] == "p":
-                pairs(int(w[1]))
+            if w[0] in "pm":
+                (pairs if w[0] == "p" else marks)(int(w[1]))
             else:
                 step[w]()
         if end:
@@ -906,26 +932,12 @@ def rank_program(g, core, T, topo):
             else:
                 dma([(T["ym"][:, :], r("F", FN, FP, p=(14, 128, 16)))])
             break
-        cp(ind(r("F", FN, FE), r("LS", 48 * t + 16, 48 * t + 32)), r("FW", 256, 512))
-        fo, fi = ind(r("F", FN, FE), r("LS", 48 * t, 48 * t + 16)), r("FW", 0, 256)
-        node("a", [fo], [fi], [lambda fo=fo, fi=fi: g.scalar.activation(fo[0], fi[0], AF.Silu)], cost(fo, [fi]))
-        if t == 0:
-            node("x", [], [r("XH")], [], 0.0, 0.0, 0, ("sx", sent["sx"]), {sends["aX0"]: 0})
-        cp(ind(r("XH"), vs), nx)
+        keep = chain[0]
         chain[0] = None
-        arrive("N%d" % t, [r("XU", 256 * t, 256 * t + 256)], n_in, lat=3500.0)
-        arrive("L%d" % t, [r("LU", 16 * t, 16 * t + 16)], n_in, lat=3000.0)
         if t == RO - 2:
             dma([(r("FC"), r("F", FN, FP, p=(14, 128, 16)))])
-            act(r("FR", 0, 256), r("FC"), bias=CR)
-            act(r("FR", 256, 512), r("FR", 0, 256), bias=-CR)
-            tt(r("MO", 0, 256), r("FC"), r("FR", 256, 512), A.subtract)
-            ts(r("FR", 0, 256), r("FC"), 2047.75, A.is_gt, 0.5, A.mult)
-            tt(r("FR", 256, 512), r("MO", 0, 256), r("FR", 0, 256), A.max)
-            act(r("MO", 256, 512), r("FR", 256, 512), scale=8192.0)
-            send([(prv, eng_p, T["dM"][:, :], r("MO", 256, 512), "aM")])
 
     final, wait = emit_in_planned_order(nodes, Q, T)
-    final.update(sent)
+    final["sent"] = sent[0]
     for s in final:
         wait("g", s, final[s])

from concourse.bass import DstId, RemoteDMATransfer
from concourse.mybir import AluOpType as A, AxisListType, ActivationFunctionType as AF

V = 4096
RO = 4
FN, FP, FD, FE = 256, 4352, 4384, 4896
DUMP = 4128
CR = 12582912.0
CAP = 1040.0 * 65536
PEN = 134217728.0
OPT = dict(XG_V=(3,), PEN_V=(1,), RED_V=(0, 4), Z_A=(4, 0), FB_A=((0, 1024), (1024, 2304)), FB_V=((2304, 4096),),
           ORDER="p0 f0 g0 p1 i0 f1 e0 x0 f2 d0 i1 y1 y0 a0 e1 i2 f3 e2 c0 d1 y2 x1 a1 A0 C0 x2 i3 q0 y4 y3 q1 s0 d2 e3 A1 d3 c1 C1 x3 a2 q2 r0 y5 b0 A2 c2 C2 q3 K0 a3 k0 s1 c3 B0 A3 r1 b1 C3 B1",
           ORDER2="c p3 p2 t m0 p0 m1 p4 m2 m3 p5 f x Q p1 s p7 r p6 h z H d a y l w q g u n o e",
           LAST="c p4 p0 p5 t p1 p6 p3 p2 p7 h H d a n l")
CY, PE, GA, SC, HOP = 0.83, 0.47, 1.56, 3.8, 120.0

f32, bf, f16, i32, u16 = "float32", "bfloat16", "float16", "int32", "uint16"


def _sb(n, dt):
    return ("sbuf", [128] + (n if isinstance(n, list) else [n]), dt)


SCRATCH = {
    "B": _sb(4104, i32), "BF": _sb(4104, f32), "F": _sb(FE, f32), "BG": _sb(4112, i32), "XH": _sb(4384, bf),
    "BKI": _sb(4384, f32),
    "FO": _sb(4096, f16), "XO": _sb(4096, bf), "AB": _sb([32, 128], bf), "EQ": _sb([16, 128], bf),
    "VO": _sb(256, u16), "V16": _sb(256, f16), "WL": _sb(272, u16), "YA": _sb(1024, bf),
    "PI": _sb(8, i32), "CO": _sb(64, f32), "N256": _sb(256, f32), "QN": _sb(256, f32),
    "NB": _sb(256, bf), "DMN": _sb(256, f32), "NH": _sb(256, f32),
    "J2": _sb([8, 32], f32), "SEI": _sb(24, f32), "SEL": _sb(24, f32), "HL": _sb(48, bf),
    "DM": _sb(256, f32), "RST": _sb(128, f32), "STA": _sb(256, bf),
    "UB": _sb(144, bf), "UH": _sb(144, bf), "TRI": _sb(128, bf), "UPR": _sb(128, bf),
    "TRC": _sb(128, bf), "MB": _sb(128, bf), "MU": _sb(384, bf),
    "ID": _sb(512, bf), "IDf": _sb(256, f32), "S": _sb(2048, bf), "ROT": _sb([8, 32], bf), "RON": _sb([8, 32], bf),
    "PD": _sb(1024, bf), "CK": _sb(1024, bf), "JT": _sb(512, bf), "ONE": _sb(256, bf), "ZERO": _sb(128, bf),
    "B8": _sb(64, bf), "SM": _sb(16 * 24, f32), "SB": _sb(96, bf), "SI": _sb(64, i32), "SU": _sb(16 * 8, u16),
    "MP": _sb(256, i32), "T1": _sb([16, 32], f32), "T2": _sb([16, 32], f32), "T3": _sb(256, f32), "WS": _sb(256, u16),
    "IF": _sb(128, bf), "ZC": _sb(256, f32), "ZN": _sb(256, f32), "W0": _sb(272, u16),
    "Y0": _sb(1024, bf), "UQ": _sb(48, u16), "UO": _sb(48, u16), "WR": _sb(256, u16),
    "KC": _sb(1024, i32), "KF": _sb(768, f32),
    "OH": _sb(2048, bf), "OQ": _sb(256, bf), "FT": _sb(128, bf), "QB": _sb(144, bf), "Z": _sb([16, 128], bf),
    "P": _sb(136, f32), "CMP": _sb(256, bf), "JK": _sb(4096, bf),
    "PEN": _sb(256, bf), "SUP": _sb(256, bf), "KS": _sb(256, f32),
    "E1": _sb(256, f32), "E2": _sb(256, bf), "E5": _sb(256, bf), "EU": _sb(256, bf),
    "G1": _sb(256, f32), "R": _sb(256, bf), "LE": _sb(256, bf), "LO": _sb(256, bf),
    "NEW": _sb(256, f32), "FW": _sb(512, f32), "XT": _sb(256, bf),
    "VAL": _sb(96, f32), "DW3": _sb(48, f32), "LF": _sb(48, f32), "LS": _sb(192, u16), "NX": _sb(768, bf),
    "FC": _sb(256, f32), "FR": _sb(512, f32), "MO": _sb(256, f32), "GV": _sb(512, f32), "GO": _sb(256, f32),
    "ML": _sb(32, u16),
    "dZ": ("dram", [128, 256], f32), "dM": ("dram", [128, 256], f32), "dB": ("dram", [4, 128, 1024], i32),
}
for _k in range(8):
    SCRATCH["ps%d" % _k] = ("psum", [128, 512], f32)
SIZE = {f32: 4, i32: 4, bf: 2, f16: 2, u16: 2}

MSG = ["W", "w", "Y0", "Y1", "Y2", "Y3", "Z", "B0", "B1", "B2", "B3", "U1", "U2", "U3", "M", "G", "E"]
SEMAPHORES = (["qv", "qa", "qt", "qg", "sent", "h1", "h2"] + ["a" + m for m in MSG]
              + ["d%d" % k for k in range(30)])


def _mask(engines):
    m = 0
    for e in engines:
        m |= 1 << e
    return m


def helper_of(T, topo, r):
    me, nxt = T.cores[r], T.cores[(r + 1) % len(T.cores)]
    for c in topo.cores_of(me):
        if T.rank_of(c) is None and topo.die(c) != topo.die(me) and topo.may_write(c, nxt):
            return c
    return None


def landing(T, rot):
    d = {}
    for k in range(4):
        lo = 1024 * k + (8 if k >= 2 else 0)
        d["B%d" % k] = T["dB"][k] if rot else T["BG"][:, lo:lo + 1024]
    return d


def helper_program(g, core, T, topo, r):
    n = len(T.cores)
    nxt = T.cores[(r + 1) % n]
    land = landing(T, (r + 1) % n == 0)
    cnt = len([e for e in topo.engines(T.cores[r], core) if e not in topo.engines(T.cores[r], nxt)])
    rid, pid, _ = topo.addr(nxt)
    m = topo.mask(core, nxt)
    tot = 0
    for s, src, name in (("h1", T["BG"][:, 0:1024], "B3"), ("h2", T["BG"][:, 1024:2048], "B1")):
        g.wait_ge(T.sem[s], cnt)
        g.remote_dma(land[name], src, T.sem["a" + name], T.sem["sent"], pid, rid, m)
        tot += len(topo.engines(core, nxt))
    g.wait_ge(T.sem["sent"], tot)


def emit_in_planned_order(nodes, Q, T):
    succ = [[] for _ in nodes]
    for i, nd in enumerate(nodes):
        for p in nd["pre"]:
            succ[p].append(i)
    prio = [0.0] * len(nodes)
    for i in range(len(nodes) - 1, -1, -1):
        prio[i] = nodes[i]["cost"] + nodes[i]["lat"] + max([prio[s] + HOP for s in succ[i]] + [0.0])
    left = [len(nd["pre"]) for nd in nodes]
    at = [0.0] * len(nodes)
    free = {}
    ready = [i for i in range(len(nodes)) if left[i] == 0]
    order = []
    while ready:
        st = {i: max(at[i], free.get(nodes[i]["q"], 0.0) if nodes[i]["q"] != "x" else 0.0) for i in ready}
        i = min(ready, key=lambda k: (st[k], -prio[k]))
        for k in ready:
            if nodes[k]["q"] == nodes[i]["q"] != "x" and prio[k] > prio[i] and st[k] < st[i] + min(
                    0.6 * nodes[i]["cost"], 0.5 * (prio[k] - prio[i])) + 1:
                i = k
        ready.remove(i)
        nd = nodes[i]
        free[nd["q"]] = st[i] + nd["cost"]
        order.append(i)
        for s in succ[i]:
            done = st[i] + nd["cost"] + (nd["lat"] + HOP if nodes[s]["pre"][i] != 0 or nd["q"] == "x" else 0.0)
            at[s] = max(at[s], done)
            left[s] -= 1
            if left[s] == 0:
                ready.append(s)
    count, final = {}, {}
    for i in order:
        nd = nodes[i]
        if nd["tok"] is None and nd["inc"]:
            count[nd["q"]] = count.get(nd["q"], 0) + len(nd["emit"])
            nd["tok"] = ("q" + nd["q"], count[nd["q"]])
    waited = {q: {} for q in Q}

    def wait(q, s, v):
        if waited[q].get(s, 0) < v:
            Q[q].wait_ge(T.sem[s], v)
            waited[q][s] = v

    for i in order:
        nd = nodes[i]
        if nd["tok"] is not None:
            final[nd["tok"][0]] = max(final.get(nd["tok"][0], 0), nd["tok"][1])
        if nd["q"] == "x":
            continue
        need = {}
        for p in nd["pre"]:
            if nd["pre"][p] == 1:
                s, v = nodes[p]["tok"]
                need[s] = max(need.get(s, 0), v)
        for s in need:
            wait(nd["q"], s, need[s])
        for e in nd["emit"]:
            h = e()
            if nd["inc"]:
                h.then_inc(T.sem[nd["tok"][0]], nd["inc"])
    return final, wait


def rank_program(g, core, T, topo):
    rank = T.rank_of(core)
    n = len(T.cores)
    if rank is None:
        for r in range(n):
            if helper_of(T, topo, r) == core:
                helper_program(g, core, T, topo, r)
        return
    nxt, prv = T.cores[(rank + 1) % n], T.cores[(rank - 1) % n]
    hlp = helper_of(T, topo, rank)
    rot_in = rank == 0
    rot_out = rank == n - 1
    Q = {"v": g.vector, "a": g.scalar, "t": g.tensor, "g": g, "s": g.sync}
    nodes, log, last, sends = [], {}, {}, {}
    nd = [0]
    group = []
    chain = [None]

    def r(name, lo=0, hi=None, step=1, p=None):
        t = T[name]
        if hi is None:
            hi = t.shape[1]
        ps = slice(None) if p is None else slice(*p)
        return (t[ps, lo:hi:step] if step != 1 else t[ps, lo:hi], [(name, lo, hi)], len(range(lo, hi, step)), name, "")

    def r3(name, a0, a1, b0, b1):
        w = T[name].shape[2]
        return (T[name][:, a0:a1, b0:b1], [(name, a0 * w, a1 * w)], (a1 - a0) * (b1 - b0), name, "")

    def ind(win, off):
        return (win[0].indirect(off[0]), win[1] + off[1], 16 * off[2], win[3], "i")

    def dr(apx, name):
        return (apx, [(name, 0, 1)], 0, name, "")

    def sm(k, lo=0, hi=16):
        return r("SM", 16 * k + lo, 16 * k + hi)

    def sb(k, lo=0, hi=16):
        return r("SB", 16 * k + lo, 16 * k + hi)

    def su(k, w=16):
        return r("SU", 16 * k, 16 * k + w)

    def co(k):
        return r("CO", k, k + 1)

    def regs(xs, out=False):
        rd, wr = [], []
        for x in xs:
            if isinstance(x, tuple):
                if out:
                    wr += x[1][:1]
                    rd += x[1][1:]
                else:
                    rd += x[1]
        return rd, wr

    def ap(x):
        return x[0] if isinstance(x, tuple) else x

    def node(q, outs, ins, emit, cost, lat=0.0, inc=1, tok=None, extra=None, keep=True):
        rd2, wr = regs(outs, True)
        rd = regs(ins)[0] + rd2
        me = len(nodes)
        pre = dict(extra or {})
        for rs, w in ((rd, False), (wr, True)):
            for name, lo, hi in rs:
                psum = name.startswith("ps")
                for lo2, hi2, k, w2 in log.get(name, []):
                    q2 = nodes[k]["q"]
                    if psum and q2 == q == "t":
                        pre.setdefault(k, 0)
                    elif (psum and q2 != q) or ((w or w2) and lo < hi2 and lo2 < hi):
                        pre[k] = 1
                    elif psum:
                        pre.setdefault(k, 0)
        if q in "gs":
            if q in last:
                pre.setdefault(last[q], 0)
            last[q] = me
        if chain[0] is not None and q in chain[0].get("on", "va"):
            if q in chain[0]:
                pre.setdefault(chain[0][q], 0)
            chain[0][q] = me
        nodes.append(dict(q=q, emit=emit, cost=cost, lat=lat, inc=inc, tok=tok, pre=pre))
        for rs, w in ((wr, True), (rd, False)):
            for name, lo, hi in (rs if keep else []):
                old = log.get(name, [])
                if name.startswith("ps"):
                    old = [e for e in old if e[2] == me or (nodes[e[2]]["q"] == q != "t")]
                if w:
                    old = [e for e in old if not (lo <= e[0] and e[1] <= hi)]
                log[name] = old + [(lo, hi, me, w)]
        return me

    def cost(o, ins, k=1.0):
        if o[4]:
            return 50 + o[2] * SC * CY
        if ins[0][4]:
            return 50 + o[2] * GA * CY
        if k == 1.0 and all(SIZE[SCRATCH[x[3]][2]] == 2 for x in [o] + ins):
            k = 0.5
        return 30 + max(64, max(o[2], ins[0][2]) * k) * CY

    def ts(o, i, s1, op0, s2=None, op1=None):
        if op1 is None:
            node("v", [o], [i, s1], [lambda: g.vector.tensor_scalar(o[0], i[0], ap(s1), None, op0)], cost(o, [i]))
        else:
            node("v", [o], [i, s1, s2], [lambda: g.vector.tensor_scalar(o[0], i[0], ap(s1), ap(s2), op0, op1)], cost(o, [i]))

    def tt(o, a, b, f):
        k = 1.01 if "ps" in (a[3][:2], b[3][:2]) else 2.0
        node("v", [o], [a, b], [lambda: g.vector.tensor_tensor(o[0], a[0], b[0], f)], cost(o, [a, b], k))

    def cp(o, i):
        node("v", [o], [i], [lambda: g.vector.tensor_copy(o[0], i[0])], cost(o, [i]))

    def ms(o, c):
        node("v", [o], [], [lambda: g.vector.memset(o[0], c)], cost(o, [o]))

    def scan(o, d0, d1, init, op0, op1):
        node("v", [o], [d0, d1, init], [lambda: g.vector.tensor_tensor_scan(o[0], d0[0], d1[0], ap(init), op0, op1)], cost(o, [d0, d1]))

    def red(o, i, f):
        node("v", [o], [i], [lambda: g.vector.tensor_reduce(o[0], i[0], AxisListType.X, f)], cost(o, [i], 1.01))

    def act(o, i, f=AF.Identity, bias=0.0, scale=1.0, acc=None):
        c = cost(o, [i], 1.01) + 30
        if acc is None:
            node("a", [o], [i, bias, scale], [lambda: g.scalar.activation(o[0], i[0], f, bias=ap(bias), scale=ap(scale))], c)
        else:
            node("a", [o, acc], [i, bias, scale],
                 [lambda: g.scalar.activation(o[0], i[0], f, bias=ap(bias), scale=ap(scale), accum_out=acc[0])], c)

    def mm(o, l, rh, start=True, stop=True):
        group.append((o, l, rh, start, stop))

    def go():
        ms_ = list(group)
        del group[:]
        em = [(lambda m=m: g.tensor.matmul(m[0][0], m[1][0], m[2][0], m[3], m[4])) for m in ms_]
        c = sum(max(64, m[2][2]) * SIZE[SCRATCH[m[1][3]][2]] ** 2 / 4 * PE for m in ms_)
        node("t", [m[0] for m in ms_], [m[1] for m in ms_] + [m[2] for m in ms_], em, c)

    def iota(o, pat, base=0, ch=0, fl=True):
        if fl:
            node("g", [o], [], [lambda: g.iota(o[0], pat, base, ch, allow_small_or_imprecise_dtypes=True)], 130 + 2 * o[2])
        else:
            node("g", [o], [], [lambda: g.iota(o[0], pat, base, ch)], 130 + 2 * o[2])

    def select(o, i, pat, f, fill, base, ch):
        node("g", [o], [i], [lambda: g.affine_select(o[0], i[0], pat, f, fill, base, ch)], 170 + 2 * o[2])

    def diagonal(o, i, fill):
        select(o, i, [[-1, 128]], A.not_equal, fill, 0, 1)

    def dma(pairs, lat=2200.0, add=False):
        s = "d%d" % nd[0]
        nd[0] += 1
        if add:
            em = [(lambda a=a, b=b: g.dma_start(ap(a), ap(b), accum_op=A.add, max_dma_last_dim=8192)) for a, b in pairs]
        else:
            em = [(lambda a=a, b=b: g.sync.dma_start(ap(a), ap(b))) for a, b in pairs]
        node("g" if add else "s", [a for a, _ in pairs], [b for _, b in pairs], em, 100.0 * len(pairs), lat, 16,
             (s, 16 * len(pairs)))

    eng_n, eng_p = topo.engines(core, nxt), topo.engines(core, prv)
    eng_h = [e for e in topo.engines(core, hlp) if e not in eng_n]
    sent = [0]

    def send(items, c=1200.0):
        def em():
            if len(items) == 1:
                d, en, o, s, name = items[0]
                rid, pid, _ = topo.addr(d)
                return g.remote_dma(o, s[0], T.sem[name], T.sem["sent"], pid, rid, _mask(en))
            tr = []
            for d, en, o, s, name in items:
                rid, pid, _ = topo.addr(d)
                tr.append(RemoteDMATransfer(dst_ids=[DstId(rid=rid, pnc=pid)], dma_engine_mask=_mask(en),
                                            remote_sem=T.sem[name], src=s[0], dst=o))
            return g.remote_dma_fused(tr, local_sem=T.sem["sent"])
        k = node("g", [], [it[3] for it in items], [em], c, 0.0, 0, keep=False)
        for it in items:
            sends[it[4]] = k
        sent[0] += sum(len(it[1]) for it in items)

    n_in = len(topo.engines(prv, core))
    n_bk = len(topo.engines(nxt, core))
    n_h = len(topo.engines(helper_of(T, topo, (rank - 1) % n), core))

    def arrive(name, outs, count, like=None, lat=2500.0):
        node("x", outs, [], [], 0.0, lat, 0, ("a" + name, count), {sends[like or "a" + name]: 0})

    def arrive_turned(name, b, lo, hi, d, count, like=None, lat=2500.0):
        if not rot_in:
            arrive(name, [r(b, lo, hi)], count, like, lat)
            return
        arrive(name, [dr(d, "d" + name)], count, like, lat)
        dma([(r(b, lo, hi, p=(16, 128)), dr(d[0:112, :], "d" + name)), (r(b, lo, hi, p=(0, 16)), dr(d[112:128, :], "d" + name))])

    (cP, cQ, cG, cE1, cE0, cU, cLT, cBit, cBp, cVo, cHi, cH1, cL1, cL2, cO1, cO2, cMB, cPW, cW14,
     cUH, cNB, cZN, cST, cLo, cOff, cA, cB, cC) = range(28)
    SK = 32
    sOW0, sOW1, sOW2, sNOW, sRES, sACC, sB8, sZ, sA1, sA2, sA3, sA4, sPW, sU0, sF8 = range(15)
    bCC, bT2, bN8, bMF, bOFF = range(5)
    uLB, uLT, uM, uV, uG2, uL3 = range(6)
    uU = r("WL", 256, 272)
    ID, NID, ID75, ID25, IDf = r("ID", 0, 128), r("ID", 128, 256), r("ID", 256, 384), r("ID", 384, 512), r("IDf", 0, 128)
    FWD, BACK = r("IDf", 112, 240), r("IDf", 16, 144)
    B8, B8s, B8n = r("B8", 0, 8), r("B8", 16, 24), r("B8", 32, 40)
    one1 = r("ONE", 0, 128, p=(0, 1))
    found = r("ps6", 272, 288)
    land = landing(T, rot_out)

    def fill(o, c):
        act(o, r("N256", 0, o[2]), bias=c, scale=0.0)

    def between(o, lo_, hi_):
        select(o, r("ONE", 0, o[2]), lo_[0], A.is_ge, 0.0, lo_[1], lo_[2])
        select(o, o, hi_[0], A.is_ge, 0.0, hi_[1], hi_[2])

    def counts():
        mm(r("ps5", 256, 264), r("QB", 1, 129), B8)
        go()
        mm(r("ps1", 128, 256), r("TRI"), r("QB", 1, 129), True, False)
        mm(r("ps1", 128, 256), r("UPR"), r("QB", 0, 128), False, True)
        go()
        cp(sb(bCC, 0, 8), r("ps5", 256, 264))

    def prefix():
        cp(r("P", 0, 128), r("ps1", 128, 256))

    def level1(z_=1):
        for k in range(8):
            z = (T["Z"][:, :, 16 * k:16 * k + 16], [("Z", k, k + 1)], 256, "Z", "")
            if k < 8 - OPT["Z_A"][z_]:
                ts(z, r("NB"), sb(bCC, k, k + 1), A.is_lt, 2.0, A.mult)
            else:
                act(z, r("NH"), AF.Sign, bias=sb(bCC, k, k + 1), scale=-1.0)
        mm(r("ps5", 272, 288), ID, sb(bOFF + z_), True, False)
        for b in range(16):
            mm(r("ps5", 272 + b, 273 + b), (T["Z"][:, b, :], [("Z", 0, 8)], 128, "Z", ""), sb(bN8, 0, 1), False, b == 15)
        go()

    def level2(copy=act):
        ts(su(uM), r("ps5", 272, 288), 1.0 / 16, A.mult, 128.0, A.add)
        copy(sb(bMF), r("ps5", 272, 288))
        mm(found, ID, sb(bMF), True, False)
        tt(r("CMP"), ind(r("P", 0, 136), su(uM)), r("N256"), A.is_le)
        for q in range(16):
            mm(found, r("UB", 15 - q, 143 - q), r("CMP", q, 256, 16), False, q == 15)
        go()

    def features(t, win, lst):
        y = r("Y0", 256 * t, 256 * t + 256)
        act(y, ind(win, lst), AF.Copy)
        send([(nxt, eng_n, T["YA"][:, 256 * t:256 * t + 256], y, "aY%d" % t)])
        arrive("Y%d" % t, [r("YA", 256 * t, 256 * t + 256)], n_in)

    def as_float(k):
        ts(r("BF", 1024 * k, 1024 * k + 1024), r("B", 1024 * k, 1024 * k + 1024), -2048.0, A.add)

    def codes(k0, k1):
        for k in range(k0, k1):
            for a in range(0, 1 << k, 1024):
                b = min(a + 1024, 1 << k)
                act(r("BKI", (1 << k) + a, (1 << k) + b), r("BKI", a, b), scale=co(SK + k))

    chain[0] = {}
    if rot_out:
        dma([(r("MP", p=(16, 128)), T["mp"][0:7, :]), (r("MP", p=(0, 16)), T["mp"][7:8, :])], 2000.0)
    else:
        dma([(r("MP"), T["mp"][:, :])], 2000.0)
    for k in range(4):
        dma([(r("B", 1024 * k, 1024 * k + 1024), T["nb"][:, 1024 * k:1024 * k + 1024])], 3500.0 + 1900.0 * k)
    dma([(r("XH", 0, V), T["x"][:, :])], 13500.0)
    dma([(r("KC", 0, 256), T["ky"][:, :]), (r("KC", 256, 512), T["iv"][:, :])], 10000.0)
    iota(r("PI", 0, 1), [[0, 1]], 0, 1, False)
    iota(r("N256"), [[1, 256]])
    iota(r("QN"), [[0, 16], [1, 16]])
    ms(r("ONE"), 1.0)
    ms(r("ZERO"), 0.0)
    between(r("TRI"), ([[-16, 8], [0, 16]], 0, 1), ([[16, 8], [1, 16]], 0, -1))
    between(r("UPR"), ([[-16, 8], [-1, 16]], -1, 1), ([[16, 8], [0, 16]], 15, -1))
    select(r3("ROT", 0, 8, 0, 32), r("ONE"), [[-16, 8], [0, 2], [-1, 16]], A.is_equal, 0.0, 0, 1)
    ts(r("PI", 1, 2), r("PI", 0, 1), 15, A.bitwise_and)
    ts(r("PI", 2, 3), r("PI", 0, 1), 4, A.logical_shift_right)
    ts(r("PI", 3, 4), r("PI", 0, 1), 4, A.logical_shift_right, 1, A.bitwise_and)
    cp(r("CO", 0, 4), r("PI", 0, 4))
    ms(r("QB", 0, 16), 0.0)
    act(co(cE0), co(cE1), bias=1.0, scale=-1.0)
    act(co(cLT), co(cQ), scale=16.0)
    act(co(cU), co(cG), bias=15.0, scale=16.0)
    act(co(cBp), co(cQ), bias=4096.0, scale=2.0)
    ts(IDf, r("N256", 0, 128), co(cP), A.is_equal)
    ts(B8, r("N256", 0, 8), co(cG), A.is_equal)
    ts(su(uLT), r("N256", 0, 16), co(cLT), A.add)
    for k in range(2):
        if OPT["Z_A"][k]:
            ts(co(cOff), co(cG), 7.5 - OPT["Z_A"][k], A.is_gt, -1024.0, A.mult)
            fill(sb(bOFF + k), co(cOff))
        else:
            ms(sb(bOFF + k), 0.0)
    ts(co(cBit), co(cQ), 11.5, A.is_lt)
    ts(r("DM"), r("QN"), co(cQ), A.is_equal)
    ts(r("UB"), r("N256", 0, 144), co(cU), A.is_equal)
    act(r("NB"), r("N256"))
    act(ID, IDf)
    fill(r("P", 128, 136), 9999.0)
    fill(sb(bN8, 0, 2), -8.0)
    act(r("NH"), r("N256"), bias=0.5)
    ts(r3("T1", 0, 16, 0, 16), r("MP"), co(cE0), A.mult)
    ts(r3("T1", 0, 16, 16, 32), r("MP"), co(cE1), A.mult)
    node("v", [r3("T2", 0, 16, 0, 32)], [r3("T1", 0, 16, 0, 32)],
         [lambda: g.vector.transpose(T["T2"][:, :, :], T["T1"][:, :, :])], 550.0)
    tt(r("T3"), r3("T2", 0, 16, 0, 16), r3("T2", 0, 16, 16, 32), A.add)
    cp(r("WS"), ind(r("T3"), su(uLT)))
    send([(nxt, eng_n, T["WR"][:, :], r("WS"), "aW")], c=3000.0)
    arrive("W", [r("WR")], n_in, lat=3000.0)
    act(co(cVo), co(cBp), bias=-2048.0)
    fill(r("BF", V, V + 8), co(cVo))
    act(r("CO", SK, SK + 12), r("DM", 0, 12), bias=1.0, scale=-2.0)
    act(r("BKI", 0, 1), co(cBit))
    for i in range(9):
        codes(i, i + 1)
        act(r("S", 128 * i, 128 * i + 128), IDf, scale=r("DM", i, i + 1))
    if rot_out or rot_in:
        act(r("IDf", 128, 256), IDf)

    ts(r("IF"), r("WS", 0, 128), 4095.5, A.is_gt)
    scan(r("QB", 1, 129), r("ONE", 0, 128), r("IF"), 0.0, A.mult, A.add)
    for k in range(1, 9):
        diagonal(r("PD", 128 * (k - 1), 128 * k), r3("ROT", 0, 8, k, k + 16), -1.0)
    counts()
    level1(0)
    prefix()
    as_float(0)
    codes(9, 11)
    for i in range(9, 16):
        act(r("S", 128 * i, 128 * i + 128), IDf, scale=r("DM", i, i + 1))
    act(NID, FWD if rot_in else IDf, scale=-1.0)
    if rot_in:
        act(ID25, FWD, scale=0.25)
    act(r3("RON", 0, 8, 0, 32), r3("ROT", 0, 8, 0, 32), scale=-1048576.0)
    act(B8s, B8, scale=65536.0)
    act(B8n, B8, scale=-8192.0)
    act(sm(sB8, 0, 8), B8)
    act(co(cA), r("DM", 0, 1), scale=1.0 / 8192)
    act(sm(sF8, 0, 8), B8, scale=co(cA))
    act(co(cHi), r("DM", 14, 15), bias=r("DM", 15, 16))
    act(co(cUH), r("DM", 14, 15), bias=r("DM", 15, 16), scale=16.0)
    act(co(cMB), co(cBit), scale=1.0 / 512)
    act(co(cST), r("DM", 12, 13), scale=1.0 / 256)
    act(co(cLo), co(cQ), bias=float(DUMP))
    level2(cp)
    as_float(1)
    ts(r("W0", 256, 272), found, 2048.0, A.add)
    ts(sm(sA3), found, -0.5, A.is_gt, 2048.0, A.mult)
    ts(sm(sU0), found, 2048.0, A.add)
    ts(r("B", V, V + 8), r("N256", 0, 8), 0.0, A.mult, co(cBp), A.add)
    tt(sm(sA4), sm(sA3), sm(sU0), A.add)
    if rot_out:
        mm(r("ps0", 0, 16), BACK, sm(sA4))
        go()
        as_float(2)
        cp(su(uG2), r("ps0", 0, 16))
        cp(r("T3"), ind(r("B", 0, V + 8), su(uG2)))
        mm(r("ps0", 0, 256), FWD, r("T3"))
        go()
        as_float(3)
        cp(r("W0", 0, 256), r("ps0", 0, 256))
    else:
        cp(su(uG2), sm(sA4))
        as_float(2)
        cp(r("W0", 0, 256), ind(r("B", 0, V + 8), su(uG2)))
        as_float(3)
    send([(nxt, eng_n, T["WL"][:, :], r("W0"), "aw")])
    arrive("w", [r("WL")], n_in)
    iota(r3("J2", 0, 8, 0, 32), [[0, 16], [4096, 16]])
    iota(r("XH", V, DUMP), [[0, 32]])

    for a, b in OPT["FB_A"]:
        act(r("F", FN + a, FN + b), ind(r("BF", 0, V + 8), r("WR", a // 16, b // 16)), AF.Copy)
    for a, b in OPT["FB_V"]:
        ts(r("F", FN + a, FN + b), ind(r("B", 0, V + 8), r("WR", a // 16, b // 16)), -2048.0, A.add)
    fill(r("F", FP, FD), co(cVo))
    features(0, r("XH", 0, DUMP), su(uG2))
    ts(r("ZC"), r("MP"), 1.0 / 8192, A.mult)
    send([(nxt, eng_n, T["dZ"][:, :], r("ZC"), "aZ")])
    arrive("Z", [dr(None, "dZ")], n_in, lat=8000.0)
    act(co(cZN), co(cQ), scale=256.0 / 8192)
    act(r("ZN"), r("N256"), bias=co(cZN), scale=1.0 / 8192)
    dma([(r("BF", 0, V, p=(14, 128, 16)), r("ZN"))], 4000.0, True)
    ts(r("KC", 512, 768), r("KC", 256, 512), 4, A.logical_shift_right)
    ts(r("KC", 768, 1024), r("KC", 256, 512), 4096 + 15, A.bitwise_and)
    cp(r("KF", 0, 256), r("KC", 0, 256))
    cp(r("KF", 256, 768), r("KC", 512, 1024))
    send([(nxt, eng_n, land["B2"], r("B", 2048, 3072), "aB2"), (hlp, eng_h, T["BG"][:, 0:1024], r("B", 3072, V), "h1")])
    send([(hlp, eng_h, T["BG"][:, 1024:2048], r("B", 1024, 2048), "h2")])

    codes(11, 12)
    act(r("BKI", V, V + 16), r("N256", 0, 16))
    dma([(r("BKI", 0, V, p=(13 + k, 128, 16)), r("KF", 256 * k, 256 * k + 256)) for k in range(3)], 4000.0)
    for k in range(1, 8):
        diagonal(r("CK", 128 * k - 128, 128 * k), r3("RON", 0, 8, 16 - k, 32 - k), -1048576.0)
    for o, c in ((r("CK", 896, 1024), -1048576.0), (ID75, 0.75)) + (() if rot_in else ((ID25, 0.25),)):
        diagonal(o, r("ZERO"), c)
    iota(r("SEI"), [[16, 8], [1, 3]], 13)
    iota(r("E2"), [[0, 256]])
    iota(sm(sOW0), [[-128, 2], [0, 8]], 6143 * 256, -1)
    iota(r("BG", 2048, 2056), [[0, 8]], 4096, 0, False)
    iota(r("BG", 4104, 4112), [[0, 8]], 4096, 0, False)
    iota(r("GV", 0, 256), [[0, 256]], 4096)
    keep = chain[0]
    chain[0] = None
    act(co(cH1), co(cHi), bias=-1.0)
    act(co(cL1), co(cBit), bias=co(cHi), scale=512.0)
    act(r("UH"), r("UB"), scale=co(cUH))
    act(co(cL2), co(cBit), bias=co(cH1))
    act(co(cO1), co(cL1), scale=co(cE1))
    act(r("MB"), IDf, scale=co(cMB))
    act(co(cO2), co(cL2), scale=co(cE1))
    act(r("DW3", 0, 32), r("N256", 0, 32), bias=co(cLo), scale=16.0)
    act(r("DW3", 32, 48), r("N256", 0, 16), bias=co(cLo), scale=16.0)
    act(r("STA"), r("N256"), scale=co(cST))
    act(r("DMN"), r("DM"), bias=-1.0, scale=1.001)

    def constants():
        ts(r("TRC"), r("N256", 0, 128), co(cP), A.is_ge)
        cp(su(uLB), r("N256", 0, 16))
        ts(su(uL3), r("N256", 0, 16), 3.0, A.mult, 2.0, A.add)
        ts(r("SEL"), r("SEI"), co(cP), A.is_equal)
        ts(sm(sOW1), sm(sOW0), 1.0 / 256, A.mult)
        ms(sm(sA1), 2.0)
        ms(sm(sZ), 0.0)
        scan(sm(sPW), sm(sA1), sm(sZ), 0.5, A.mult, A.add)
        tt(sm(sA2), sm(sPW), r("DM", 0, 16), A.mult)
        ts(co(cB), r("DM", 15, 16), 7.5, A.mult)
        red(co(cPW), sm(sA2, 0, 12), A.add)
        red(co(cC), sm(sA2, 0, 4), A.add)
        ts(co(cNB), r("DM", 14, 15), 127.5, A.mult, co(cB), A.add)
        ts(co(cW14), co(cC), co(cPW), A.subtract, 1.0 / 32, A.mult)
        ts(r("MU", 128, 256), r("UB", 0, 128), co(cC), A.mult, -0.5, A.mult)
        ts(r("MU", 256, 384), r("UB", 1, 129), co(cPW), A.mult, -1.0 / 1024, A.mult)
        ts(r("MU", 0, 128), r("UB", 1, 129), co(cW14), A.mult)

    def expand(o, src, mask, f=A.mult):
        tt(o, ind(src, su(uLB)), mask, f)

    for t in range(RO):
        lo = 2048 * (t % 2)
        s0 = 2048 - lo
        end = t == RO - 1
        val = 48 * (t % 2)
        early = []

        def fg(c):
            ts(r("FO", 1024 * c, 1024 * c + 1024), ind(r("F", FN, FD), r("WL", 64 * c, 64 * c + 64)), CR, A.add, CR, A.subtract)

        def pick(c):
            for i in range(16):
                j = (i - t) % 16
                mm(r("ps0", 64 * c, 64 * c + 64), r("S", 128 * i, 128 * i + 128), r("FO", 1024 * c + j, 1024 * c + 1024, 16), i == 0, i == 15)
            go()

        def ev(c):
            ts(r("VO", 64 * c, 64 * c + 64), r("ps0", 64 * c, 64 * c + 64), 2048.0, A.add)
            cp(r("V16", 64 * c, 64 * c + 64), r("ps0", 64 * c, 64 * c + 64))

        def turned(c):
            for k in range(8):
                mm(r("ps7" if c % 2 else "ps1", 64 * k, 64 * k + 64), r("PD", 128 * k, 128 * k + 128), r("V16", 64 * c, 64 * c + 64))
            go()

        def eq(c):
            hh, o = c // 2, 64 * (c % 2)
            ts((T["EQ"][:, 8 * hh:8 * hh + 8, o:o + 64], [("EQ", 4 * c, 4 * c + 1)], 512, "EQ", ""),
               r("ps7" if c % 2 else "ps1"), 0.0, A.is_equal)

        def xg(c):
            xo, xi = r("XO", 1024 * c, 1024 * c + 1024), ind(r("XH", 0, DUMP), r("VO", 64 * c, 64 * c + 64))
            if c in OPT["XG_V"]:
                cp(xo, xi)
            else:
                act(xo, xi, AF.Copy)

        def mine(c, u):
            early.append((c, u))
            bank = "ps%d" % (2 + (2 * c + u) % 3)
            for k in range(8):
                mm(r(bank, 64 * k, 64 * k + 64), NID, r("YA", 256 * t + 64 * c, 256 * t + 64 * c + 64), k == 0, False)
            go()

        def ab(c, u):
            bank = "ps%d" % (2 + (2 * c + u) % 3)
            if (c, u) not in early:
                mine(c, u)
            for k in range(8):
                mm(r(bank, 64 * k, 64 * k + 64), ID, r("XO", 1024 * c + 8 * u + k, 1024 * c + 1024, 16), False, k == 7)
            go()

        def size(c, u):
            hh, o = c // 2, 64 * (c % 2)
            bank = "ps%d" % (2 + (2 * c + u) % 3)
            k = 16 * hh + 8 * u
            act((T["AB"][:, k:k + 8, o:o + 64], [("AB", 8 * hh + 4 * u + c % 2, 8 * hh + 4 * u + c % 2 + 1)], 512, "AB", ""),
                r(bank), AF.Abs)

        def support(hh):
            bank, a, b = "ps%d" % (6 + hh), 128 * hh, 128 * hh + 128
            eqs = [(T["EQ"][:, 8 * hh + k, :], [("EQ", 8 * hh, 8 * hh + 8)], 128, "EQ", "") for k in range(8)]
            for k in range(8):
                mm(r(bank, 0, 128), eqs[k], r("CK", 128 * k, 128 * k + 128), k == 0, k == 7)
            go()
            if hh in OPT["PEN_V"]:
                ts(r("PEN", a, b), r(bank, 0, 128), -0.5, A.is_gt, PEN, A.mult)
                cp(r("SUP", a, b), r(bank, 0, 128))
            else:
                act(r("PEN", a, b), r(bank, 0, 128), AF.Relu, bias=PEN, scale=128.0)
                act(r("SUP", a, b), r(bank, 0, 128))

        def rest(hh):
            bank, a, b = "ps%d" % (6 + hh), 128 * hh, 128 * hh + 128
            mm(r(bank, 0, 128), r("V16", a, b), ID, True, False)
            mm(r(bank, 0, 128), one1, r("JT", 128 * t, 128 * t + 128, p=(0, 1)), False, False)
            mm(r(bank, 0, 128), ID, r("SUP", a, b), False, False)
            mm(r(bank, 0, 128), ID, r("PEN", a, b), False, False)
            go()

        def best(hh, u):
            bank, a, b = "ps%d" % (6 + hh), 128 * hh, 128 * hh + 128
            for i in range(8 * u, 8 * u + 8):
                mm(r(bank, i, 128, 16), (T["AB"][:, 16 * hh + i, :], [("AB", 8 * hh + 4 * u, 8 * hh + 4 * u + 2)], 128, "AB", ""),
                   B8s, False, i == 15)
            go()
            if u:
                scan(r("KS", a, b), r("RST"), r(bank, 0, 128), 0.0, A.max, A.min)

        def asked(_):
            if t > 0:
                arrive("U%d" % t, [r("UQ", 16 * t - 16, 16 * t)], n_bk)
                features(t, r("XH", lo, lo + 2064), r("UQ", 16 * t - 16, 16 * t))

        def keys(_):
            if t > 0:
                cp(ind(r("BKI"), r("LS", 48 * t - 16, 48 * t)), r("NEW"))

        def before(h):
            if not end:
                if h == 0:
                    mm(r("ps5", 0, 128), one1, r("ZERO", p=(0, 1)), True, False)
                for q in range(8 * h, 8 * h + 8):
                    mm(r("ps5", q, 128, 16), r("F", FN + s0 + q, FN + s0 + 2048, 16), sm(sF8, 0, 8), False, False)
                go()

        if t == 0:
            act(r("JT", 0, 128), r3("J2", 0, 8, 16, 32))
            ts(r("RST"), r("QN", 0, 128), -2 * CAP, A.mult, CAP - 2048.0, A.add)
        chain[0] = dict(keep, on="vat")
        step = dict(K=lambda _: t or constants(), g=asked, k=keys, p=before, f=fg, i=pick, e=ev, d=turned, q=eq, x=xg,
                    s=support, r=rest, y=lambda u: mine(u // 2, u % 2), a=lambda c: ab(c, 0), c=lambda c: ab(c, 1),
                    A=lambda c: size(c, 0), C=lambda c: size(c, 1), b=lambda h: best(h, 0), B=lambda h: best(h, 1))
        for w in OPT["ORDER"].split():
            step[w[0]](int(w[1]))
        keep = chain[0]
        chain[0] = None
        if t == 0:
            dma([(r("F", FN, FP, p=(14, 128, 16)), dr(T["dZ"][:, :], "dZ"))], 2800.0, True)
            for k in (2, 3):
                arrive_turned("B%d" % k, "BG", 1024 * k + 8, 1024 * k + 1032, T["dB"][k], n_h if k % 2 else n_in,
                              "h1" if k % 2 else None, 12000.0)
        if end:
            chain[0] = keep
            act(r("FR", 0, 256), r("FC"), bias=CR)
            act(r("FR", 256, 512), r("FR", 0, 256), AF.Relu, bias=CR + 2047.0, scale=-1.0)
            chain[0] = None

        sY, sV, sC = r("SI", 0, 16), r("SI", 16, 32), r("SI", 32, 48)
        score = r("E2", 13, 256, 16)
        red_v = OPT["RED_V"][end]
        nv = 2 * red_v
        vs = r("LS", 48 * t + 32, 48 * t + 48)
        nx = r("NX", 256 * (t % 3), 256 * (t % 3) + 256)
        uo = r("UO", 16 * (t % 3), 16 * (t % 3) + 16)
        mine_u = uU if rot_in else uo
        banks = ["ps2", "ps3", "ps4", "ps7"]

        def choice():
            if t == 0:
                act(r("FW", 0, 256), r("N256"), AF.Silu, bias=co(cVo), scale=0.0)
                ts(r("VAL", 16, 32), uU, 0.0, A.add)
                act(r("EU"), ind(r("BKI", 0, 2064), uU), AF.Copy)
            ts(sY, r("KS", 15, 256, 16), 2048.0, A.add)
            ts(sV, sY, 4095, A.bitwise_and)
            expand(r("E1"), sV, r("DM"))
            for hh in range(2):
                mm(r("ps0", 8 * hh, 8 * hh + 8), r("E1", 128 * hh, 128 * hh + 128), sm(sB8, 0, 8))
            go()
            ts(sC, sY, 16, A.arith_shift_right)
            ts(score, sC, -16.0, A.add)
            cp(su(uV), r("ps0", 0, 16))
            act(r("G1"), ind(r("BKI", 0, V), su(uV)), AF.Copy)
            tt(sm(sOW2), score, sm(sOW1), A.subtract)
            act(r("LE"), r("G1"), bias=co(cL2), scale=co(cL1))
            act(r("LO"), r("G1"), bias=co(cO2), scale=co(cO1))
            if not end:
                ts(r("XT"), ind(r("XH", 0, V), su(uV)), -0.5, A.add)
            else:
                tt(r("FR", 0, 256), r("FC"), r("FR", 256, 512), A.add)
                ts(r("FC"), r("FR", 0, 256), -2047.0, A.add, 0.5, A.min)
            for hh in range(2):
                mm(r("ps6", 24 * hh, 24 * hh + 24), r("G1", 128 * hh, 128 * hh + 128), r("SEL"))
            go()
            mm(r("ps1", 0, 256), ID, r("STA"), True, False)
            for hh in range(2):
                mm(r("ps1", 128 * hh, 128 * hh + 128), r("E2", 128 * hh, 128 * hh + 128), ID, False, False)
            go()
            mm(r("ps1", 0, 256), r("MB"), r("LE"), False, True)
            go()
            act(r("R"), r("ps1", 0, 256))
            act(r("VAL", val + 32, val + 48), r("ps0", 0, 16))
            if end:
                act(r("MO"), r("FC"), scale=8192.0)
                send([(prv, eng_p, T["dM"][:, :], r("MO"), "aM")])
                arrive("M", [dr(None, "dM")], n_bk, lat=3000.0)
                dma([(r("F", FN, FP, p=(14, 128, 16)), dr(T["dM"][:, :], "dM"))])
            tt(sb(bT2), score, r("ps6", 0, 48, 3), A.is_lt)
            if not end:
                cp(r("HL"), r("ps6", 0, 48))
            tt(sm(sNOW), sm(sOW2), sb(bT2), A.subtract)

        def marks(part):
            for k in range(4 * part, 4 * part + 4):
                ts(r("OH", 128 * k, 128 * k + 128), r("NB", s0 // 16, s0 // 16 + 128), r("HL", 3 * k + 1, 3 * k + 2), A.is_equal,
                   sb(bT2, k, k + 1), A.mult)
                if k == 0:
                    tt(r("OQ"), ind(r("HL"), su(uL3)), r("QN"), A.is_equal)
            for m in range(4 * part, 4 * part + 4):
                mm(r("ps5", 16 * (m % 8), 16 * (m % 8) + 16), r("OH", 128 * m, 128 * m + 128), r("OQ", 16 * m, 16 * m + 16), False, m == 15)
            go()

        def holders():
            for q in range(16):
                mm(r("ps0", 128, 144), r("UH", 15 - q, 143 - q), r("LE", q, 256, 16), q == 0, q == 15)
            go()

        def held():
            tt(r("VAL", val, val + 16), r("ps0", 128, 144), r("DW3", 0, 16), A.min)

        def flags():
            ts(r("FT"), r("ps5", 0, 128), 2047.5 / 8192, A.is_gt)
            mm(r("ps5", 128, 256), r("FT"), r("TRC"))
            go()

        def places():
            cp(r("QB", 1, 129), r("ps5", 128, 256))

        def pairs(k):
            gp, hh, bank = k % 4, k // 4, banks.pop(0)
            banks.append(bank)
            for e in range(2):
                p = (32 * gp, 32 * gp + (32 if e else 16))
                mm(r(bank, 256 * e, 256 * e + 256), r("LO" if e else "LE", 128 * hh, 128 * hh + 128, p=p), r("R", p=p))
                go()
            for e in range(2):
                col = 2 * k + e
                src, res = r(bank, 256 * e, 256 * e + 256), sm(sRES, col, col + 1)
                if k < red_v:
                    red(sm(sACC, col, col + 1), src, A.max)
                else:
                    act(r("JK", 256 * col, 256 * col + 256), src, AF.Relu, bias=sm(sNOW, col, col + 1), acc=res)

        def newkeys():
            mm(r("ps1", 256, 512), r("MU", 0, 128), r("EU"), True, False)
            mm(r("ps1", 256, 512), r("MU", 128, 256), r("EU"), False, False)
            mm(r("ps1", 256, 512), r("MB"), r("LE"), False, False)
            for hh in range(2):
                mm(r("ps1", 256 + 128 * hh, 384 + 128 * hh), r("E2", 128 * hh, 128 * hh + 128), ID, False, hh == 1)
            go()
            act(r("NEW"), r("ps1", 256, 512), bias=co(cNB))

        def theirs():
            if end:
                mm(r("ps0", 256, 512), r("MU", 256, 384), r("LE"))
                go()
                act(r("GO"), r("ps0", 256, 512), bias=2047.5)
                send([(prv, eng_p, T["GV"][:, 256:512], r("GO"), "aG")])
                arrive("G", [r("GV", 256, 512)], n_bk)
            else:
                mm(r("ps0", 256, 512), ID75, r("XT"), True, False)
                mm(r("ps0", 256, 512), ID25, r("YA", 256 * t, 256 * t + 256), False, True)
                go()

        def mixed():
            ts(nx, r("ps0", 256, 512), CR, A.add, CR, A.subtract)

        def columns():
            act(r("FW", 256, 512), ind(r("BF", 0, V), su(uV)), AF.Copy)

        def dumps():
            mm(r("ps0", 64, 112), IDf, r("DW3"), True, False)
            go()

        def accepted():
            if nv:
                tt(sm(sRES, 0, nv), sm(sACC, 0, nv), sm(sNOW, 0, nv), A.add)
            expand(r("E5"), sm(sRES), r("DMN"), A.is_lt)
            for k in range(6):
                mm(r("ps0", 64 + 8 * k, 72 + 8 * k), r("E5", 128 * (k % 2), 128 * (k % 2) + 128), B8n, False, k == 5)
            go()

        def lists():
            tt(r("LF"), r("ps0", 64, 112), r("VAL", val, val + 48), A.max)
            cp(r("LS", 48 * t, 48 * t + 48), r("LF"))
            if end:
                send([(prv, eng_p, T["ML"][:, :], r("LS", 48 * t, 48 * t + 32), "aE")])

        def changes():
            cp(ind(r("F", FN, FE), r("LS", 48 * t + 16, 48 * t + 32)), r("FW", 256, 512))
            fo, fi = ind(r("F", FN, FE), r("LS", 48 * t, 48 * t + 16)), r("FW", 0, 256)
            node("a", [fo], [fi], [lambda: g.scalar.activation(fo[0], fi[0], AF.Silu)], cost(fo, [fi]))

        def own():
            cp(ind(r("XH"), vs), nx)

        def request():
            ts(mine_u, found, 2048.0, A.add)
            if rot_in:
                act(sm(sU0), found, bias=2048.0)
                mm(r("ps1", 0, 16), BACK, sm(sU0))
                go()
            else:
                send([(prv, eng_p, T["UQ"][:, 16 * t:16 * t + 16], uo, "aU%d" % (t + 1))])

        def askers():
            if t == 1:
                arrive_turned("B1", "BG", 1024, 2048, T["dB"][1], n_h, "h2", 12000.0)
                arrive_turned("B0", "BG", 0, 1024, T["dB"][0], n_in, None, 8000.0)
            if rot_in:
                cp(uo, r("ps1", 0, 16))
                send([(prv, eng_p, T["UQ"][:, 16 * t:16 * t + 16], uo, "aU%d" % (t + 1))])
            b0 = 2056 if t % 2 == 0 else 0
            cp(r("WL", 0, 256), ind(r("BG", b0, b0 + 2056), mine_u))
            if t == 0:
                send([(nxt, eng_n, land["B0"], r("B", 0, 1024), "aB0")])

        def numbers():
            act(r("VAL", 64 - val, 80 - val), found, bias=2048.0 + s0)
            act(r("EU"), ind(r("BKI", s0, s0 + 2064), mine_u), AF.Copy)
            act(r("JT", 128 * t + 128, 128 * t + 256), r3("J2", 0, 8, 15 - t, 31 - t))

        chain[0] = dict(keep, on="vat")
        step = dict(c=choice, h=holders, H=held, f=flags, Q=places, s=counts, r=prefix, z=level1, y=level2, q=request,
                    u=askers, e=numbers, t=theirs, x=mixed, w=columns, n=newkeys, d=dumps, a=accepted, l=lists,
                    g=changes, o=own)
        for w in OPT["LAST" if end else "ORDER2"].split():
            if w[0] in "pm":
                (pairs if w[0] == "p" else marks)(int(w[1]))
            else:
                step[w]()
        if end:
            arrive("E", [r("ML")], n_bk)
            cp(ind(r("BKI"), vs), r("NEW"))
            dma([(T["yk"][:, :], r("BKI", 0, V, p=(13, 128, 16)))])
            cp(ind(r("F", FN, FE), r("ML")), r("GV"))
            if rot_out:
                dma([(T["ym"][0:7, :], r("F", FN, FP, p=(30, 128, 16))), (T["ym"][7:8, :], r("F", FN, FP, p=(14, 15)))])
            else:
                dma([(T["ym"][:, :], r("F", FN, FP, p=(14, 128, 16)))])
            break
        keep = chain[0]
        chain[0] = None
        if t == RO - 2:
            dma([(r("FC"), r("F", FN, FP, p=(14, 128, 16)))])

    final, wait = emit_in_planned_order(nodes, Q, T)
    final["sent"] = sent[0]
    for s in final:
        wait("g", s, final[s])
